import numpy as np
import ml_dtypes


def mxq(x, axis, fmt="e4m3"):
    dtype, down = {"e4m3": (ml_dtypes.float8_e4m3fn, 7), "e5m2": (ml_dtypes.float8_e5m2, 14)}[fmt]
    v = np.moveaxis(np.asarray(x, np.float32).astype(ml_dtypes.bfloat16).astype(np.float64), axis, -1)
    blocks = v.reshape(v.shape[:-1] + (-1, 32))
    amax = np.abs(blocks).max(-1, keepdims=True)
    byte = np.maximum(np.where(amax > 0, np.frexp(amax)[1] - 1 + 127, 0) - down, 1)
    scale = np.exp2(byte - 127.0)
    codes = (blocks / scale).astype(np.float32).astype(dtype).astype(np.float64)
    return np.moveaxis((codes * scale).reshape(v.shape), -1, axis)


WIDE = False


def mx_kscale(k):
    if not WIDE:
        return np.ones(k)
    levels = np.array([10, -10, 5, -5, 0])
    if k % 512:
        return np.exp2(np.random.permutation(np.resize(levels, k // 32))).repeat(32)
    a = np.empty((k // 512, 16))
    for p in range(k // 512):
        a[p, :8] = np.random.permutation(np.resize(levels, 8))
        for g in range(8):
            far = levels[np.abs(levels - a[p, g]) >= 10]
            a[p, g + 8] = far[np.random.randint(len(far))]
    return np.exp2(a.ravel()).repeat(32)


def f64(x):
    return np.asarray(x).astype(np.float64)


def striped(idx):
    return np.tile(idx.reshape(-1, 16).T, (8, 1)).astype(np.uint16)


def unstriped(offs):
    return offs[:16].T.reshape(-1).astype(np.int64)


def pack_weight(w):
    k, n = w.shape
    w = f64(np.asarray(w, np.float32).astype(ml_dtypes.bfloat16)).reshape(k // 32, 32, n)
    amax = np.abs(w).max(1)
    byte = np.clip(np.where(amax > 0, np.frexp(amax)[1] - 1 + 127 - 7, 1), 1, 254)
    scaled = (w * np.exp2(127.0 - byte)[:, None, :]).reshape(k, n).astype(np.float32)
    words = np.ascontiguousarray(scaled.reshape(k // 512, 128, 4, n).transpose(0, 1, 3, 2)).astype(ml_dtypes.float8_e4m3fn).view(np.uint8)
    return words, np.ascontiguousarray(byte.astype(np.uint8).reshape(k // 512, 16, n))


def unpack_weight(words, scales):
    g, p, n, _ = words.shape
    vals = np.ascontiguousarray(words).view(ml_dtypes.float8_e4m3fn).astype(np.float64) * np.repeat(np.exp2(scales.astype(np.float64) - 127.0), 8, axis=1)[..., None]
    return vals.transpose(0, 1, 3, 2).reshape(g * 512, n)


def silu(v):
    return v / (1.0 + np.exp(-np.maximum(v, -700.0)))


K, T, S, H, N = 1024, 1024, 512, 512, 128


def setup_inputs():
    n = np.random.standard_normal
    s = mx_kscale(K)[:, None]
    u = mx_kscale(H)
    near = np.random.permutation(S)
    packed_xT = pack_weight(n((K, T)) * s)
    return {
        "x_words": packed_xT[0],
        "x_scales": packed_xT[1],
        "w1": (n((K, H)) / np.sqrt(K) / s * u).astype(np.float32),
        "w2": (n((H, N)) / np.sqrt(H) / u[:, None]).astype(np.float32),
        "taps": (0.6 * n((H, 3))).astype(np.float32),
        "offs": striped(np.random.permutation(T)[:S]),
        "order": striped(near),
        "back": striped(np.argsort(near)),
    }


def reference(x_words, x_scales, w1, w2, taps, offs, order, back):
    xq = unpack_weight(x_words, x_scales)[:, unstriped(offs)]
    y = mxq(f64(w1), 0, "e4m3").T @ xq
    gg = y[:, unstriped(order)]
    rr = silu(f64(taps)[:, 0:1] * gg + f64(taps)[:, 1:2] * (np.pad(gg, ((0, 0), (1, 0)))[:, :S]) + f64(taps)[:, 2:3] * (np.pad(gg, ((0, 0), (2, 0)))[:, :S]))
    z = rr[:, unstriped(back)] + y
    return mxq(f64(w2), 0, "e4m3").T @ mxq(z, 0, "e4m3")

@@ -1,0 +1,227 @@
+from contextlib import ExitStack
+
+import concourse.mybir as mybir
+
+K, T, S, H, N = 1024, 1024, 512, 512, 128
+FLOPS = 2 * K * H * S + 2 * H * N * S
+
+F32 = mybir.dt.float32
+BF16 = mybir.dt.bfloat16
+I32 = mybir.dt.int32
+U32 = mybir.dt.uint32
+U16 = mybir.dt.uint16
+U8 = mybir.dt.uint8
+FP8X4 = mybir.dt.float8_e4m3fn_x4
+MULT = mybir.AluOpType.mult
+ADD = mybir.AluOpType.add
+COPY = mybir.ActivationFunctionType.Copy
+SILU = mybir.ActivationFunctionType.Silu
+
+P = 128
+PACK = 4
+PASSES = K // (P * PACK)
+HALF = S // 2
+LIST_COLS = S // 16
+Y_WINDOW = 704
+RR_WINDOW = 528
+
+
+def tile_picked_yserial_silu_p_kernel(
+    tc, x_words, x_scales, w1, w2, taps, offs, order, back, out
+):
+    nc = tc.nc
+    with ExitStack() as ctx:
+        keep = ctx.enter_context(tc.tile_pool(name="keep", bufs=1))
+        psum = ctx.enter_context(tc.psum_pool(name="psum", bufs=1))
+
+        def sb(name, shape, dtype):
+            return keep.tile(shape, dtype, name=name, align_bytes=64)
+
+        offs_sb = sb("offs_sb", [P, LIST_COLS], U16)
+        order_sb = sb("order_sb", [P, LIST_COLS], U16)
+        back_sb = sb("back_sb", [P, LIST_COLS], U16)
+        x_table = [sb("x_table%d" % o, [P, T], I32) for o in range(PASSES)]
+        scale_table = sb("scale_table", [P, T], U8)
+        w1_raw = [sb("w1_raw%d" % o, [P, PACK, H], F32) for o in range(PASSES)]
+        w2_raw = sb("w2_raw", [P, PACK, N], F32)
+        taps_sb = sb("taps_sb", [P, PACK * 3], F32)
+        y = [sb("y%d" % t, [P, Y_WINDOW], F32) for t in range(PACK)]
+        rr = [sb("rr%d" % t, [P, RR_WINDOW], F32) for t in range(PACK)]
+        zeros = sb("zeros", [P, RR_WINDOW - S], F32)
+
+        def load_words(o):
+            nc.sync.dma_start(out=x_table[o][:], in_=x_words[o].rearrange("p n r -> p (n r)").bitcast(I32))
+
+        def load_w1(o):
+            rows = w1[o * P * PACK : (o + 1) * P * PACK, :]
+            nc.sync.dma_start(out=w1_raw[o][:], in_=rows.rearrange("(p j) c -> p j c", j=PACK))
+
+        nc.gpsimd.memset(scale_table[:].bitcast(I32), 0)
+        nc.sync.dma_start(offs_sb[:], offs)
+        for q in range(4):
+            nc.sync.dma_start(
+                out=scale_table[32 * q : 32 * q + 4 * PASSES, :].bitcast(I32),
+                in_=x_scales[:, 4 * q : 4 * q + 4, :].bitcast(I32),
+            )
+        load_words(0)
+        load_w1(0)
+        load_w1(1)
+        load_words(1)
+        nc.sync.dma_start(order_sb[:], order)
+        nc.sync.dma_start(out=taps_sb[:], in_=taps.rearrange("(p t) k -> p (t k)", t=PACK))
+        nc.sync.dma_start(back_sb[:], back)
+        nc.sync.dma_start(out=w2_raw[:], in_=w2.rearrange("(p j) m -> p j m", j=PACK))
+
+        nc.gpsimd.memset(zeros[:], 0.0)
+        for t in range(PACK):
+            nc.scalar.activation(rr[t][:, S:], zeros[:], SILU)
+            nc.gpsimd.memset(y[t][:, S:], 0.0)
+
+        x_codes0 = sb("x_codes0", [P, S], U32)
+        x_scale = sb("x_scale", [P, S], U8)
+        nc.vector.tensor_copy(x_codes0[:], x_table[0][:].bitcast(U32).indirect(offs_sb[:]))
+        nc.vector.tensor_copy(x_scale[:], scale_table[:].indirect(offs_sb[:]))
+
+        w1_bf = [[sb("w1_bf%d_%d" % (o, u), [P, 2 * P * PACK], BF16) for u in range(2)] for o in range(PASSES)]
+        w1_codes = [[sb("w1_codes%d_%d" % (o, u), [P, 2 * P], U32) for u in range(2)] for o in range(PASSES)]
+        w1_scale = [[sb("w1_scale%d_%d" % (o, u), [P, 2 * P], U8) for u in range(2)] for o in range(PASSES)]
+
+        def weave_w1(o, u, copy):
+            copy(
+                out=w1_bf[o][u][:].rearrange("p (t m j) -> p m j t", t=2, j=PACK),
+                in_=w1_raw[o][:].rearrange("p j (m t) -> p m j t", t=PACK)[:, :, :, 2 * u : 2 * u + 2],
+            )
+
+        def quantize_w1(o, u):
+            nc.vector.quantize_mx(out=w1_codes[o][u][:].bitcast(FP8X4), scales=w1_scale[o][u][:], in_=w1_bf[o][u][:])
+
+        y_first = [psum.tile([P, HALF], F32, name="y_first%d" % h) for h in range(2)]
+        y_rest = [psum.tile([P, S], F32, name="y_rest%d" % t) for t in range(1, PACK)]
+
+        def product1(o, t, acc, codes, cols):
+            m = slice((t % 2) * P, (t % 2 + 1) * P)
+            nc.tensor.matmul_mx(
+                out=acc,
+                lhsT=w1_codes[o][t // 2][:, m].bitcast(FP8X4),
+                lhsT_scale=w1_scale[o][t // 2][:, m],
+                rhs=codes.bitcast(FP8X4),
+                rhs_scale=x_scale[4 * o :, cols],
+                start=(o == 0),
+                stop=(o == PASSES - 1),
+            )
+
+        halves = [slice(h * HALF, (h + 1) * HALF) for h in range(2)]
+        list_halves = [slice(h * LIST_COLS // 2, (h + 1) * LIST_COLS // 2) for h in range(2)]
+
+        weave_w1(0, 0, nc.vector.tensor_copy)
+        weave_w1(0, 1, nc.scalar.copy)
+        quantize_w1(0, 0)
+        quantize_w1(0, 1)
+        for h in range(2):
+            product1(0, 0, y_first[h][:], x_codes0[:, halves[h]], halves[h])
+        for t in range(1, PACK):
+            product1(0, t, y_rest[t - 1][:], x_codes0[:], slice(0, S))
+
+        weave_w1(1, 0, nc.vector.tensor_copy)
+        weave_w1(1, 1, nc.scalar.copy)
+        quantize_w1(1, 0)
+        x_codes1_all = sb("x_codes1_all", [P, S], U32)
+        for h in range(2):
+            nc.vector.tensor_copy(
+                x_codes1_all[:, halves[h]], x_table[1][:].bitcast(U32).indirect(offs_sb[:, list_halves[h]])
+            )
+            product1(1, 0, y_first[h][:], x_codes1_all[:, halves[h]], halves[h])
+            nc.scalar.copy(out=y[0][:, halves[h]], in_=y_first[h][:])
+        quantize_w1(1, 1)
+        for t in range(1, PACK):
+            product1(1, t, y_rest[t - 1][:], x_codes1_all[:], slice(0, S))
+
+        w2_bf = sb("w2_bf", [P, N * PACK], BF16)
+        w2_codes = sb("w2_codes", [P, N], U32)
+        w2_scale = sb("w2_scale", [P, N], U8)
+        nc.vector.tensor_copy(
+            out=w2_bf[:].rearrange("p (c i j) -> p c j i", i=4, j=PACK),
+            in_=w2_raw[:].rearrange("p j (c i) -> p c j i", i=4),
+        )
+        nc.vector.quantize_mx(out=w2_codes[:].bitcast(FP8X4), scales=w2_scale[:], in_=w2_bf[:])
+
+        gg = [sb("gg%d" % t, [P, S], F32) for t in range(PACK)]
+        filt = [sb("filt%d" % t, [P, S], F32) for t in range(PACK)]
+        z = [sb("z%d" % h, [P, PACK, HALF], F32) for h in range(2)]
+
+        def tap(t, k):
+            return taps_sb[:, 3 * t + k : 3 * t + k + 1]
+
+        def leave_bank(t):
+            nc.scalar.copy(out=y[t][:, :S], in_=y_rest[t - 1][:])
+
+        def to_curve(t):
+            nc.vector.tensor_copy(gg[t][:], y[t][:].indirect(order_sb[:]))
+
+        def first_tap(t):
+            nc.scalar.activation(filt[t][:], gg[t][:], COPY, scale=tap(t, 0))
+
+        def other_taps(t):
+            for k in (1, 2):
+                nc.vector.scalar_tensor_tensor(
+                    out=filt[t][:, k:], in0=gg[t][:, : S - k], scalar=tap(t, k), in1=filt[t][:, k:], op0=MULT, op1=ADD
+                )
+
+        def silu(t):
+            nc.scalar.activation(rr[t][:, :S], filt[t][:], SILU)
+
+        def to_points(t, h):
+            nc.vector.tensor_tensor(z[h][:, t, :], rr[t][:].indirect(back_sb[:, list_halves[h]]), y[t][:, halves[h]], ADD)
+
+        leave_bank(1)
+        to_curve(0)
+        leave_bank(2)
+        to_curve(1)
+        first_tap(0)
+        leave_bank(3)
+        other_taps(0)
+        first_tap(1)
+        to_curve(2)
+        silu(0)
+        other_taps(1)
+        first_tap(2)
+        to_curve(3)
+        silu(1)
+        other_taps(2)
+        first_tap(3)
+        to_points(0, 0)
+        to_points(0, 1)
+        other_taps(3)
+        silu(2)
+        silu(3)
+        to_points(1, 0)
+        to_points(2, 0)
+        to_points(3, 0)
+        to_points(1, 1)
+        to_points(2, 1)
+        to_points(3, 1)
+
+        weavers = (nc.scalar.copy, nc.vector.tensor_copy)
+        z_bf = [sb("z_bf%d" % h, [P, HALF * PACK], BF16) for h in range(2)]
+        z_codes = [sb("z_codes%d" % h, [P, HALF], U32) for h in range(2)]
+        z_scale = [sb("z_scale%d" % h, [P, HALF], U8) for h in range(2)]
+        out_ps = [psum.tile([P, HALF], F32, name="out_ps%d" % h) for h in range(2)]
+        out_sb = [sb("out_sb%d" % h, [P, HALF], F32) for h in range(2)]
+        for h in range(2):
+            weavers[h](
+                out=z_bf[h][:].rearrange("p (c i t) -> p c t i", i=4, t=PACK),
+                in_=z[h][:].rearrange("p t (c i) -> p c t i", i=4),
+            )
+        for h in range(2):
+            nc.vector.quantize_mx(out=z_codes[h][:].bitcast(FP8X4), scales=z_scale[h][:], in_=z_bf[h][:])
+            nc.tensor.matmul_mx(
+                out=out_ps[h][:],
+                lhsT=w2_codes[:].bitcast(FP8X4),
+                lhsT_scale=w2_scale[:],
+                rhs=z_codes[h][:].bitcast(FP8X4),
+                rhs_scale=z_scale[h][:],
+                start=True,
+                stop=True,
+            )
+            weavers[h](out=out_sb[h][:], in_=out_ps[h][:])
+            nc.sync.dma_start(out=out[:, halves[h]], in_=out_sb[h][:])

@@ -1,6 +1,7 @@
 from contextlib import ExitStack
 
 import concourse.mybir as mybir
+from concourse.masks import make_identity
 
 K, T, S, H, N = 1024, 1024, 512, 512, 128
 FLOPS = 2 * K * H * S + 2 * H * N * S
@@ -24,6 +25,9 @@ HALF = S // 2
 LIST_COLS = S // 16
 Y_WINDOW = 704
 RR_WINDOW = 528
+Z_STEP = 1024
+PAD = 8
+QUARTER = S // 4
 
 
 def tile_picked_yserial_silu_p_kernel(
@@ -34,8 +38,8 @@ def tile_picked_yserial_silu_p_kernel(
         keep = ctx.enter_context(tc.tile_pool(name="keep", bufs=1))
         psum = ctx.enter_context(tc.psum_pool(name="psum", bufs=1))
 
-        def sb(name, shape, dtype):
-            return keep.tile(shape, dtype, name=name, align_bytes=64)
+        def sb(name, shape, dtype, tag=""):
+            return keep.tile(shape, dtype, name=name, tag=tag or name, align_bytes=64)
 
         offs_sb = sb("offs_sb", [P, LIST_COLS], U16)
         order_sb = sb("order_sb", [P, LIST_COLS], U16)
@@ -45,7 +49,11 @@ def tile_picked_yserial_silu_p_kernel(
         w1_raw = [sb("w1_raw%d" % o, [P, PACK, H], F32) for o in range(PASSES)]
         w2_raw = sb("w2_raw", [P, PACK, N], F32)
         taps_sb = sb("taps_sb", [P, PACK * 3], F32)
-        y = [sb("y%d" % t, [P, Y_WINDOW], F32) for t in range(PACK)]
+        z_home = sb("z_home", [P, PACK * Z_STEP], F32)
+        z = z_home[:].rearrange("p (t c) -> p t c", t=PACK)
+        y_start = (PACK - 1) * Z_STEP - HALF
+        y = [z_home[:, y_start : y_start + Y_WINDOW]]
+        y.extend(sb("y%d" % t, [P, Y_WINDOW], F32)[:] for t in range(1, PACK))
         rr = [sb("rr%d" % t, [P, RR_WINDOW], F32) for t in range(PACK)]
         zeros = sb("zeros", [P, RR_WINDOW - S], F32)
 
@@ -145,83 +153,90 @@ def tile_picked_yserial_silu_p_kernel(
         )
         nc.vector.quantize_mx(out=w2_codes[:].bitcast(FP8X4), scales=w2_scale[:], in_=w2_bf[:])
 
-        gg = [sb("gg%d" % t, [P, S], F32) for t in range(PACK)]
-        filt = [sb("filt%d" % t, [P, S], F32) for t in range(PACK)]
-        z = [sb("z%d" % h, [P, PACK, HALF], F32) for h in range(2)]
+        gg = [sb("gg%d" % t, [P, PAD + S], F32) for t in range(PACK)]
+        for t in range(PACK):
+            nc.gpsimd.memset(gg[t][:, :PAD], 0.0)
+        shared = sb("shared", [P, 4 * S], F32, tag="w1_codes1_1")
+        scaled = [shared[:, k * S : (k + 1) * S] for k in range(3)]
+        filt = [sb("filt0", [P, S], F32)[:], shared[:, 3 * S :], sb("filt2", [P, S], F32)[:], sb("filt3", [P, S], F32)[:]]
+        ident = sb("ident", [P, P], F32)
+        make_identity(nc, ident[:])
+        blocks = [slice(b * P, (b + 1) * P) for b in range(S // P)]
 
         def tap(t, k):
             return taps_sb[:, 3 * t + k : 3 * t + k + 1]
 
-        def leave_bank(t):
-            nc.scalar.copy(out=y[t][:, :S], in_=y_rest[t - 1][:])
+        def delayed(t, k):
+            return gg[t][:, PAD - k : PAD - k + S]
 
-        def to_curve(t):
-            nc.vector.tensor_copy(gg[t][:], y[t][:].indirect(order_sb[:]))
+        for t in range(PACK):
+            if t > 0:
+                nc.scalar.copy(out=y[t][:, :S], in_=y_rest[t - 1][:])
+            nc.vector.tensor_copy(delayed(t, 0), y[t].indirect(order_sb[:]))
 
-        def first_tap(t):
-            nc.scalar.activation(filt[t][:], gg[t][:], COPY, scale=tap(t, 0))
+        summed = psum.tile([P, S], F32, name="summed", tag="y_first0")
+        for k in range(3):
+            nc.scalar.activation(scaled[k], delayed(0, k), COPY, scale=tap(0, k))
+            for b, block in enumerate(blocks):
+                nc.tensor.matmul(
+                    summed[:, block],
+                    lhsT=scaled[k][:, block],
+                    rhs=ident[:],
+                    is_transpose=True,
+                    start=(k == 0 and b == 0),
+                    stop=(k == 2 and b == len(blocks) - 1),
+                )
+        nc.scalar.copy(out=filt[0], in_=summed[:])
+        restored = psum.tile([P, S], F32, name="restored", tag="y_first1")
+        for block in blocks:
+            nc.tensor.transpose(restored[:, block], filt[0][:, block], ident[:])
 
-        def other_taps(t):
-            for k in (1, 2):
-                nc.vector.scalar_tensor_tensor(
-                    out=filt[t][:, k:], in0=gg[t][:, : S - k], scalar=tap(t, k), in1=filt[t][:, k:], op0=MULT, op1=ADD
+        for t in range(1, PACK):
+            nc.scalar.activation(filt[t], delayed(t, 0), COPY, scale=tap(t, 0))
+        nc.scalar.activation(rr[0][:, :S], restored[:], SILU)
+        for t, k in ((1, 1), (2, 1), (1, 2), (3, 1), (2, 2), (3, 2)):
+            nc.vector.scalar_tensor_tensor(
+                out=filt[t], in0=delayed(t, k), scalar=tap(t, k), in1=filt[t], op0=MULT, op1=ADD
+            )
+        for t in range(1, PACK):
+            nc.scalar.activation(rr[t][:, :S], filt[t], SILU)
+
+        for t in (1, 2):
+            nc.vector.tensor_tensor(z[:, t, :S], rr[t][:].indirect(back_sb[:]), y[t][:, :S], ADD)
+        for h in (1, 0):
+            for t in (3, 0):
+                nc.vector.tensor_tensor(
+                    z[:, t, halves[h]], rr[t][:].indirect(back_sb[:, list_halves[h]]), y[t][:, halves[h]], ADD
                 )
 
-        def silu(t):
-            nc.scalar.activation(rr[t][:, :S], filt[t][:], SILU)
-
-        def to_points(t, h):
-            nc.vector.tensor_tensor(z[h][:, t, :], rr[t][:].indirect(back_sb[:, list_halves[h]]), y[t][:, halves[h]], ADD)
-
-        leave_bank(1)
-        to_curve(0)
-        leave_bank(2)
-        to_curve(1)
-        first_tap(0)
-        leave_bank(3)
-        other_taps(0)
-        first_tap(1)
-        to_curve(2)
-        silu(0)
-        other_taps(1)
-        first_tap(2)
-        to_curve(3)
-        silu(1)
-        other_taps(2)
-        first_tap(3)
-        to_points(0, 0)
-        to_points(0, 1)
-        other_taps(3)
-        silu(2)
-        silu(3)
-        to_points(1, 0)
-        to_points(2, 0)
-        to_points(3, 0)
-        to_points(1, 1)
-        to_points(2, 1)
-        to_points(3, 1)
-
-        weavers = (nc.scalar.copy, nc.vector.tensor_copy)
-        z_bf = [sb("z_bf%d" % h, [P, HALF * PACK], BF16) for h in range(2)]
-        z_codes = [sb("z_codes%d" % h, [P, HALF], U32) for h in range(2)]
-        z_scale = [sb("z_scale%d" % h, [P, HALF], U8) for h in range(2)]
-        out_ps = [psum.tile([P, HALF], F32, name="out_ps%d" % h) for h in range(2)]
-        out_sb = [sb("out_sb%d" % h, [P, HALF], F32) for h in range(2)]
-        for h in range(2):
-            weavers[h](
-                out=z_bf[h][:].rearrange("p (c i t) -> p c t i", i=4, t=PACK),
-                in_=z[h][:].rearrange("p t (c i) -> p c t i", i=4),
+        out_sb = sb("out_sb", [P, S], F32)
+        z_codes = sb("z_codes", [P, S], U32)
+        z_scale = sb("z_scale", [P, S], U8)
+        pieces = (
+            (HALF, HALF, nc.scalar.copy, nc.scalar.copy),
+            (0, QUARTER, nc.vector.tensor_copy, nc.scalar.copy),
+            (QUARTER, QUARTER, nc.scalar.copy, nc.vector.tensor_copy),
+        )
+        z_bf = [sb("z_bf%d" % n, [P, piece[1] * PACK], BF16) for n, piece in enumerate(pieces)]
+        out_ps = [psum.tile([P, piece[1]], F32, name="out_ps%d" % n) for n, piece in enumerate(pieces)]
+        for n, (first, width, weave, leave) in enumerate(pieces):
+            weave(
+                out=z_bf[n][:].rearrange("p (c i t) -> p c t i", i=4, t=PACK),
+                in_=z[:, :, first : first + width].rearrange("p t (c i) -> p c t i", i=4),
             )
-        for h in range(2):
-            nc.vector.quantize_mx(out=z_codes[h][:].bitcast(FP8X4), scales=z_scale[h][:], in_=z_bf[h][:])
+        for n, (first, width, weave, leave) in enumerate(pieces):
+            cols = slice(first, first + width)
+            nc.vector.quantize_mx(out=z_codes[:, cols].bitcast(FP8X4), scales=z_scale[:, cols], in_=z_bf[n][:])
             nc.tensor.matmul_mx(
-                out=out_ps[h][:],
+                out=out_ps[n][:],
                 lhsT=w2_codes[:].bitcast(FP8X4),
                 lhsT_scale=w2_scale[:],
-                rhs=z_codes[h][:].bitcast(FP8X4),
-                rhs_scale=z_scale[h][:],
+                rhs=z_codes[:, cols].bitcast(FP8X4),
+                rhs_scale=z_scale[:, cols],
                 start=True,
                 stop=True,
             )
-            weavers[h](out=out_sb[h][:], in_=out_ps[h][:])
-            nc.sync.dma_start(out=out[:, halves[h]], in_=out_sb[h][:])
+            leave(out=out_sb[:, cols], in_=out_ps[n][:])
+            if n != 1:
+                half = halves[first // HALF]
+                nc.sync.dma_start(out=out[:, half], in_=out_sb[:, half])

@@ -65,20 +65,20 @@ def tile_picked_yserial_silu_p_kernel(
             nc.sync.dma_start(out=w1_raw[o][:], in_=rows.rearrange("(p j) c -> p j c", j=PACK))
 
         nc.gpsimd.memset(scale_table[:].bitcast(I32), 0)
+        load_words(0)
         nc.sync.dma_start(offs_sb[:], offs)
         for q in range(4):
             nc.sync.dma_start(
                 out=scale_table[32 * q : 32 * q + 4 * PASSES, :].bitcast(I32),
                 in_=x_scales[:, 4 * q : 4 * q + 4, :].bitcast(I32),
             )
-        load_words(0)
         load_w1(0)
         load_w1(1)
         load_words(1)
+        nc.sync.dma_start(out=w2_raw[:], in_=w2.rearrange("(p j) m -> p j m", j=PACK))
         nc.sync.dma_start(order_sb[:], order)
         nc.sync.dma_start(out=taps_sb[:], in_=taps.rearrange("(p t) k -> p (t k)", t=PACK))
         nc.sync.dma_start(back_sb[:], back)
-        nc.sync.dma_start(out=w2_raw[:], in_=w2.rearrange("(p j) m -> p j m", j=PACK))
 
         nc.gpsimd.memset(zeros[:], 0.0)
         for t in range(PACK):
@@ -100,8 +100,13 @@ def tile_picked_yserial_silu_p_kernel(
                 in_=w1_raw[o][:].rearrange("p j (m t) -> p m j t", t=PACK)[:, :, :, 2 * u : 2 * u + 2],
             )
 
-        def quantize_w1(o, u):
-            nc.vector.quantize_mx(out=w1_codes[o][u][:].bitcast(FP8X4), scales=w1_scale[o][u][:], in_=w1_bf[o][u][:])
+        def quantize_w1(o, u, first=0, tiles=2):
+            cols = slice(first * P, (first + tiles) * P)
+            nc.vector.quantize_mx(
+                out=w1_codes[o][u][:, cols].bitcast(FP8X4),
+                scales=w1_scale[o][u][:, cols],
+                in_=w1_bf[o][u][:, first * P * PACK : (first + tiles) * P * PACK],
+            )
 
         y_first = [psum.tile([P, HALF], F32, name="y_first%d" % h) for h in range(2)]
         y_rest = [psum.tile([P, S], F32, name="y_rest%d" % t) for t in range(1, PACK)]
@@ -132,7 +137,7 @@ def tile_picked_yserial_silu_p_kernel(
 
         weave_w1(1, 0, nc.vector.tensor_copy)
         weave_w1(1, 1, nc.scalar.copy)
-        quantize_w1(1, 0)
+        quantize_w1(1, 0, 0, 1)
         x_codes1_all = sb("x_codes1_all", [P, S], U32)
         for h in range(2):
             nc.vector.tensor_copy(
@@ -140,6 +145,7 @@ def tile_picked_yserial_silu_p_kernel(
             )
             product1(1, 0, y_first[h][:], x_codes1_all[:, halves[h]], halves[h])
             nc.scalar.copy(out=y[0][:, halves[h]], in_=y_first[h][:])
+        quantize_w1(1, 0, 1, 1)
         quantize_w1(1, 1)
         for t in range(1, PACK):
             product1(1, t, y_rest[t - 1][:], x_codes1_all[:], slice(0, S))
@@ -147,7 +153,7 @@ def tile_picked_yserial_silu_p_kernel(
         w2_bf = sb("w2_bf", [P, N * PACK], BF16)
         w2_codes = sb("w2_codes", [P, N], U32)
         w2_scale = sb("w2_scale", [P, N], U8)
-        nc.vector.tensor_copy(
+        nc.scalar.copy(
             out=w2_bf[:].rearrange("p (c i j) -> p c j i", i=4, j=PACK),
             in_=w2_raw[:].rearrange("p j (c i) -> p c j i", i=4),
         )
@@ -186,20 +192,20 @@ def tile_picked_yserial_silu_p_kernel(
                     start=(k == 0 and b == 0),
                     stop=(k == 2 and b == len(blocks) - 1),
                 )
+        for t in range(1, PACK):
+            nc.scalar.activation(filt[t], delayed(t, 0), COPY, scale=tap(t, 0))
         nc.scalar.copy(out=filt[0], in_=summed[:])
         restored = psum.tile([P, S], F32, name="restored", tag="y_first1")
         for block in blocks:
             nc.tensor.transpose(restored[:, block], filt[0][:, block], ident[:])
 
-        for t in range(1, PACK):
-            nc.scalar.activation(filt[t], delayed(t, 0), COPY, scale=tap(t, 0))
-        nc.scalar.activation(rr[0][:, :S], restored[:], SILU)
         for t, k in ((1, 1), (2, 1), (1, 2), (3, 1), (2, 2), (3, 2)):
             nc.vector.scalar_tensor_tensor(
                 out=filt[t], in0=delayed(t, k), scalar=tap(t, k), in1=filt[t], op0=MULT, op1=ADD
             )
         for t in range(1, PACK):
             nc.scalar.activation(rr[t][:, :S], filt[t], SILU)
+        nc.scalar.activation(rr[0][:, :S], restored[:], SILU)
 
         for t in (1, 2):
             nc.vector.tensor_tensor(z[:, t, :S], rr[t][:].indirect(back_sb[:]), y[t][:, :S], ADD)

@@ -21,13 +21,20 @@ SILU = mybir.ActivationFunctionType.Silu
 P = 128
 PACK = 4
 PASSES = K // (P * PACK)
+TAPS = 3
+LINE = 4
+PER_COLUMN = 16
+LIST_COLS = S // PER_COLUMN
 HALF = S // 2
-LIST_COLS = S // 16
+QUARTER = S // 4
+QUADRANTS = 4
+SCALE_ROWS = 4
 Y_WINDOW = 704
 RR_WINDOW = 528
 Z_STEP = 1024
 PAD = 8
-QUARTER = S // 4
+LAST_ON_TENSOR = HALF
+FIRST_PIECES = ((0, HALF), (HALF, QUARTER), (HALF + QUARTER, QUARTER))
 
 
 def tile_picked_yserial_silu_p_kernel(
@@ -41,6 +48,9 @@ def tile_picked_yserial_silu_p_kernel(
         def sb(name, shape, dtype, tag=""):
             return keep.tile(shape, dtype, name=name, tag=tag or name, align_bytes=64)
 
+        halves = [slice(h * HALF, (h + 1) * HALF) for h in range(2)]
+        list_halves = [slice(h * LIST_COLS // 2, (h + 1) * LIST_COLS // 2) for h in range(2)]
+
         offs_sb = sb("offs_sb", [P, LIST_COLS], U16)
         order_sb = sb("order_sb", [P, LIST_COLS], U16)
         back_sb = sb("back_sb", [P, LIST_COLS], U16)
@@ -48,7 +58,7 @@ def tile_picked_yserial_silu_p_kernel(
         scale_table = sb("scale_table", [P, T], U8)
         w1_raw = [sb("w1_raw%d" % o, [P, PACK, H], F32) for o in range(PASSES)]
         w2_raw = sb("w2_raw", [P, PACK, N], F32)
-        taps_sb = sb("taps_sb", [P, PACK * 3], F32)
+        taps_sb = sb("taps_sb", [P, PACK * TAPS], F32)
         z_home = sb("z_home", [P, PACK * Z_STEP], F32)
         z = z_home[:].rearrange("p (t c) -> p t c", t=PACK)
         y_start = (PACK - 1) * Z_STEP - HALF
@@ -67,10 +77,10 @@ def tile_picked_yserial_silu_p_kernel(
         nc.gpsimd.memset(scale_table[:].bitcast(I32), 0)
         load_words(0)
         nc.sync.dma_start(offs_sb[:], offs)
-        for q in range(4):
+        for q in range(QUADRANTS):
             nc.sync.dma_start(
-                out=scale_table[32 * q : 32 * q + 4 * PASSES, :].bitcast(I32),
-                in_=x_scales[:, 4 * q : 4 * q + 4, :].bitcast(I32),
+                out=scale_table[32 * q : 32 * q + SCALE_ROWS * PASSES, :].bitcast(I32),
+                in_=x_scales[:, SCALE_ROWS * q : SCALE_ROWS * (q + 1), :].bitcast(I32),
             )
         load_w1(0)
         load_w1(1)
@@ -94,118 +104,143 @@ def tile_picked_yserial_silu_p_kernel(
         w1_codes = [[sb("w1_codes%d_%d" % (o, u), [P, 2 * P], U32) for u in range(2)] for o in range(PASSES)]
         w1_scale = [[sb("w1_scale%d_%d" % (o, u), [P, 2 * P], U8) for u in range(2)] for o in range(PASSES)]
 
-        def weave_w1(o, u, copy):
-            copy(
-                out=w1_bf[o][u][:].rearrange("p (t m j) -> p m j t", t=2, j=PACK),
-                in_=w1_raw[o][:].rearrange("p j (m t) -> p m j t", t=PACK)[:, :, :, 2 * u : 2 * u + 2],
-            )
+        def weave_w1(o):
+            for u, copy in enumerate((nc.vector.tensor_copy, nc.scalar.copy)):
+                copy(
+                    out=w1_bf[o][u][:].rearrange("p (e m j) -> p m j e", e=2, j=PACK),
+                    in_=w1_raw[o][:].rearrange("p j (m t) -> p m j t", t=PACK)[:, :, :, 2 * u : 2 * u + 2],
+                )
 
-        def quantize_w1(o, u, first=0, tiles=2):
-            cols = slice(first * P, (first + tiles) * P)
+        def quantize_w1(o, first_tile, tiles):
+            u, e = divmod(first_tile, 2)
+            cols = slice(e * P, (e + tiles) * P)
             nc.vector.quantize_mx(
                 out=w1_codes[o][u][:, cols].bitcast(FP8X4),
                 scales=w1_scale[o][u][:, cols],
-                in_=w1_bf[o][u][:, first * P * PACK : (first + tiles) * P * PACK],
+                in_=w1_bf[o][u][:, e * P * PACK : (e + tiles) * P * PACK],
             )
 
-        y_first = [psum.tile([P, HALF], F32, name="y_first%d" % h) for h in range(2)]
+        y_first = [psum.tile([P, width], F32, name="y_first%d" % n) for n, (start, width) in enumerate(FIRST_PIECES)]
         y_rest = [psum.tile([P, S], F32, name="y_rest%d" % t) for t in range(1, PACK)]
 
-        def product1(o, t, acc, codes, cols):
+        def product1(o, t, acc, x_codes, cols):
             m = slice((t % 2) * P, (t % 2 + 1) * P)
             nc.tensor.matmul_mx(
                 out=acc,
                 lhsT=w1_codes[o][t // 2][:, m].bitcast(FP8X4),
                 lhsT_scale=w1_scale[o][t // 2][:, m],
-                rhs=codes.bitcast(FP8X4),
-                rhs_scale=x_scale[4 * o :, cols],
+                rhs=x_codes[:, cols].bitcast(FP8X4),
+                rhs_scale=x_scale[SCALE_ROWS * o :, cols],
                 start=(o == 0),
                 stop=(o == PASSES - 1),
             )
 
-        halves = [slice(h * HALF, (h + 1) * HALF) for h in range(2)]
-        list_halves = [slice(h * LIST_COLS // 2, (h + 1) * LIST_COLS // 2) for h in range(2)]
-
-        weave_w1(0, 0, nc.vector.tensor_copy)
-        weave_w1(0, 1, nc.scalar.copy)
-        quantize_w1(0, 0)
-        quantize_w1(0, 1)
-        for h in range(2):
-            product1(0, 0, y_first[h][:], x_codes0[:, halves[h]], halves[h])
+        weave_w1(0)
+        quantize_w1(0, 0, 2)
+        quantize_w1(0, 2, 2)
+        for n, (start, width) in enumerate(FIRST_PIECES):
+            product1(0, 0, y_first[n][:], x_codes0, slice(start, start + width))
         for t in range(1, PACK):
-            product1(0, t, y_rest[t - 1][:], x_codes0[:], slice(0, S))
+            product1(0, t, y_rest[t - 1][:], x_codes0, slice(0, S))
 
-        weave_w1(1, 0, nc.vector.tensor_copy)
-        weave_w1(1, 1, nc.scalar.copy)
-        quantize_w1(1, 0, 0, 1)
-        x_codes1_all = sb("x_codes1_all", [P, S], U32)
-        for h in range(2):
-            nc.vector.tensor_copy(
-                x_codes1_all[:, halves[h]], x_table[1][:].bitcast(U32).indirect(offs_sb[:, list_halves[h]])
-            )
-            product1(1, 0, y_first[h][:], x_codes1_all[:, halves[h]], halves[h])
-            nc.scalar.copy(out=y[0][:, halves[h]], in_=y_first[h][:])
-        quantize_w1(1, 0, 1, 1)
-        quantize_w1(1, 1)
+        weave_w1(1)
+        quantize_w1(1, 0, 1)
+        x_codes1 = sb("x_codes1", [P, S], U32)
+        for n, (start, width) in enumerate(FIRST_PIECES):
+            cols = slice(start, start + width)
+            entries = offs_sb[:, start // PER_COLUMN : (start + width) // PER_COLUMN]
+            nc.vector.tensor_copy(x_codes1[:, cols], x_table[1][:].bitcast(U32).indirect(entries))
+            product1(1, 0, y_first[n][:], x_codes1, cols)
+            nc.scalar.copy(out=y[0][:, cols], in_=y_first[n][:])
+        quantize_w1(1, 1, 1)
+        quantize_w1(1, 2, 2)
         for t in range(1, PACK):
-            product1(1, t, y_rest[t - 1][:], x_codes1_all[:], slice(0, S))
+            product1(1, t, y_rest[t - 1][:], x_codes1, slice(0, S))
 
         w2_bf = sb("w2_bf", [P, N * PACK], BF16)
         w2_codes = sb("w2_codes", [P, N], U32)
         w2_scale = sb("w2_scale", [P, N], U8)
         nc.scalar.copy(
-            out=w2_bf[:].rearrange("p (c i j) -> p c j i", i=4, j=PACK),
-            in_=w2_raw[:].rearrange("p j (c i) -> p c j i", i=4),
+            out=w2_bf[:].rearrange("p (c i j) -> p c j i", i=LINE, j=PACK),
+            in_=w2_raw[:].rearrange("p j (c i) -> p c j i", i=LINE),
         )
         nc.vector.quantize_mx(out=w2_codes[:].bitcast(FP8X4), scales=w2_scale[:], in_=w2_bf[:])
 
         gg = [sb("gg%d" % t, [P, PAD + S], F32) for t in range(PACK)]
         for t in range(PACK):
             nc.gpsimd.memset(gg[t][:, :PAD], 0.0)
-        shared = sb("shared", [P, 4 * S], F32, tag="w1_codes1_1")
-        scaled = [shared[:, k * S : (k + 1) * S] for k in range(3)]
-        filt = [sb("filt0", [P, S], F32)[:], shared[:, 3 * S :], sb("filt2", [P, S], F32)[:], sb("filt3", [P, S], F32)[:]]
+        on_tensor = {0: S, PACK - 1: LAST_ON_TENSOR}
+        on_vector = {t: slice(on_tensor.get(t, 0), S) for t in range(1, PACK)}
+        shared = sb("shared", [P, (TAPS + 1) * S], F32, tag="w1_codes1_1")
+        scaled_last = sb("scaled_last", [P, TAPS * LAST_ON_TENSOR], F32)
+        scaled = {
+            0: [shared[:, k * S : (k + 1) * S] for k in range(TAPS)],
+            PACK - 1: [scaled_last[:, k * LAST_ON_TENSOR : (k + 1) * LAST_ON_TENSOR] for k in range(TAPS)],
+        }
+        summed_sb = {t: sb("summed_sb%d" % t, [P, width], F32) for t, width in on_tensor.items()}
+        filt = {1: shared[:, TAPS * S :], 2: sb("filt2", [P, S], F32)[:], 3: sb("filt3", [P, S], F32)[:]}
         ident = sb("ident", [P, P], F32)
         make_identity(nc, ident[:])
-        blocks = [slice(b * P, (b + 1) * P) for b in range(S // P)]
+        summed = {
+            0: psum.tile([P, S], F32, name="summed0", tag="y_first0"),
+            PACK - 1: psum.tile([P, LAST_ON_TENSOR], F32, name="summed3"),
+        }
+        restored = {
+            0: psum.tile([P, S], F32, name="restored0", tag="y_first1"),
+            PACK - 1: psum.tile([P, LAST_ON_TENSOR], F32, name="restored3"),
+        }
 
         def tap(t, k):
-            return taps_sb[:, 3 * t + k : 3 * t + k + 1]
+            return taps_sb[:, TAPS * t + k : TAPS * t + k + 1]
 
         def delayed(t, k):
             return gg[t][:, PAD - k : PAD - k + S]
+
+        def chunks(t):
+            return [slice(start, start + P) for start in range(0, on_tensor[t], P)]
+
+        def sum_by_transposes(t):
+            for k in range(TAPS):
+                nc.scalar.activation(scaled[t][k], delayed(t, k)[:, : on_tensor[t]], COPY, scale=tap(t, k))
+                for chunk in chunks(t):
+                    nc.tensor.matmul(
+                        summed[t][:, chunk],
+                        lhsT=scaled[t][k][:, chunk],
+                        rhs=ident[:],
+                        is_transpose=True,
+                        start=(k == 0 and chunk.start == 0),
+                        stop=(k == TAPS - 1 and chunk.stop == on_tensor[t]),
+                    )
+
+        def turn_back(t):
+            nc.scalar.copy(out=summed_sb[t][:], in_=summed[t][:])
+            for chunk in chunks(t):
+                nc.tensor.transpose(restored[t][:, chunk], summed_sb[t][:, chunk], ident[:])
 
         for t in range(PACK):
             if t > 0:
                 nc.scalar.copy(out=y[t][:, :S], in_=y_rest[t - 1][:])
             nc.vector.tensor_copy(delayed(t, 0), y[t].indirect(order_sb[:]))
 
-        summed = psum.tile([P, S], F32, name="summed", tag="y_first0")
-        for k in range(3):
-            nc.scalar.activation(scaled[k], delayed(0, k), COPY, scale=tap(0, k))
-            for b, block in enumerate(blocks):
-                nc.tensor.matmul(
-                    summed[:, block],
-                    lhsT=scaled[k][:, block],
-                    rhs=ident[:],
-                    is_transpose=True,
-                    start=(k == 0 and b == 0),
-                    stop=(k == 2 and b == len(blocks) - 1),
-                )
-        for t in range(1, PACK):
-            nc.scalar.activation(filt[t], delayed(t, 0), COPY, scale=tap(t, 0))
-        nc.scalar.copy(out=filt[0], in_=summed[:])
-        restored = psum.tile([P, S], F32, name="restored", tag="y_first1")
-        for block in blocks:
-            nc.tensor.transpose(restored[:, block], filt[0][:, block], ident[:])
+        sum_by_transposes(0)
+        for t, cols in on_vector.items():
+            nc.scalar.activation(filt[t][:, cols], delayed(t, 0)[:, cols], COPY, scale=tap(t, 0))
+        sum_by_transposes(PACK - 1)
+        for t in on_tensor:
+            turn_back(t)
 
-        for t, k in ((1, 1), (2, 1), (1, 2), (3, 1), (2, 2), (3, 2)):
-            nc.vector.scalar_tensor_tensor(
-                out=filt[t], in0=delayed(t, k), scalar=tap(t, k), in1=filt[t], op0=MULT, op1=ADD
-            )
-        for t in range(1, PACK):
-            nc.scalar.activation(rr[t][:, :S], filt[t], SILU)
-        nc.scalar.activation(rr[0][:, :S], restored[:], SILU)
+        for step in range(2, PACK + TAPS - 1):
+            for k in range(1, TAPS):
+                t = step - k
+                if t in on_vector:
+                    acc = filt[t][:, on_vector[t]]
+                    nc.vector.scalar_tensor_tensor(
+                        out=acc, in0=delayed(t, k)[:, on_vector[t]], scalar=tap(t, k), in1=acc, op0=MULT, op1=ADD
+                    )
+        for t, cols in on_vector.items():
+            nc.scalar.activation(rr[t][:, cols], filt[t][:, cols], SILU)
+        for t in (PACK - 1, 0):
+            nc.scalar.activation(rr[t][:, : on_tensor[t]], restored[t][:], SILU)
 
         for t in (1, 2):
             nc.vector.tensor_tensor(z[:, t, :S], rr[t][:].indirect(back_sb[:]), y[t][:, :S], ADD)
@@ -218,20 +253,23 @@ def tile_picked_yserial_silu_p_kernel(
         out_sb = sb("out_sb", [P, S], F32)
         z_codes = sb("z_codes", [P, S], U32)
         z_scale = sb("z_scale", [P, S], U8)
-        pieces = (
-            (HALF, HALF, nc.scalar.copy, nc.scalar.copy),
+        upper = [(HALF, HALF, nc.scalar.copy, nc.scalar.copy)]
+        lower = [
             (0, QUARTER, nc.vector.tensor_copy, nc.scalar.copy),
             (QUARTER, QUARTER, nc.scalar.copy, nc.vector.tensor_copy),
-        )
+        ]
+        pieces = upper + lower
         z_bf = [sb("z_bf%d" % n, [P, piece[1] * PACK], BF16) for n, piece in enumerate(pieces)]
-        out_ps = [psum.tile([P, piece[1]], F32, name="out_ps%d" % n) for n, piece in enumerate(pieces)]
-        for n, (first, width, weave, leave) in enumerate(pieces):
+        out_ps = [
+            psum.tile([P, piece[1]], F32, name="out_ps%d" % n, tag="y_rest%d" % (n + 1)) for n, piece in enumerate(pieces)
+        ]
+        for n, (start, width, weave, leave) in enumerate(pieces):
             weave(
-                out=z_bf[n][:].rearrange("p (c i t) -> p c t i", i=4, t=PACK),
-                in_=z[:, :, first : first + width].rearrange("p t (c i) -> p c t i", i=4),
+                out=z_bf[n][:].rearrange("p (c i t) -> p c t i", i=LINE, t=PACK),
+                in_=z[:, :, start : start + width].rearrange("p t (c i) -> p c t i", i=LINE),
             )
-        for n, (first, width, weave, leave) in enumerate(pieces):
-            cols = slice(first, first + width)
+        for n, (start, width, weave, leave) in enumerate(pieces):
+            cols = slice(start, start + width)
             nc.vector.quantize_mx(out=z_codes[:, cols].bitcast(FP8X4), scales=z_scale[:, cols], in_=z_bf[n][:])
             nc.tensor.matmul_mx(
                 out=out_ps[n][:],
@@ -243,6 +281,6 @@ def tile_picked_yserial_silu_p_kernel(
                 stop=True,
             )
             leave(out=out_sb[:, cols], in_=out_ps[n][:])
-            if n != 1:
-                half = halves[first // HALF]
+            if (start + width) % HALF == 0:
+                half = halves[start // HALF]
                 nc.sync.dma_start(out=out[:, half], in_=out_sb[:, half])

@@ -15,6 +15,7 @@ U8 = mybir.dt.uint8
 FP8X4 = mybir.dt.float8_e4m3fn_x4
 MULT = mybir.AluOpType.mult
 ADD = mybir.AluOpType.add
+IS_LT = mybir.AluOpType.is_lt
 COPY = mybir.ActivationFunctionType.Copy
 SILU = mybir.ActivationFunctionType.Silu
 
@@ -33,8 +34,8 @@ Y_WINDOW = 704
 RR_WINDOW = 528
 Z_STEP = 1024
 PAD = 8
-LAST_ON_TENSOR = HALF
-FIRST_PIECES = ((0, HALF), (HALF, QUARTER), (HALF + QUARTER, QUARTER))
+SPLIT_ON_TENSOR = HALF
+TINY = 2.0**-32
 
 
 def tile_picked_yserial_silu_p_kernel(
@@ -56,23 +57,27 @@ def tile_picked_yserial_silu_p_kernel(
         back_sb = sb("back_sb", [P, LIST_COLS], U16)
         x_table = [sb("x_table%d" % o, [P, T], I32) for o in range(PASSES)]
         scale_table = sb("scale_table", [P, T], U8)
-        w1_raw = [sb("w1_raw%d" % o, [P, PACK, H], F32) for o in range(PASSES)]
+        w1_parts = ((0, 0, PACK), (1, 0, 2), (1, 2, 2))
+        w1_raw = [sb("w1_raw%d" % n, [P, part[2], H], F32) for n, part in enumerate(w1_parts)]
         w2_raw = sb("w2_raw", [P, PACK, N], F32)
         taps_sb = sb("taps_sb", [P, PACK * TAPS], F32)
         z_home = sb("z_home", [P, PACK * Z_STEP], F32)
         z = z_home[:].rearrange("p (t c) -> p t c", t=PACK)
-        y_start = (PACK - 1) * Z_STEP - HALF
-        y = [z_home[:, y_start : y_start + Y_WINDOW]]
-        y.extend(sb("y%d" % t, [P, Y_WINDOW], F32)[:] for t in range(1, PACK))
+        y_start = Z_STEP - HALF
+        y = [
+            z_home[:, y_start : y_start + Y_WINDOW] if t == 2 else sb("y%d" % t, [P, Y_WINDOW], F32)[:]
+            for t in range(PACK)
+        ]
         rr = [sb("rr%d" % t, [P, RR_WINDOW], F32) for t in range(PACK)]
         zeros = sb("zeros", [P, RR_WINDOW - S], F32)
 
         def load_words(o):
             nc.sync.dma_start(out=x_table[o][:], in_=x_words[o].rearrange("p n r -> p (n r)").bitcast(I32))
 
-        def load_w1(o):
-            rows = w1[o * P * PACK : (o + 1) * P * PACK, :]
-            nc.sync.dma_start(out=w1_raw[o][:], in_=rows.rearrange("(p j) c -> p j c", j=PACK))
+        def load_w1(n):
+            o, first, count = w1_parts[n]
+            rows = w1[o * P * PACK : (o + 1) * P * PACK, :].rearrange("(p j) c -> p j c", j=PACK)
+            nc.sync.dma_start(out=w1_raw[n][:], in_=rows[:, first : first + count, :])
 
         nc.gpsimd.memset(scale_table[:].bitcast(I32), 0)
         load_words(0)
@@ -82,12 +87,13 @@ def tile_picked_yserial_silu_p_kernel(
                 out=scale_table[32 * q : 32 * q + SCALE_ROWS * PASSES, :].bitcast(I32),
                 in_=x_scales[:, SCALE_ROWS * q : SCALE_ROWS * (q + 1), :].bitcast(I32),
             )
+        nc.sync.dma_start(out=taps_sb[:], in_=taps.rearrange("(p t) k -> p (t k)", t=PACK))
         load_w1(0)
-        load_w1(1)
         load_words(1)
+        load_w1(1)
+        load_w1(2)
         nc.sync.dma_start(out=w2_raw[:], in_=w2.rearrange("(p j) m -> p j m", j=PACK))
         nc.sync.dma_start(order_sb[:], order)
-        nc.sync.dma_start(out=taps_sb[:], in_=taps.rearrange("(p t) k -> p (t k)", t=PACK))
         nc.sync.dma_start(back_sb[:], back)
 
         nc.gpsimd.memset(zeros[:], 0.0)
@@ -100,15 +106,30 @@ def tile_picked_yserial_silu_p_kernel(
         nc.vector.tensor_copy(x_codes0[:], x_table[0][:].bitcast(U32).indirect(offs_sb[:]))
         nc.vector.tensor_copy(x_scale[:], scale_table[:].indirect(offs_sb[:]))
 
+        taps3 = taps_sb[:].rearrange("p (t k) -> p t k", k=TAPS)
+        square = sb("square", [P, PACK], F32)
+        shift = sb("shift", [P, PACK], F32)
+        lead = sb("lead", [P, PACK], F32)
+        inverse = sb("inverse", [P, PACK], F32)
+        ratio = sb("ratio", [P, PACK, TAPS - 1], F32)
+        nc.gpsimd.tensor_tensor(square[:], taps3[:, :, 0], taps3[:, :, 0], MULT)
+        nc.gpsimd.tensor_scalar(shift[:], square[:], TINY * TINY, 2.0 * TINY, op0=IS_LT, op1=MULT)
+        nc.gpsimd.tensor_tensor(lead[:], taps3[:, :, 0], shift[:], ADD)
+        nc.vector.reciprocal(inverse[:], lead[:])
+        nc.gpsimd.tensor_tensor(
+            ratio[:], taps3[:, :, 1:], inverse[:].unsqueeze(2).to_broadcast([P, PACK, TAPS - 1]), MULT
+        )
+
         w1_bf = [[sb("w1_bf%d_%d" % (o, u), [P, 2 * P * PACK], BF16) for u in range(2)] for o in range(PASSES)]
         w1_codes = [[sb("w1_codes%d_%d" % (o, u), [P, 2 * P], U32) for u in range(2)] for o in range(PASSES)]
         w1_scale = [[sb("w1_scale%d_%d" % (o, u), [P, 2 * P], U8) for u in range(2)] for o in range(PASSES)]
 
-        def weave_w1(o):
+        def weave_w1(n):
+            o, first, count = w1_parts[n]
             for u, copy in enumerate((nc.vector.tensor_copy, nc.scalar.copy)):
                 copy(
-                    out=w1_bf[o][u][:].rearrange("p (e m j) -> p m j e", e=2, j=PACK),
-                    in_=w1_raw[o][:].rearrange("p j (m t) -> p m j t", t=PACK)[:, :, :, 2 * u : 2 * u + 2],
+                    out=w1_bf[o][u][:].rearrange("p (e m j) -> p m j e", e=2, j=PACK)[:, :, first : first + count, :],
+                    in_=w1_raw[n][:].rearrange("p j (m t) -> p m j t", t=PACK)[:, :, :, 2 * u : 2 * u + 2],
                 )
 
         def quantize_w1(o, first_tile, tiles):
@@ -120,7 +141,7 @@ def tile_picked_yserial_silu_p_kernel(
                 in_=w1_bf[o][u][:, e * P * PACK : (e + tiles) * P * PACK],
             )
 
-        y_first = [psum.tile([P, width], F32, name="y_first%d" % n) for n, (start, width) in enumerate(FIRST_PIECES)]
+        y_first = [psum.tile([P, HALF], F32, name="y_first%d" % h) for h in range(2)]
         y_rest = [psum.tile([P, S], F32, name="y_rest%d" % t) for t in range(1, PACK)]
 
         def product1(o, t, acc, x_codes, cols):
@@ -135,27 +156,27 @@ def tile_picked_yserial_silu_p_kernel(
                 stop=(o == PASSES - 1),
             )
 
+        def products(o, x_codes):
+            for h in range(2):
+                product1(o, 0, y_first[h][:], x_codes, halves[h])
+            for t in range(1, PACK):
+                product1(o, t, y_rest[t - 1][:], x_codes, slice(0, S))
+
         weave_w1(0)
         quantize_w1(0, 0, 2)
         quantize_w1(0, 2, 2)
-        for n, (start, width) in enumerate(FIRST_PIECES):
-            product1(0, 0, y_first[n][:], x_codes0, slice(start, start + width))
-        for t in range(1, PACK):
-            product1(0, t, y_rest[t - 1][:], x_codes0, slice(0, S))
+        products(0, x_codes0)
 
-        weave_w1(1)
-        quantize_w1(1, 0, 1)
         x_codes1 = sb("x_codes1", [P, S], U32)
-        for n, (start, width) in enumerate(FIRST_PIECES):
-            cols = slice(start, start + width)
-            entries = offs_sb[:, start // PER_COLUMN : (start + width) // PER_COLUMN]
-            nc.vector.tensor_copy(x_codes1[:, cols], x_table[1][:].bitcast(U32).indirect(entries))
-            product1(1, 0, y_first[n][:], x_codes1, cols)
-            nc.scalar.copy(out=y[0][:, cols], in_=y_first[n][:])
+        nc.vector.tensor_copy(x_codes1[:], x_table[1][:].bitcast(U32).indirect(offs_sb[:]))
+        weave_w1(1)
+        weave_w1(2)
+        quantize_w1(1, 0, 1)
         quantize_w1(1, 1, 1)
         quantize_w1(1, 2, 2)
-        for t in range(1, PACK):
-            product1(1, t, y_rest[t - 1][:], x_codes1, slice(0, S))
+        products(1, x_codes1)
+        nc.scalar.copy(out=y[0][:, halves[0]], in_=y_first[0][:])
+        nc.vector.tensor_copy(out=y[0][:, halves[1]], in_=y_first[1][:])
 
         w2_bf = sb("w2_bf", [P, N * PACK], BF16)
         w2_codes = sb("w2_codes", [P, N], U32)
@@ -169,29 +190,23 @@ def tile_picked_yserial_silu_p_kernel(
         gg = [sb("gg%d" % t, [P, PAD + S], F32) for t in range(PACK)]
         for t in range(PACK):
             nc.gpsimd.memset(gg[t][:, :PAD], 0.0)
-        on_tensor = {0: S, PACK - 1: LAST_ON_TENSOR}
-        on_vector = {t: slice(on_tensor.get(t, 0), S) for t in range(1, PACK)}
-        shared = sb("shared", [P, (TAPS + 1) * S], F32, tag="w1_codes1_1")
-        scaled_last = sb("scaled_last", [P, TAPS * LAST_ON_TENSOR], F32)
-        scaled = {
-            0: [shared[:, k * S : (k + 1) * S] for k in range(TAPS)],
-            PACK - 1: [scaled_last[:, k * LAST_ON_TENSOR : (k + 1) * LAST_ON_TENSOR] for k in range(TAPS)],
-        }
-        summed_sb = {t: sb("summed_sb%d" % t, [P, width], F32) for t, width in on_tensor.items()}
-        filt = {1: shared[:, TAPS * S :], 2: sb("filt2", [P, S], F32)[:], 3: sb("filt3", [P, S], F32)[:]}
+        on_tensor = {0: S, 1: S, 2: SPLIT_ON_TENSOR}
+        on_vector = {2: slice(SPLIT_ON_TENSOR, S), 3: slice(0, S)}
+        shared = sb("shared", [P, len(on_tensor), TAPS - 1, S], F32, tag="w1_codes1_1")
+        summed_sb = {0: rr[3][:, :S], 1: rr[2][:, :S], 2: sb("summed_sb2", [P, SPLIT_ON_TENSOR], F32)[:]}
+        filt = {t: sb("filt%d" % t, [P, S], F32) for t in on_vector}
         ident = sb("ident", [P, P], F32)
         make_identity(nc, ident[:])
         summed = {
-            0: psum.tile([P, S], F32, name="summed0", tag="y_first0"),
-            PACK - 1: psum.tile([P, LAST_ON_TENSOR], F32, name="summed3"),
+            0: psum.tile([P, S], F32, name="summed0"),
+            1: psum.tile([P, S], F32, name="summed1"),
+            2: psum.tile([P, S], F32, name="summed2", tag="y_first1"),
         }
         restored = {
-            0: psum.tile([P, S], F32, name="restored0", tag="y_first1"),
-            PACK - 1: psum.tile([P, LAST_ON_TENSOR], F32, name="restored3"),
+            0: psum.tile([P, S], F32, name="restored0"),
+            1: psum.tile([P, S], F32, name="restored1", tag="y_first0"),
+            2: psum.tile([P, S], F32, name="restored2", tag="y_rest1"),
         }
-
-        def tap(t, k):
-            return taps_sb[:, TAPS * t + k : TAPS * t + k + 1]
 
         def delayed(t, k):
             return gg[t][:, PAD - k : PAD - k + S]
@@ -200,55 +215,66 @@ def tile_picked_yserial_silu_p_kernel(
             return [slice(start, start + P) for start in range(0, on_tensor[t], P)]
 
         def sum_by_transposes(t):
-            for k in range(TAPS):
-                nc.scalar.activation(scaled[t][k], delayed(t, k)[:, : on_tensor[t]], COPY, scale=tap(t, k))
+            order_of_terms = (0, 1, 2) if t == 0 else (1, 0, 2)
+            for k in order_of_terms:
+                term = delayed(t, 0)
+                if k > 0:
+                    term = shared[:, t, k - 1, :]
+                    nc.scalar.activation(
+                        term[:, : on_tensor[t]], delayed(t, k)[:, : on_tensor[t]], COPY, scale=ratio[:, t, k - 1 : k]
+                    )
                 for chunk in chunks(t):
                     nc.tensor.matmul(
                         summed[t][:, chunk],
-                        lhsT=scaled[t][k][:, chunk],
+                        lhsT=term[:, chunk],
                         rhs=ident[:],
                         is_transpose=True,
-                        start=(k == 0 and chunk.start == 0),
+                        start=(k == order_of_terms[0] and chunk.start == 0),
                         stop=(k == TAPS - 1 and chunk.stop == on_tensor[t]),
                     )
 
         def turn_back(t):
-            nc.scalar.copy(out=summed_sb[t][:], in_=summed[t][:])
+            nc.scalar.copy(out=summed_sb[t], in_=summed[t][:, : on_tensor[t]])
             for chunk in chunks(t):
                 nc.tensor.transpose(restored[t][:, chunk], summed_sb[t][:, chunk], ident[:])
+
+        def silu(t, cols, source):
+            nc.scalar.activation(rr[t][:, cols], source[:, cols], SILU, scale=lead[:, t : t + 1])
 
         for t in range(PACK):
             if t > 0:
                 nc.scalar.copy(out=y[t][:, :S], in_=y_rest[t - 1][:])
             nc.vector.tensor_copy(delayed(t, 0), y[t].indirect(order_sb[:]))
 
-        sum_by_transposes(0)
-        for t, cols in on_vector.items():
-            nc.scalar.activation(filt[t][:, cols], delayed(t, 0)[:, cols], COPY, scale=tap(t, 0))
-        sum_by_transposes(PACK - 1)
-        for t in on_tensor:
-            turn_back(t)
-
-        for step in range(2, PACK + TAPS - 1):
-            for k in range(1, TAPS):
-                t = step - k
-                if t in on_vector:
-                    acc = filt[t][:, on_vector[t]]
-                    nc.vector.scalar_tensor_tensor(
-                        out=acc, in0=delayed(t, k)[:, on_vector[t]], scalar=tap(t, k), in1=acc, op0=MULT, op1=ADD
-                    )
-        for t, cols in on_vector.items():
-            nc.scalar.activation(rr[t][:, cols], filt[t][:, cols], SILU)
-        for t in (PACK - 1, 0):
-            nc.scalar.activation(rr[t][:, : on_tensor[t]], restored[t][:], SILU)
-
-        for t in (1, 2):
-            nc.vector.tensor_tensor(z[:, t, :S], rr[t][:].indirect(back_sb[:]), y[t][:, :S], ADD)
-        for h in (1, 0):
-            for t in (3, 0):
-                nc.vector.tensor_tensor(
-                    z[:, t, halves[h]], rr[t][:].indirect(back_sb[:, list_halves[h]]), y[t][:, halves[h]], ADD
+        for k in range(1, TAPS):
+            for t, cols in on_vector.items():
+                nc.vector.scalar_tensor_tensor(
+                    out=filt[t][:, cols],
+                    in0=delayed(t, k)[:, cols],
+                    scalar=ratio[:, t, k - 1 : k],
+                    in1=(delayed(t, 0) if k == 1 else filt[t])[:, cols],
+                    op0=MULT,
+                    op1=ADD,
                 )
+
+        sum_by_transposes(0)
+        sum_by_transposes(1)
+        turn_back(0)
+        sum_by_transposes(2)
+        turn_back(1)
+        silu(0, slice(0, S), restored[0])
+        turn_back(2)
+        silu(3, on_vector[3], filt[3])
+        silu(1, slice(0, S), restored[1])
+        silu(2, on_vector[2], filt[2])
+        silu(2, slice(0, on_tensor[2]), restored[2])
+
+        for t in (0, 3):
+            nc.vector.tensor_tensor(z[:, t, :S], rr[t][:].indirect(back_sb[:]), y[t][:, :S], ADD)
+        for t, h in ((1, 1), (2, 1), (2, 0), (1, 0)):
+            nc.vector.tensor_tensor(
+                z[:, t, halves[h]], rr[t][:].indirect(back_sb[:, list_halves[h]]), y[t][:, halves[h]], ADD
+            )
 
         out_sb = sb("out_sb", [P, S], F32)
         z_codes = sb("z_codes", [P, S], U32)
@@ -260,9 +286,8 @@ def tile_picked_yserial_silu_p_kernel(
         ]
         pieces = upper + lower
         z_bf = [sb("z_bf%d" % n, [P, piece[1] * PACK], BF16) for n, piece in enumerate(pieces)]
-        out_ps = [
-            psum.tile([P, piece[1]], F32, name="out_ps%d" % n, tag="y_rest%d" % (n + 1)) for n, piece in enumerate(pieces)
-        ]
+        out_tags = ("y_rest2", "y_rest3", "summed0")
+        out_ps = [psum.tile([P, piece[1]], F32, name="out_ps%d" % n, tag=out_tags[n]) for n, piece in enumerate(pieces)]
         for n, (start, width, weave, leave) in enumerate(pieces):
             weave(
                 out=z_bf[n][:].rearrange("p (c i t) -> p c t i", i=LINE, t=PACK),

@@ -63,7 +63,7 @@ def tile_picked_yserial_silu_p_kernel(
         taps_sb = sb("taps_sb", [P, PACK * TAPS], F32)
         z_home = sb("z_home", [P, PACK * Z_STEP], F32)
         z = z_home[:].rearrange("p (t c) -> p t c", t=PACK)
-        y_start = Z_STEP - HALF
+        y_start = 1 * Z_STEP - HALF
         y = [
             z_home[:, y_start : y_start + Y_WINDOW] if t == 2 else sb("y%d" % t, [P, Y_WINDOW], F32)[:]
             for t in range(PACK)
@@ -190,84 +190,106 @@ def tile_picked_yserial_silu_p_kernel(
         gg = [sb("gg%d" % t, [P, PAD + S], F32) for t in range(PACK)]
         for t in range(PACK):
             nc.gpsimd.memset(gg[t][:, :PAD], 0.0)
-        on_tensor = {0: S, 1: S, 2: SPLIT_ON_TENSOR}
-        on_vector = {2: slice(SPLIT_ON_TENSOR, S), 3: slice(0, S)}
-        shared = sb("shared", [P, len(on_tensor), TAPS - 1, S], F32, tag="w1_codes1_1")
-        summed_sb = {0: rr[3][:, :S], 1: rr[2][:, :S], 2: sb("summed_sb2", [P, SPLIT_ON_TENSOR], F32)[:]}
-        filt = {t: sb("filt%d" % t, [P, S], F32) for t in on_vector}
+        on_gpsimd = {}
+        on_tensor = {0: slice(0, S), 1: slice(0, S), 2: slice(HALF, S)}
+        on_vector = {2: slice(0, HALF), 3: slice(0, S)}
+        shared = sb("shared", [P, PACK, TAPS - 1, S], F32, tag="w1_codes1_1")
+        scaled = {(t, k): shared[:, t, k - 1, :] for t in range(PACK) for k in range(1, TAPS)}
+        summed_sb = {0: sb("summed_sb0", [P, S], F32)[:], 1: rr[2][:, :S], 2: sb("summed_sb2", [P, S], F32)[:]}
+        partial = sb("partial", [P, S], F32)
+        filt = {t: sb("filt%d" % t, [P, S], F32) for t in range(PACK) if t in on_vector or t in on_gpsimd}
+        flat = shared[:].rearrange("p t k c -> p (t k c)")
+        filt[2] = flat[:, 0:S][:, 0:S]
+        filt[3] = flat[:, HALF : HALF + S]
+        scaled[0, 2] = rr[3][:, :S]
+        scaled[1, 1] = flat[:, 2 * S : 3 * S]
+        scaled[1, 2] = rr[3][:, :S]
+        scaled[2, 1] = flat[:, 2 * S : 3 * S]
+        scaled[2, 2] = summed_sb[0]
         ident = sb("ident", [P, P], F32)
         make_identity(nc, ident[:])
-        summed = {
-            0: psum.tile([P, S], F32, name="summed0"),
-            1: psum.tile([P, S], F32, name="summed1"),
-            2: psum.tile([P, S], F32, name="summed2", tag="y_first1"),
-        }
-        restored = {
-            0: psum.tile([P, S], F32, name="restored0"),
-            1: psum.tile([P, S], F32, name="restored1", tag="y_first0"),
-            2: psum.tile([P, S], F32, name="restored2", tag="y_rest1"),
-        }
+        sum_tags = {0: "summed0", 1: "summed1", 2: "y_first1", 3: "y_rest2"}
+        back_tags = {0: "restored0", 1: "y_first0", 2: "y_rest1", 3: "y_rest3"}
+        summed = {t: psum.tile([P, S], F32, name="summed%d" % t, tag=sum_tags[t]) for t in on_tensor}
+        restored = {t: psum.tile([P, S], F32, name="restored%d" % t, tag=back_tags[t]) for t in on_tensor}
 
         def delayed(t, k):
             return gg[t][:, PAD - k : PAD - k + S]
 
         def chunks(t):
-            return [slice(start, start + P) for start in range(0, on_tensor[t], P)]
+            return [slice(start, start + P) for start in range(on_tensor[t].start, on_tensor[t].stop, P)]
 
-        def sum_by_transposes(t):
-            order_of_terms = (0, 1, 2) if t == 0 else (1, 0, 2)
+        def scale_term(t, k, cols):
+            nc.scalar.activation(scaled[t, k][:, cols], delayed(t, k)[:, cols], COPY, scale=ratio[:, t, k - 1 : k])
+
+        def sum_by_transposes(t, order_of_terms):
             for k in order_of_terms:
                 term = delayed(t, 0)
                 if k > 0:
-                    term = shared[:, t, k - 1, :]
-                    nc.scalar.activation(
-                        term[:, : on_tensor[t]], delayed(t, k)[:, : on_tensor[t]], COPY, scale=ratio[:, t, k - 1 : k]
-                    )
+                    term = scaled[t, k]
+                    scale_term(t, k, on_tensor[t])
                 for chunk in chunks(t):
                     nc.tensor.matmul(
                         summed[t][:, chunk],
                         lhsT=term[:, chunk],
                         rhs=ident[:],
                         is_transpose=True,
-                        start=(k == order_of_terms[0] and chunk.start == 0),
-                        stop=(k == TAPS - 1 and chunk.stop == on_tensor[t]),
+                        start=(k == order_of_terms[0] and chunk.start == on_tensor[t].start),
+                        stop=(k == order_of_terms[-1] and chunk.stop == on_tensor[t].stop),
                     )
 
         def turn_back(t):
-            nc.scalar.copy(out=summed_sb[t], in_=summed[t][:, : on_tensor[t]])
+            nc.scalar.copy(out=summed_sb[t][:, on_tensor[t]], in_=summed[t][:, on_tensor[t]])
             for chunk in chunks(t):
                 nc.tensor.transpose(restored[t][:, chunk], summed_sb[t][:, chunk], ident[:])
+
+        def sum_on_gpsimd(t):
+            cols = on_gpsimd[t]
+            for k in range(1, TAPS):
+                nc.gpsimd.tensor_scalar(
+                    scaled[t, k][:, cols], delayed(t, k)[:, cols], ratio[:, t, k - 1 : k], 0.0, op0=MULT, op1=ADD
+                )
+            nc.gpsimd.tensor_tensor(partial[:, cols], delayed(t, 0)[:, cols], scaled[t, 1][:, cols], ADD)
+            nc.gpsimd.tensor_tensor(filt[t][:, cols], partial[:, cols], scaled[t, 2][:, cols], ADD)
+
+        def add_tap(t, k):
+            cols = on_vector[t]
+            nc.vector.scalar_tensor_tensor(
+                out=filt[t][:, cols],
+                in0=delayed(t, k)[:, cols],
+                scalar=ratio[:, t, k - 1 : k],
+                in1=(delayed(t, 0) if k == 1 else filt[t])[:, cols],
+                op0=MULT,
+                op1=ADD,
+            )
 
         def silu(t, cols, source):
             nc.scalar.activation(rr[t][:, cols], source[:, cols], SILU, scale=lead[:, t : t + 1])
 
-        for t in range(PACK):
+        def gather_by_order(t):
             if t > 0:
                 nc.scalar.copy(out=y[t][:, :S], in_=y_rest[t - 1][:])
             nc.vector.tensor_copy(delayed(t, 0), y[t].indirect(order_sb[:]))
 
-        for k in range(1, TAPS):
-            for t, cols in on_vector.items():
-                nc.vector.scalar_tensor_tensor(
-                    out=filt[t][:, cols],
-                    in0=delayed(t, k)[:, cols],
-                    scalar=ratio[:, t, k - 1 : k],
-                    in1=(delayed(t, 0) if k == 1 else filt[t])[:, cols],
-                    op0=MULT,
-                    op1=ADD,
-                )
-
-        sum_by_transposes(0)
-        sum_by_transposes(1)
+        gather_by_order(0)
+        gather_by_order(1)
+        gather_by_order(2)
+        gather_by_order(3)
+        sum_by_transposes(0, (0, 1, 2))
         turn_back(0)
-        sum_by_transposes(2)
+        sum_by_transposes(1, (1, 0, 2))
+        silu(0, on_tensor[0], restored[0])
+        sum_by_transposes(2, (1, 0, 2))
+        add_tap(2, 1)
+        add_tap(3, 1)
+        add_tap(2, 2)
+        add_tap(3, 2)
         turn_back(1)
-        silu(0, slice(0, S), restored[0])
-        turn_back(2)
         silu(3, on_vector[3], filt[3])
-        silu(1, slice(0, S), restored[1])
+        turn_back(2)
+        silu(1, on_tensor[1], restored[1])
         silu(2, on_vector[2], filt[2])
-        silu(2, slice(0, on_tensor[2]), restored[2])
+        silu(2, on_tensor[2], restored[2])
 
         for t in (0, 3):
             nc.vector.tensor_tensor(z[:, t, :S], rr[t][:].indirect(back_sb[:]), y[t][:, :S], ADD)

@@ -32,7 +32,7 @@ QUADRANTS = 4
 SCALE_ROWS = 4
 Y_WINDOW = 704
 RR_WINDOW = 528
-Z_STEP = 1024
+Z_STEP = 704
 PAD = 8
 SPLIT_ON_TENSOR = HALF
 TINY = 2.0**-32
@@ -61,11 +61,12 @@ def tile_picked_yserial_silu_p_kernel(
         w1_raw = [sb("w1_raw%d" % n, [P, part[2], H], F32) for n, part in enumerate(w1_parts)]
         w2_raw = sb("w2_raw", [P, PACK, N], F32)
         taps_sb = sb("taps_sb", [P, PACK * TAPS], F32)
-        z_home = sb("z_home", [P, PACK * Z_STEP], F32)
-        z = z_home[:].rearrange("p (t c) -> p t c", t=PACK)
-        y_start = 1 * Z_STEP - HALF
+        z_lower = sb("z_lower", [P, PACK * Z_STEP], F32)
+        z_upper = sb("z_upper", [P, PACK, HALF], F32)
+        z = [z_lower[:].rearrange("p (t c) -> p t c", t=PACK), z_upper[:]]
+        y_start = Z_STEP - HALF
         y = [
-            z_home[:, y_start : y_start + Y_WINDOW] if t == 2 else sb("y%d" % t, [P, Y_WINDOW], F32)[:]
+            z_lower[:, y_start : y_start + Y_WINDOW] if t == 2 else sb("y%d" % t, [P, Y_WINDOW], F32)[:]
             for t in range(PACK)
         ]
         rr = [sb("rr%d" % t, [P, RR_WINDOW], F32) for t in range(PACK)]
@@ -132,23 +133,34 @@ def tile_picked_yserial_silu_p_kernel(
                     in_=w1_raw[n][:].rearrange("p j (m t) -> p m j t", t=PACK)[:, :, :, 2 * u : 2 * u + 2],
                 )
 
+        last_codes0 = sb("last_codes0", [P, P], U32)
+
+        def codes_of(o, first_tile, tiles):
+            if (o, first_tile) == (PASSES - 1, 0):
+                return last_codes0[:]
+            u, e = divmod(first_tile, 2)
+            return w1_codes[o][u][:, e * P : (e + tiles) * P]
+
         def quantize_w1(o, first_tile, tiles):
             u, e = divmod(first_tile, 2)
             cols = slice(e * P, (e + tiles) * P)
             nc.vector.quantize_mx(
-                out=w1_codes[o][u][:, cols].bitcast(FP8X4),
+                out=codes_of(o, first_tile, tiles).bitcast(FP8X4),
                 scales=w1_scale[o][u][:, cols],
                 in_=w1_bf[o][u][:, e * P * PACK : (e + tiles) * P * PACK],
             )
 
-        y_first = [psum.tile([P, HALF], F32, name="y_first%d" % h) for h in range(2)]
+        first_pieces = (slice(0, HALF), slice(HALF, HALF + QUARTER), slice(HALF + QUARTER, S))
+        y_first = [
+            psum.tile([P, cols.stop - cols.start], F32, name="y_first%d" % n) for n, cols in enumerate(first_pieces)
+        ]
         y_rest = [psum.tile([P, S], F32, name="y_rest%d" % t) for t in range(1, PACK)]
 
         def product1(o, t, acc, x_codes, cols):
             m = slice((t % 2) * P, (t % 2 + 1) * P)
             nc.tensor.matmul_mx(
                 out=acc,
-                lhsT=w1_codes[o][t // 2][:, m].bitcast(FP8X4),
+                lhsT=codes_of(o, t, 1).bitcast(FP8X4),
                 lhsT_scale=w1_scale[o][t // 2][:, m],
                 rhs=x_codes[:, cols].bitcast(FP8X4),
                 rhs_scale=x_scale[SCALE_ROWS * o :, cols],
@@ -157,8 +169,8 @@ def tile_picked_yserial_silu_p_kernel(
             )
 
         def products(o, x_codes):
-            for h in range(2):
-                product1(o, 0, y_first[h][:], x_codes, halves[h])
+            for n, cols in enumerate(first_pieces):
+                product1(o, 0, y_first[n][:], x_codes, cols)
             for t in range(1, PACK):
                 product1(o, t, y_rest[t - 1][:], x_codes, slice(0, S))
 
@@ -175,11 +187,11 @@ def tile_picked_yserial_silu_p_kernel(
         quantize_w1(1, 1, 1)
         quantize_w1(1, 2, 2)
         products(1, x_codes1)
-        nc.scalar.copy(out=y[0][:, halves[0]], in_=y_first[0][:])
-        nc.vector.tensor_copy(out=y[0][:, halves[1]], in_=y_first[1][:])
+        for n, copy in enumerate((nc.scalar.copy, nc.vector.tensor_copy, nc.vector.tensor_copy)):
+            copy(out=y[0][:, first_pieces[n]], in_=y_first[n][:])
 
         w2_bf = sb("w2_bf", [P, N * PACK], BF16)
-        w2_codes = sb("w2_codes", [P, N], U32)
+        w2_codes = sb("w2_codes", [P, N], U32, tag="last_codes0")
         w2_scale = sb("w2_scale", [P, N], U8)
         nc.scalar.copy(
             out=w2_bf[:].rearrange("p (c i j) -> p c j i", i=LINE, j=PACK),
@@ -208,7 +220,7 @@ def tile_picked_yserial_silu_p_kernel(
         scaled[2, 2] = summed_sb[0]
         ident = sb("ident", [P, P], F32)
         make_identity(nc, ident[:])
-        sum_tags = {0: "summed0", 1: "summed1", 2: "y_first1", 3: "y_rest2"}
+        sum_tags = {0: "summed0", 1: "y_first2", 2: "y_first1", 3: "y_rest2"}
         back_tags = {0: "restored0", 1: "y_first0", 2: "y_rest1", 3: "y_rest3"}
         summed = {t: psum.tile([P, S], F32, name="summed%d" % t, tag=sum_tags[t]) for t in on_tensor}
         restored = {t: psum.tile([P, S], F32, name="restored%d" % t, tag=back_tags[t]) for t in on_tensor}
@@ -291,16 +303,12 @@ def tile_picked_yserial_silu_p_kernel(
         silu(2, on_vector[2], filt[2])
         silu(2, on_tensor[2], restored[2])
 
-        for t in (0, 3):
-            nc.vector.tensor_tensor(z[:, t, :S], rr[t][:].indirect(back_sb[:]), y[t][:, :S], ADD)
-        for t, h in ((1, 1), (2, 1), (2, 0), (1, 0)):
+        for t, h in ((0, 0), (0, 1), (3, 0), (3, 1), (1, 1), (2, 1), (2, 0), (1, 0)):
             nc.vector.tensor_tensor(
-                z[:, t, halves[h]], rr[t][:].indirect(back_sb[:, list_halves[h]]), y[t][:, halves[h]], ADD
+                z[h][:, t, :HALF], rr[t][:].indirect(back_sb[:, list_halves[h]]), y[t][:, halves[h]], ADD
             )
 
         out_sb = sb("out_sb", [P, S], F32)
-        z_codes = sb("z_codes", [P, S], U32)
-        z_scale = sb("z_scale", [P, S], U8)
         upper = [(HALF, HALF, nc.scalar.copy, nc.scalar.copy)]
         lower = [
             (0, QUARTER, nc.vector.tensor_copy, nc.scalar.copy),
@@ -313,17 +321,19 @@ def tile_picked_yserial_silu_p_kernel(
         for n, (start, width, weave, leave) in enumerate(pieces):
             weave(
                 out=z_bf[n][:].rearrange("p (c i t) -> p c t i", i=LINE, t=PACK),
-                in_=z[:, :, start : start + width].rearrange("p t (c i) -> p c t i", i=LINE),
+                in_=z[start // HALF][:, :, start % HALF : start % HALF + width].rearrange("p t (c i) -> p c t i", i=LINE),
             )
         for n, (start, width, weave, leave) in enumerate(pieces):
             cols = slice(start, start + width)
-            nc.vector.quantize_mx(out=z_codes[:, cols].bitcast(FP8X4), scales=z_scale[:, cols], in_=z_bf[n][:])
+            z_codes = sb("z_codes%d" % n, [P, width], U32, tag="z_upper" if n == 1 else "")
+            z_scale = sb("z_scale%d" % n, [P, width], U8)
+            nc.vector.quantize_mx(out=z_codes[:].bitcast(FP8X4), scales=z_scale[:], in_=z_bf[n][:])
             nc.tensor.matmul_mx(
                 out=out_ps[n][:],
                 lhsT=w2_codes[:].bitcast(FP8X4),
                 lhsT_scale=w2_scale[:],
-                rhs=z_codes[:, cols].bitcast(FP8X4),
-                rhs_scale=z_scale[:, cols],
+                rhs=z_codes[:].bitcast(FP8X4),
+                rhs_scale=z_scale[:],
                 start=True,
                 stop=True,
             )

@@ -133,19 +133,11 @@ def tile_picked_yserial_silu_p_kernel(
                     in_=w1_raw[n][:].rearrange("p j (m t) -> p m j t", t=PACK)[:, :, :, 2 * u : 2 * u + 2],
                 )
 
-        last_codes0 = sb("last_codes0", [P, P], U32)
-
-        def codes_of(o, first_tile, tiles):
-            if (o, first_tile) == (PASSES - 1, 0):
-                return last_codes0[:]
-            u, e = divmod(first_tile, 2)
-            return w1_codes[o][u][:, e * P : (e + tiles) * P]
-
         def quantize_w1(o, first_tile, tiles):
             u, e = divmod(first_tile, 2)
             cols = slice(e * P, (e + tiles) * P)
             nc.vector.quantize_mx(
-                out=codes_of(o, first_tile, tiles).bitcast(FP8X4),
+                out=w1_codes[o][u][:, cols].bitcast(FP8X4),
                 scales=w1_scale[o][u][:, cols],
                 in_=w1_bf[o][u][:, e * P * PACK : (e + tiles) * P * PACK],
             )
@@ -160,7 +152,7 @@ def tile_picked_yserial_silu_p_kernel(
             m = slice((t % 2) * P, (t % 2 + 1) * P)
             nc.tensor.matmul_mx(
                 out=acc,
-                lhsT=codes_of(o, t, 1).bitcast(FP8X4),
+                lhsT=w1_codes[o][t // 2][:, m].bitcast(FP8X4),
                 lhsT_scale=w1_scale[o][t // 2][:, m],
                 rhs=x_codes[:, cols].bitcast(FP8X4),
                 rhs_scale=x_scale[SCALE_ROWS * o :, cols],
@@ -190,34 +182,27 @@ def tile_picked_yserial_silu_p_kernel(
         for n, copy in enumerate((nc.scalar.copy, nc.vector.tensor_copy, nc.vector.tensor_copy)):
             copy(out=y[0][:, first_pieces[n]], in_=y_first[n][:])
 
-        w2_bf = sb("w2_bf", [P, N * PACK], BF16)
-        w2_codes = sb("w2_codes", [P, N], U32, tag="last_codes0")
-        w2_scale = sb("w2_scale", [P, N], U8)
-        nc.scalar.copy(
-            out=w2_bf[:].rearrange("p (c i j) -> p c j i", i=LINE, j=PACK),
-            in_=w2_raw[:].rearrange("p j (c i) -> p c j i", i=LINE),
-        )
-        nc.vector.quantize_mx(out=w2_codes[:].bitcast(FP8X4), scales=w2_scale[:], in_=w2_bf[:])
-
         gg = [sb("gg%d" % t, [P, PAD + S], F32) for t in range(PACK)]
         for t in range(PACK):
             nc.gpsimd.memset(gg[t][:, :PAD], 0.0)
         on_gpsimd = {}
         on_tensor = {0: slice(0, S), 1: slice(0, S), 2: slice(HALF, S)}
         on_vector = {2: slice(0, HALF), 3: slice(0, S)}
+        scaled_on_gpsimd = ((0, 1), (1, 2))
         shared = sb("shared", [P, PACK, TAPS - 1, S], F32, tag="w1_codes1_1")
         scaled = {(t, k): shared[:, t, k - 1, :] for t in range(PACK) for k in range(1, TAPS)}
         summed_sb = {0: sb("summed_sb0", [P, S], F32)[:], 1: rr[2][:, :S], 2: sb("summed_sb2", [P, S], F32)[:]}
         partial = sb("partial", [P, S], F32)
         filt = {t: sb("filt%d" % t, [P, S], F32) for t in range(PACK) if t in on_vector or t in on_gpsimd}
         flat = shared[:].rearrange("p t k c -> p (t k c)")
-        filt[2] = flat[:, 0:S][:, 0:S]
-        filt[3] = flat[:, HALF : HALF + S]
         scaled[0, 2] = rr[3][:, :S]
-        scaled[1, 1] = flat[:, 2 * S : 3 * S]
+        scaled[1, 1] = flat[:, 2 * S + HALF : 3 * S + HALF]
         scaled[1, 2] = rr[3][:, :S]
-        scaled[2, 1] = flat[:, 2 * S : 3 * S]
-        scaled[2, 2] = summed_sb[0]
+        scaled[0, 1] = flat[:, S : 2 * S]
+        scaled[2, 1] = flat[:, S - 64 : 2 * S - 64]
+        scaled[2, 2] = flat[:, S + 192 : 2 * S + 192]
+        filt[2] = flat[:, 2 * S + HALF : 3 * S + HALF]
+        filt[3] = flat[:, 3 * S : 4 * S]
         ident = sb("ident", [P, P], F32)
         make_identity(nc, ident[:])
         sum_tags = {0: "summed0", 1: "y_first2", 2: "y_first1", 3: "y_rest2"}
@@ -232,7 +217,11 @@ def tile_picked_yserial_silu_p_kernel(
             return [slice(start, start + P) for start in range(on_tensor[t].start, on_tensor[t].stop, P)]
 
         def scale_term(t, k, cols):
-            nc.scalar.activation(scaled[t, k][:, cols], delayed(t, k)[:, cols], COPY, scale=ratio[:, t, k - 1 : k])
+            factor = ratio[:, t, k - 1 : k]
+            if (t, k) in scaled_on_gpsimd:
+                nc.gpsimd.tensor_scalar(scaled[t, k][:, cols], delayed(t, k)[:, cols], factor, 0.0, op0=MULT, op1=ADD)
+            else:
+                nc.scalar.activation(scaled[t, k][:, cols], delayed(t, k)[:, cols], COPY, scale=factor)
 
         def sum_by_transposes(t, order_of_terms):
             for k in order_of_terms:
@@ -252,7 +241,7 @@ def tile_picked_yserial_silu_p_kernel(
 
         def turn_back(t):
             nc.scalar.copy(out=summed_sb[t][:, on_tensor[t]], in_=summed[t][:, on_tensor[t]])
-            for chunk in chunks(t):
+            for chunk in reversed(chunks(t)):
                 nc.tensor.transpose(restored[t][:, chunk], summed_sb[t][:, chunk], ident[:])
 
         def sum_on_gpsimd(t):
@@ -287,11 +276,11 @@ def tile_picked_yserial_silu_p_kernel(
         gather_by_order(1)
         gather_by_order(2)
         gather_by_order(3)
-        sum_by_transposes(0, (0, 1, 2))
+        sum_by_transposes(0, (0, 2, 1))
         turn_back(0)
         sum_by_transposes(1, (1, 0, 2))
-        silu(0, on_tensor[0], restored[0])
         sum_by_transposes(2, (1, 0, 2))
+        silu(0, on_tensor[0], restored[0])
         add_tap(2, 1)
         add_tap(3, 1)
         add_tap(2, 2)
@@ -303,13 +292,23 @@ def tile_picked_yserial_silu_p_kernel(
         silu(2, on_vector[2], filt[2])
         silu(2, on_tensor[2], restored[2])
 
+        w2_bf = sb("w2_bf", [P, N * PACK], BF16, tag="summed_sb2")
+        w2_scale = sb("w2_scale", [P, N], U8)
+        nc.scalar.copy(
+            out=w2_bf[:].rearrange("p (c i j) -> p c j i", i=LINE, j=PACK),
+            in_=w2_raw[:].rearrange("p j (c i) -> p c j i", i=LINE),
+        )
+
         for t, h in ((0, 0), (0, 1), (3, 0), (3, 1), (1, 1), (2, 1), (2, 0), (1, 0)):
             nc.vector.tensor_tensor(
                 z[h][:, t, :HALF], rr[t][:].indirect(back_sb[:, list_halves[h]]), y[t][:, halves[h]], ADD
             )
 
+        w2_codes = sb("w2_codes", [P, N], U32, tag="rr2")
+        nc.vector.quantize_mx(out=w2_codes[:].bitcast(FP8X4), scales=w2_scale[:], in_=w2_bf[:])
+
         out_sb = sb("out_sb", [P, S], F32)
-        upper = [(HALF, HALF, nc.scalar.copy, nc.scalar.copy)]
+        upper = [(HALF, HALF, nc.scalar.copy, nc.vector.tensor_copy)]
         lower = [
             (0, QUARTER, nc.vector.tensor_copy, nc.scalar.copy),
             (QUARTER, QUARTER, nc.scalar.copy, nc.vector.tensor_copy),

@@ -34,8 +34,8 @@ Y_WINDOW = 704
 RR_WINDOW = 528
 Z_STEP = 704
 PAD = 8
-SPLIT_ON_TENSOR = HALF
 TINY = 2.0**-32
+SPLIT = HALF
 
 
 def tile_picked_yserial_silu_p_kernel(
@@ -49,6 +49,7 @@ def tile_picked_yserial_silu_p_kernel(
         def sb(name, shape, dtype, tag=""):
             return keep.tile(shape, dtype, name=name, tag=tag or name, align_bytes=64)
 
+        whole = slice(0, S)
         halves = [slice(h * HALF, (h + 1) * HALF) for h in range(2)]
         list_halves = [slice(h * LIST_COLS // 2, (h + 1) * LIST_COLS // 2) for h in range(2)]
 
@@ -164,7 +165,7 @@ def tile_picked_yserial_silu_p_kernel(
             for n, cols in enumerate(first_pieces):
                 product1(o, 0, y_first[n][:], x_codes, cols)
             for t in range(1, PACK):
-                product1(o, t, y_rest[t - 1][:], x_codes, slice(0, S))
+                product1(o, t, y_rest[t - 1][:], x_codes, whole)
 
         weave_w1(0)
         quantize_w1(0, 0, 2)
@@ -185,115 +186,98 @@ def tile_picked_yserial_silu_p_kernel(
         gg = [sb("gg%d" % t, [P, PAD + S], F32) for t in range(PACK)]
         for t in range(PACK):
             nc.gpsimd.memset(gg[t][:, :PAD], 0.0)
-        on_gpsimd = {}
-        on_tensor = {0: slice(0, S), 1: slice(0, S), 2: slice(HALF, S)}
-        on_vector = {2: slice(0, HALF), 3: slice(0, S)}
+
+        on_tensor = {0: whole, 1: whole, 2: slice(SPLIT, S)}
+        on_vector = {2: slice(0, SPLIT), 3: whole}
         scaled_on_gpsimd = ((0, 1), (1, 2))
-        shared = sb("shared", [P, PACK, TAPS - 1, S], F32, tag="w1_codes1_1")
-        scaled = {(t, k): shared[:, t, k - 1, :] for t in range(PACK) for k in range(1, TAPS)}
-        summed_sb = {0: sb("summed_sb0", [P, S], F32)[:], 1: rr[2][:, :S], 2: sb("summed_sb2", [P, S], F32)[:]}
-        partial = sb("partial", [P, S], F32)
-        filt = {t: sb("filt%d" % t, [P, S], F32) for t in range(PACK) if t in on_vector or t in on_gpsimd}
-        flat = shared[:].rearrange("p t k c -> p (t k c)")
-        scaled[0, 2] = rr[3][:, :S]
-        scaled[1, 1] = flat[:, 2 * S + HALF : 3 * S + HALF]
-        scaled[1, 2] = rr[3][:, :S]
-        scaled[0, 1] = flat[:, S : 2 * S]
-        scaled[2, 1] = flat[:, S - 64 : 2 * S - 64]
-        scaled[2, 2] = flat[:, S + 192 : 2 * S + 192]
-        filt[2] = flat[:, 2 * S + HALF : 3 * S + HALF]
-        filt[3] = flat[:, 3 * S : 4 * S]
+
+        work = sb("work", [P, TAPS * S], F32, tag="w1_codes1_1")
+        meet = S - P // 2
+        rest = S - SPLIT
+        scaled = {
+            (0, 1): work[:, :S],
+            (0, 2): rr[3][:, :S],
+            (1, 1): work[:, S + HALF : 2 * S + HALF],
+            (1, 2): rr[3][:, :S],
+            (2, 1): work[:, meet - rest : meet],
+            (2, 2): work[:, meet : meet + rest],
+        }
+        filt = {2: work[:, S + HALF : S + HALF + SPLIT], 3: work[:, S + HALF + SPLIT : 2 * S + HALF + SPLIT]}
+        summed_sb = {0: sb("summed_sb0", [P, S], F32)[:], 1: rr[2][:, :S], 2: sb("summed_sb2", [P, rest], F32)[:]}
         ident = sb("ident", [P, P], F32)
         make_identity(nc, ident[:])
-        sum_tags = {0: "summed0", 1: "y_first2", 2: "y_first1", 3: "y_rest2"}
-        back_tags = {0: "restored0", 1: "y_first0", 2: "y_rest1", 3: "y_rest3"}
-        summed = {t: psum.tile([P, S], F32, name="summed%d" % t, tag=sum_tags[t]) for t in on_tensor}
-        restored = {t: psum.tile([P, S], F32, name="restored%d" % t, tag=back_tags[t]) for t in on_tensor}
+        sum_banks = {0: "summed0", 1: "y_first2", 2: "y_first1"}
+        back_banks = {0: "restored0", 1: "y_first0", 2: "y_rest1"}
+        summed = {t: psum.tile([P, S], F32, name="summed%d" % t, tag=sum_banks[t]) for t in on_tensor}
+        restored = {t: psum.tile([P, S], F32, name="restored%d" % t, tag=back_banks[t]) for t in on_tensor}
 
-        def delayed(t, k):
-            return gg[t][:, PAD - k : PAD - k + S]
+        def delayed(t, k, cols):
+            return gg[t][:, PAD - k + cols.start : PAD - k + cols.stop]
 
         def chunks(t):
-            return [slice(start, start + P) for start in range(on_tensor[t].start, on_tensor[t].stop, P)]
+            return [slice(start, start + P) for start in range(0, on_tensor[t].stop - on_tensor[t].start, P)]
 
-        def scale_term(t, k, cols):
-            factor = ratio[:, t, k - 1 : k]
-            if (t, k) in scaled_on_gpsimd:
-                nc.gpsimd.tensor_scalar(scaled[t, k][:, cols], delayed(t, k)[:, cols], factor, 0.0, op0=MULT, op1=ADD)
-            else:
-                nc.scalar.activation(scaled[t, k][:, cols], delayed(t, k)[:, cols], COPY, scale=factor)
+        def gather_by_order(t):
+            if t > 0:
+                nc.scalar.copy(out=y[t][:, :S], in_=y_rest[t - 1][:])
+            nc.vector.tensor_copy(delayed(t, 0, whole), y[t].indirect(order_sb[:]))
 
-        def sum_by_transposes(t, order_of_terms):
-            for k in order_of_terms:
-                term = delayed(t, 0)
+        def sum_by_transposes(t, taps_in_turn):
+            for k in taps_in_turn:
+                term = delayed(t, k, on_tensor[t])
                 if k > 0:
+                    factor = ratio[:, t, k - 1 : k]
+                    if (t, k) in scaled_on_gpsimd:
+                        nc.gpsimd.tensor_scalar(scaled[t, k], term, factor, 0.0, op0=MULT, op1=ADD)
+                    else:
+                        nc.scalar.activation(scaled[t, k], term, COPY, scale=factor)
                     term = scaled[t, k]
-                    scale_term(t, k, on_tensor[t])
                 for chunk in chunks(t):
                     nc.tensor.matmul(
                         summed[t][:, chunk],
                         lhsT=term[:, chunk],
                         rhs=ident[:],
                         is_transpose=True,
-                        start=(k == order_of_terms[0] and chunk.start == on_tensor[t].start),
-                        stop=(k == order_of_terms[-1] and chunk.stop == on_tensor[t].stop),
+                        start=(k == taps_in_turn[0] and chunk == chunks(t)[0]),
+                        stop=(k == taps_in_turn[-1] and chunk == chunks(t)[-1]),
                     )
 
         def turn_back(t):
-            nc.scalar.copy(out=summed_sb[t][:, on_tensor[t]], in_=summed[t][:, on_tensor[t]])
+            nc.scalar.copy(out=summed_sb[t], in_=summed[t][:, : chunks(t)[-1].stop])
             for chunk in reversed(chunks(t)):
                 nc.tensor.transpose(restored[t][:, chunk], summed_sb[t][:, chunk], ident[:])
 
-        def sum_on_gpsimd(t):
-            cols = on_gpsimd[t]
-            for k in range(1, TAPS):
-                nc.gpsimd.tensor_scalar(
-                    scaled[t, k][:, cols], delayed(t, k)[:, cols], ratio[:, t, k - 1 : k], 0.0, op0=MULT, op1=ADD
-                )
-            nc.gpsimd.tensor_tensor(partial[:, cols], delayed(t, 0)[:, cols], scaled[t, 1][:, cols], ADD)
-            nc.gpsimd.tensor_tensor(filt[t][:, cols], partial[:, cols], scaled[t, 2][:, cols], ADD)
-
-        def add_tap(t, k):
-            cols = on_vector[t]
-            nc.vector.scalar_tensor_tensor(
-                out=filt[t][:, cols],
-                in0=delayed(t, k)[:, cols],
-                scalar=ratio[:, t, k - 1 : k],
-                in1=(delayed(t, 0) if k == 1 else filt[t])[:, cols],
-                op0=MULT,
-                op1=ADD,
-            )
-
         def silu(t, cols, source):
-            nc.scalar.activation(rr[t][:, cols], source[:, cols], SILU, scale=lead[:, t : t + 1])
+            nc.scalar.activation(rr[t][:, cols], source, SILU, scale=lead[:, t : t + 1])
 
-        def gather_by_order(t):
-            if t > 0:
-                nc.scalar.copy(out=y[t][:, :S], in_=y_rest[t - 1][:])
-            nc.vector.tensor_copy(delayed(t, 0), y[t].indirect(order_sb[:]))
+        def silu_of_transposed(t):
+            silu(t, on_tensor[t], restored[t][:, : chunks(t)[-1].stop])
 
-        gather_by_order(0)
-        gather_by_order(1)
-        gather_by_order(2)
-        gather_by_order(3)
+        for t in range(PACK):
+            gather_by_order(t)
         sum_by_transposes(0, (0, 2, 1))
         turn_back(0)
         sum_by_transposes(1, (1, 0, 2))
         sum_by_transposes(2, (1, 0, 2))
-        silu(0, on_tensor[0], restored[0])
-        add_tap(2, 1)
-        add_tap(3, 1)
-        add_tap(2, 2)
-        add_tap(3, 2)
+        silu_of_transposed(0)
+        for k in range(1, TAPS):
+            for t, cols in on_vector.items():
+                nc.vector.scalar_tensor_tensor(
+                    out=filt[t],
+                    in0=delayed(t, k, cols),
+                    scalar=ratio[:, t, k - 1 : k],
+                    in1=delayed(t, 0, cols) if k == 1 else filt[t],
+                    op0=MULT,
+                    op1=ADD,
+                )
         turn_back(1)
         silu(3, on_vector[3], filt[3])
         turn_back(2)
-        silu(1, on_tensor[1], restored[1])
+        silu_of_transposed(1)
         silu(2, on_vector[2], filt[2])
-        silu(2, on_tensor[2], restored[2])
+        silu_of_transposed(2)
 
         w2_bf = sb("w2_bf", [P, N * PACK], BF16, tag="summed_sb2")
-        w2_scale = sb("w2_scale", [P, N], U8)
         nc.scalar.copy(
             out=w2_bf[:].rearrange("p (c i j) -> p c j i", i=LINE, j=PACK),
             in_=w2_raw[:].rearrange("p j (c i) -> p c j i", i=LINE),
@@ -305,6 +289,7 @@ def tile_picked_yserial_silu_p_kernel(
             )
 
         w2_codes = sb("w2_codes", [P, N], U32, tag="rr2")
+        w2_scale = sb("w2_scale", [P, N], U8)
         nc.vector.quantize_mx(out=w2_codes[:].bitcast(FP8X4), scales=w2_scale[:], in_=w2_bf[:])
 
         out_sb = sb("out_sb", [P, S], F32)
@@ -318,9 +303,10 @@ def tile_picked_yserial_silu_p_kernel(
         out_tags = ("y_rest2", "y_rest3", "summed0")
         out_ps = [psum.tile([P, piece[1]], F32, name="out_ps%d" % n, tag=out_tags[n]) for n, piece in enumerate(pieces)]
         for n, (start, width, weave, leave) in enumerate(pieces):
+            points = z[start // HALF][:, :, start % HALF : start % HALF + width]
             weave(
                 out=z_bf[n][:].rearrange("p (c i t) -> p c t i", i=LINE, t=PACK),
-                in_=z[start // HALF][:, :, start % HALF : start % HALF + width].rearrange("p t (c i) -> p c t i", i=LINE),
+                in_=points.rearrange("p t (c i) -> p c t i", i=LINE),
             )
         for n, (start, width, weave, leave) in enumerate(pieces):
             cols = slice(start, start + width)

@@ -183,7 +183,7 @@ def tile_picked_yserial_silu_p_kernel(
         for n, copy in enumerate((nc.scalar.copy, nc.vector.tensor_copy, nc.vector.tensor_copy)):
             copy(out=y[0][:, first_pieces[n]], in_=y_first[n][:])
 
-        gg = [sb("gg%d" % t, [P, PAD + S], F32) for t in range(PACK)]
+        gg = [sb("gg%d" % t, [P, PAD + 2 * S if t == 1 else PAD + S], F32) for t in range(PACK)]
         for t in range(PACK):
             nc.gpsimd.memset(gg[t][:, :PAD], 0.0)
 
@@ -202,11 +202,11 @@ def tile_picked_yserial_silu_p_kernel(
             (2, 1): work[:, meet - rest : meet],
             (2, 2): work[:, meet : meet + rest],
         }
-        filt = {2: work[:, S + HALF : S + HALF + SPLIT], 3: work[:, S + HALF + SPLIT : 2 * S + HALF + SPLIT]}
+        filt = {2: gg[1][:, PAD + meet - SPLIT : PAD + meet], 3: gg[1][:, PAD + meet : PAD + meet + S]}
         summed_sb = {0: sb("summed_sb0", [P, S], F32)[:], 1: rr[2][:, :S], 2: sb("summed_sb2", [P, rest], F32)[:]}
         ident = sb("ident", [P, P], F32)
         make_identity(nc, ident[:])
-        sum_banks = {0: "summed0", 1: "y_first2", 2: "y_first1"}
+        sum_banks = {0: "summed0", 1: "y_rest3", 2: "y_first1"}
         back_banks = {0: "restored0", 1: "y_first0", 2: "y_rest1"}
         summed = {t: psum.tile([P, S], F32, name="summed%d" % t, tag=sum_banks[t]) for t in on_tensor}
         restored = {t: psum.tile([P, S], F32, name="restored%d" % t, tag=back_banks[t]) for t in on_tensor}
@@ -253,11 +253,12 @@ def tile_picked_yserial_silu_p_kernel(
         def silu_of_transposed(t):
             silu(t, on_tensor[t], restored[t][:, : chunks(t)[-1].stop])
 
-        for t in range(PACK):
+        for t in range(PACK - 1):
             gather_by_order(t)
         sum_by_transposes(0, (0, 2, 1))
+        gather_by_order(PACK - 1)
         turn_back(0)
-        sum_by_transposes(1, (1, 0, 2))
+        sum_by_transposes(1, (0, 1, 2))
         sum_by_transposes(2, (1, 0, 2))
         silu_of_transposed(0)
         for k in range(1, TAPS):
@@ -300,7 +301,7 @@ def tile_picked_yserial_silu_p_kernel(
         ]
         pieces = upper + lower
         z_bf = [sb("z_bf%d" % n, [P, piece[1] * PACK], BF16) for n, piece in enumerate(pieces)]
-        out_tags = ("y_rest2", "y_rest3", "summed0")
+        out_tags = ("y_rest2", "y_first2", "summed0")
         out_ps = [psum.tile([P, piece[1]], F32, name="out_ps%d" % n, tag=out_tags[n]) for n, piece in enumerate(pieces)]
         for n, (start, width, weave, leave) in enumerate(pieces):
             points = z[start // HALF][:, :, start % HALF : start % HALF + width]

@@ -32,7 +32,6 @@ QUADRANTS = 4
 SCALE_ROWS = 4
 Y_WINDOW = 704
 RR_WINDOW = 528
-Z_STEP = 704
 PAD = 8
 TINY = 2.0**-32
 SPLIT = HALF
@@ -51,7 +50,9 @@ def tile_picked_yserial_silu_p_kernel(
 
         whole = slice(0, S)
         halves = [slice(h * HALF, (h + 1) * HALF) for h in range(2)]
-        list_halves = [slice(h * LIST_COLS // 2, (h + 1) * LIST_COLS // 2) for h in range(2)]
+
+        def entries(lst, cols):
+            return lst[:, cols.start // PER_COLUMN : cols.stop // PER_COLUMN]
 
         offs_sb = sb("offs_sb", [P, LIST_COLS], U16)
         order_sb = sb("order_sb", [P, LIST_COLS], U16)
@@ -62,14 +63,8 @@ def tile_picked_yserial_silu_p_kernel(
         w1_raw = [sb("w1_raw%d" % n, [P, part[2], H], F32) for n, part in enumerate(w1_parts)]
         w2_raw = sb("w2_raw", [P, PACK, N], F32)
         taps_sb = sb("taps_sb", [P, PACK * TAPS], F32)
-        z_lower = sb("z_lower", [P, PACK * Z_STEP], F32)
-        z_upper = sb("z_upper", [P, PACK, HALF], F32)
-        z = [z_lower[:].rearrange("p (t c) -> p t c", t=PACK), z_upper[:]]
-        y_start = Z_STEP - HALF
-        y = [
-            z_lower[:, y_start : y_start + Y_WINDOW] if t == 2 else sb("y%d" % t, [P, Y_WINDOW], F32)[:]
-            for t in range(PACK)
-        ]
+        y = [sb("y%d" % t, [P, Y_WINDOW], F32)[:] for t in range(PACK)]
+        z = sb("z", [P, PACK, S], F32)
         rr = [sb("rr%d" % t, [P, RR_WINDOW], F32) for t in range(PACK)]
         zeros = sb("zeros", [P, RR_WINDOW - S], F32)
 
@@ -89,9 +84,9 @@ def tile_picked_yserial_silu_p_kernel(
                 out=scale_table[32 * q : 32 * q + SCALE_ROWS * PASSES, :].bitcast(I32),
                 in_=x_scales[:, SCALE_ROWS * q : SCALE_ROWS * (q + 1), :].bitcast(I32),
             )
-        nc.sync.dma_start(out=taps_sb[:], in_=taps.rearrange("(p t) k -> p (t k)", t=PACK))
         load_w1(0)
         load_words(1)
+        nc.sync.dma_start(out=taps_sb[:], in_=taps.rearrange("(p t) k -> p (t k)", t=PACK))
         load_w1(1)
         load_w1(2)
         nc.sync.dma_start(out=w2_raw[:], in_=w2.rearrange("(p j) m -> p j m", j=PACK))
@@ -111,13 +106,13 @@ def tile_picked_yserial_silu_p_kernel(
         taps3 = taps_sb[:].rearrange("p (t k) -> p t k", k=TAPS)
         square = sb("square", [P, PACK], F32)
         shift = sb("shift", [P, PACK], F32)
-        lead = sb("lead", [P, PACK], F32)
+        lead = z[:, 1, :PACK]
         inverse = sb("inverse", [P, PACK], F32)
         ratio = sb("ratio", [P, PACK, TAPS - 1], F32)
         nc.gpsimd.tensor_tensor(square[:], taps3[:, :, 0], taps3[:, :, 0], MULT)
         nc.gpsimd.tensor_scalar(shift[:], square[:], TINY * TINY, 2.0 * TINY, op0=IS_LT, op1=MULT)
-        nc.gpsimd.tensor_tensor(lead[:], taps3[:, :, 0], shift[:], ADD)
-        nc.vector.reciprocal(inverse[:], lead[:])
+        nc.gpsimd.tensor_tensor(lead, taps3[:, :, 0], shift[:], ADD)
+        nc.vector.reciprocal(inverse[:], lead)
         nc.gpsimd.tensor_tensor(
             ratio[:], taps3[:, :, 1:], inverse[:].unsqueeze(2).to_broadcast([P, PACK, TAPS - 1]), MULT
         )
@@ -126,13 +121,18 @@ def tile_picked_yserial_silu_p_kernel(
         w1_codes = [[sb("w1_codes%d_%d" % (o, u), [P, 2 * P], U32) for u in range(2)] for o in range(PASSES)]
         w1_scale = [[sb("w1_scale%d_%d" % (o, u), [P, 2 * P], U8) for u in range(2)] for o in range(PASSES)]
 
-        def weave_w1(n):
+        def weave_tiles(n, copy, first_tile, tiles):
             o, first, count = w1_parts[n]
-            for u, copy in enumerate((nc.vector.tensor_copy, nc.scalar.copy)):
-                copy(
-                    out=w1_bf[o][u][:].rearrange("p (e m j) -> p m j e", e=2, j=PACK)[:, :, first : first + count, :],
-                    in_=w1_raw[n][:].rearrange("p j (m t) -> p m j t", t=PACK)[:, :, :, 2 * u : 2 * u + 2],
-                )
+            u, e = divmod(first_tile, 2)
+            woven = w1_bf[o][u][:].rearrange("p (e m j) -> p m j e", e=2, j=PACK)
+            copy(
+                out=woven[:, :, first : first + count, e : e + tiles],
+                in_=w1_raw[n][:].rearrange("p j (m t) -> p m j t", t=PACK)[:, :, :, first_tile : first_tile + tiles],
+            )
+
+        def weave_w1(n):
+            weave_tiles(n, nc.vector.tensor_copy, 0, 2)
+            weave_tiles(n, nc.scalar.copy, 2, 2)
 
         def quantize_w1(o, first_tile, tiles):
             u, e = divmod(first_tile, 2)
@@ -143,7 +143,7 @@ def tile_picked_yserial_silu_p_kernel(
                 in_=w1_bf[o][u][:, e * P * PACK : (e + tiles) * P * PACK],
             )
 
-        first_pieces = (slice(0, HALF), slice(HALF, HALF + QUARTER), slice(HALF + QUARTER, S))
+        first_pieces = [slice(start, start + QUARTER) for start in range(0, S, QUARTER)]
         y_first = [
             psum.tile([P, cols.stop - cols.start], F32, name="y_first%d" % n) for n, cols in enumerate(first_pieces)
         ]
@@ -172,15 +172,17 @@ def tile_picked_yserial_silu_p_kernel(
         quantize_w1(0, 2, 2)
         products(0, x_codes0)
 
-        x_codes1 = sb("x_codes1", [P, S], U32)
+        x_codes1 = sb("x_codes1", [P, S], U32, tag="w1_raw0")
         nc.vector.tensor_copy(x_codes1[:], x_table[1][:].bitcast(U32).indirect(offs_sb[:]))
         weave_w1(1)
-        weave_w1(2)
+        weave_tiles(2, nc.vector.tensor_copy, 0, 1)
+        weave_tiles(2, nc.vector.tensor_copy, 1, 1)
+        weave_tiles(2, nc.scalar.copy, 2, 2)
         quantize_w1(1, 0, 1)
         quantize_w1(1, 1, 1)
         quantize_w1(1, 2, 2)
         products(1, x_codes1)
-        for n, copy in enumerate((nc.scalar.copy, nc.vector.tensor_copy, nc.vector.tensor_copy)):
+        for n, copy in enumerate((nc.vector.tensor_copy, nc.scalar.copy) * 2):
             copy(out=y[0][:, first_pieces[n]], in_=y_first[n][:])
 
         gg = [sb("gg%d" % t, [P, PAD + 2 * S if t == 1 else PAD + S], F32) for t in range(PACK)]
@@ -207,7 +209,7 @@ def tile_picked_yserial_silu_p_kernel(
         ident = sb("ident", [P, P], F32)
         make_identity(nc, ident[:])
         sum_banks = {0: "summed0", 1: "y_rest3", 2: "y_first1"}
-        back_banks = {0: "restored0", 1: "y_first0", 2: "y_rest1"}
+        back_banks = {0: "y_first3", 1: "y_first0", 2: "y_rest1"}
         summed = {t: psum.tile([P, S], F32, name="summed%d" % t, tag=sum_banks[t]) for t in on_tensor}
         restored = {t: psum.tile([P, S], F32, name="restored%d" % t, tag=back_banks[t]) for t in on_tensor}
 
@@ -284,10 +286,8 @@ def tile_picked_yserial_silu_p_kernel(
             in_=w2_raw[:].rearrange("p j (c i) -> p c j i", i=LINE),
         )
 
-        for t, h in ((0, 0), (0, 1), (3, 0), (3, 1), (1, 1), (2, 1), (2, 0), (1, 0)):
-            nc.vector.tensor_tensor(
-                z[h][:, t, :HALF], rr[t][:].indirect(back_sb[:, list_halves[h]]), y[t][:, halves[h]], ADD
-            )
+        for t, cols in ((0, whole), (3, whole), (1, halves[1]), (2, halves[1]), (2, halves[0]), (1, halves[0])):
+            nc.vector.tensor_tensor(z[:, t, cols], rr[t][:].indirect(entries(back_sb, cols)), y[t][:, cols], ADD)
 
         w2_codes = sb("w2_codes", [P, N], U32, tag="rr2")
         w2_scale = sb("w2_scale", [P, N], U8)
@@ -304,14 +304,14 @@ def tile_picked_yserial_silu_p_kernel(
         out_tags = ("y_rest2", "y_first2", "summed0")
         out_ps = [psum.tile([P, piece[1]], F32, name="out_ps%d" % n, tag=out_tags[n]) for n, piece in enumerate(pieces)]
         for n, (start, width, weave, leave) in enumerate(pieces):
-            points = z[start // HALF][:, :, start % HALF : start % HALF + width]
+            points = z[:, :, start : start + width]
             weave(
                 out=z_bf[n][:].rearrange("p (c i t) -> p c t i", i=LINE, t=PACK),
                 in_=points.rearrange("p t (c i) -> p c t i", i=LINE),
             )
         for n, (start, width, weave, leave) in enumerate(pieces):
             cols = slice(start, start + width)
-            z_codes = sb("z_codes%d" % n, [P, width], U32, tag="z_upper" if n == 1 else "")
+            z_codes = sb("z_codes%d" % n, [P, width], U32, tag="z" if n == 1 else "")
             z_scale = sb("z_scale%d" % n, [P, width], U8)
             nc.vector.quantize_mx(out=z_codes[:].bitcast(FP8X4), scales=z_scale[:], in_=z_bf[n][:])
             nc.tensor.matmul_mx(

@@ -31,10 +31,9 @@ QUARTER = S // 4
 QUADRANTS = 4
 SCALE_ROWS = 4
 Y_WINDOW = 704
-RR_WINDOW = 528
+WINDOW = 528
 PAD = 8
 TINY = 2.0**-32
-SPLIT = HALF
 
 
 def tile_picked_yserial_silu_p_kernel(
@@ -63,10 +62,10 @@ def tile_picked_yserial_silu_p_kernel(
         w1_raw = [sb("w1_raw%d" % n, [P, part[2], H], F32) for n, part in enumerate(w1_parts)]
         w2_raw = sb("w2_raw", [P, PACK, N], F32)
         taps_sb = sb("taps_sb", [P, PACK * TAPS], F32)
-        y = [sb("y%d" % t, [P, Y_WINDOW], F32)[:] for t in range(PACK)]
+        y = [sb("y%d" % t, [P, Y_WINDOW if t < 2 else WINDOW], F32)[:] for t in range(PACK)]
         z = sb("z", [P, PACK, S], F32)
-        rr = [sb("rr%d" % t, [P, RR_WINDOW], F32) for t in range(PACK)]
-        zeros = sb("zeros", [P, RR_WINDOW - S], F32)
+        rr = [sb("rr%d" % t, [P, WINDOW], F32) for t in range(PACK)]
+        zeros = sb("zeros", [P, WINDOW - S], F32)
 
         def load_words(o):
             nc.sync.dma_start(out=x_table[o][:], in_=x_words[o].rearrange("p n r -> p (n r)").bitcast(I32))
@@ -106,7 +105,7 @@ def tile_picked_yserial_silu_p_kernel(
         taps3 = taps_sb[:].rearrange("p (t k) -> p t k", k=TAPS)
         square = sb("square", [P, PACK], F32)
         shift = sb("shift", [P, PACK], F32)
-        lead = z[:, 1, :PACK]
+        lead = z[:, 0, :PACK]
         inverse = sb("inverse", [P, PACK], F32)
         ratio = sb("ratio", [P, PACK, TAPS - 1], F32)
         nc.gpsimd.tensor_tensor(square[:], taps3[:, :, 0], taps3[:, :, 0], MULT)
@@ -185,111 +184,100 @@ def tile_picked_yserial_silu_p_kernel(
         for n, copy in enumerate((nc.vector.tensor_copy, nc.scalar.copy) * 2):
             copy(out=y[0][:, first_pieces[n]], in_=y_first[n][:])
 
-        gg = [sb("gg%d" % t, [P, PAD + 2 * S if t == 1 else PAD + S], F32) for t in range(PACK)]
-        for t in range(PACK):
-            nc.gpsimd.memset(gg[t][:, :PAD], 0.0)
-
-        on_tensor = {0: whole, 1: whole, 2: slice(SPLIT, S)}
-        on_vector = {2: slice(0, SPLIT), 3: whole}
-        scaled_on_gpsimd = ((0, 1), (1, 2))
-
-        work = sb("work", [P, TAPS * S], F32, tag="w1_codes1_1")
-        meet = S - P // 2
-        rest = S - SPLIT
-        scaled = {
-            (0, 1): work[:, :S],
-            (0, 2): rr[3][:, :S],
-            (1, 1): work[:, S + HALF : 2 * S + HALF],
-            (1, 2): rr[3][:, :S],
-            (2, 1): work[:, meet - rest : meet],
-            (2, 2): work[:, meet : meet + rest],
-        }
-        filt = {2: gg[1][:, PAD + meet - SPLIT : PAD + meet], 3: gg[1][:, PAD + meet : PAD + meet + S]}
-        summed_sb = {0: sb("summed_sb0", [P, S], F32)[:], 1: rr[2][:, :S], 2: sb("summed_sb2", [P, rest], F32)[:]}
+        gg = [sb("gg%d" % t, [P, PAD + S], F32) for t in range(PACK)]
+        filt = {2: sb("filt2", [P, S], F32)[:], 3: gg[2][:, :S]}
+        scaled = {(t, k): sb("scaled%d_%d" % (t, k), [P, S], F32) for t in (0, 1) for k in (1, 2)}
+        summed_sb = {0: sb("summed_sb0", [P, S], F32)[:], 1: filt[2]}
         ident = sb("ident", [P, P], F32)
         make_identity(nc, ident[:])
-        sum_banks = {0: "summed0", 1: "y_rest3", 2: "y_first1"}
-        back_banks = {0: "y_first3", 1: "y_first0", 2: "y_rest1"}
-        summed = {t: psum.tile([P, S], F32, name="summed%d" % t, tag=sum_banks[t]) for t in on_tensor}
-        restored = {t: psum.tile([P, S], F32, name="restored%d" % t, tag=back_banks[t]) for t in on_tensor}
+        sum_banks = {0: "summed0", 1: "y_rest3"}
+        back_banks = {0: "y_first3", 1: "y_first0"}
+        summed = {t: psum.tile([P, S], F32, name="summed%d" % t, tag=sum_banks[t]) for t in (0, 1)}
+        restored = {t: psum.tile([P, S], F32, name="restored%d" % t, tag=back_banks[t]) for t in (0, 1)}
+        chunks = [slice(start, start + P) for start in range(0, S, P)]
+        for t in range(PACK):
+            nc.gpsimd.memset(gg[t][:, :PAD], 0.0)
 
         def delayed(t, k, cols):
             return gg[t][:, PAD - k + cols.start : PAD - k + cols.stop]
 
-        def chunks(t):
-            return [slice(start, start + P) for start in range(0, on_tensor[t].stop - on_tensor[t].start, P)]
+        def leave_bank(t):
+            nc.scalar.copy(out=y[t][:, :S], in_=y_rest[t - 1][:])
 
         def gather_by_order(t):
-            if t > 0:
-                nc.scalar.copy(out=y[t][:, :S], in_=y_rest[t - 1][:])
-            nc.vector.tensor_copy(delayed(t, 0, whole), y[t].indirect(order_sb[:]))
+            if t < 2:
+                nc.vector.tensor_copy(delayed(t, 0, whole), y[t].indirect(order_sb[:]))
+            else:
+                nc.scalar.activation(delayed(t, 0, whole), y[t].indirect(order_sb[:]), COPY)
 
-        def sum_by_transposes(t, taps_in_turn):
-            for k in taps_in_turn:
-                term = delayed(t, k, on_tensor[t])
+        def sum_taps(t):
+            for k in range(1, TAPS):
+                for cols in halves:
+                    nc.vector.scalar_tensor_tensor(
+                        out=filt[t][:, cols],
+                        in0=delayed(t, k, cols),
+                        scalar=ratio[:, t, k - 1 : k],
+                        in1=delayed(t, 0, cols) if k == 1 else filt[t][:, cols],
+                        op0=MULT,
+                        op1=ADD,
+                    )
+
+        def sum_by_transposes(t):
+            for k in range(TAPS):
+                term = delayed(t, k, whole)
                 if k > 0:
-                    factor = ratio[:, t, k - 1 : k]
-                    if (t, k) in scaled_on_gpsimd:
-                        nc.gpsimd.tensor_scalar(scaled[t, k], term, factor, 0.0, op0=MULT, op1=ADD)
-                    else:
-                        nc.scalar.activation(scaled[t, k], term, COPY, scale=factor)
-                    term = scaled[t, k]
-                for chunk in chunks(t):
+                    engine = nc.gpsimd if t == 0 else nc.vector
+                    engine.tensor_scalar(scaled[t, k][:], term, ratio[:, t, k - 1 : k], 0.0, op0=MULT, op1=ADD)
+                    term = scaled[t, k][:]
+                for chunk in chunks:
                     nc.tensor.matmul(
                         summed[t][:, chunk],
                         lhsT=term[:, chunk],
                         rhs=ident[:],
                         is_transpose=True,
-                        start=(k == taps_in_turn[0] and chunk == chunks(t)[0]),
-                        stop=(k == taps_in_turn[-1] and chunk == chunks(t)[-1]),
+                        start=(k == 0 and chunk == chunks[0]),
+                        stop=(k == TAPS - 1 and chunk == chunks[-1]),
                     )
 
         def turn_back(t):
-            nc.scalar.copy(out=summed_sb[t], in_=summed[t][:, : chunks(t)[-1].stop])
-            for chunk in reversed(chunks(t)):
+            nc.scalar.copy(out=summed_sb[t], in_=summed[t][:])
+            for chunk in chunks:
                 nc.tensor.transpose(restored[t][:, chunk], summed_sb[t][:, chunk], ident[:])
 
-        def silu(t, cols, source):
-            nc.scalar.activation(rr[t][:, cols], source, SILU, scale=lead[:, t : t + 1])
+        def silu(t):
+            source = restored[t][:] if t < 2 else filt[t]
+            nc.scalar.activation(rr[t][:, :S], source, SILU, scale=lead[:, t : t + 1])
 
-        def silu_of_transposed(t):
-            silu(t, on_tensor[t], restored[t][:, : chunks(t)[-1].stop])
+        def gather_by_back(t, cols):
+            nc.vector.tensor_tensor(z[:, t, cols], rr[t][:].indirect(entries(back_sb, cols)), y[t][:, cols], ADD)
 
-        for t in range(PACK - 1):
+        for t in range(1, PACK):
+            leave_bank(t)
+        for t in range(PACK):
             gather_by_order(t)
-        sum_by_transposes(0, (0, 2, 1))
-        gather_by_order(PACK - 1)
+        for t in (0, 1):
+            sum_by_transposes(t)
+        for t in (2, 3):
+            sum_taps(t)
         turn_back(0)
-        sum_by_transposes(1, (0, 1, 2))
-        sum_by_transposes(2, (1, 0, 2))
-        silu_of_transposed(0)
-        for k in range(1, TAPS):
-            for t, cols in on_vector.items():
-                nc.vector.scalar_tensor_tensor(
-                    out=filt[t],
-                    in0=delayed(t, k, cols),
-                    scalar=ratio[:, t, k - 1 : k],
-                    in1=delayed(t, 0, cols) if k == 1 else filt[t],
-                    op0=MULT,
-                    op1=ADD,
-                )
+        silu(2)
         turn_back(1)
-        silu(3, on_vector[3], filt[3])
-        turn_back(2)
-        silu_of_transposed(1)
-        silu(2, on_vector[2], filt[2])
-        silu_of_transposed(2)
+        silu(3)
+        silu(0)
+        silu(1)
 
-        w2_bf = sb("w2_bf", [P, N * PACK], BF16, tag="summed_sb2")
+        w2_bf = sb("w2_bf", [P, N * PACK], BF16, tag="filt2")
         nc.scalar.copy(
             out=w2_bf[:].rearrange("p (c i j) -> p c j i", i=LINE, j=PACK),
             in_=w2_raw[:].rearrange("p j (c i) -> p c j i", i=LINE),
         )
+        for t in (2, 3):
+            gather_by_back(t, whole)
+        for cols in reversed(halves):
+            for t in (0, 1):
+                gather_by_back(t, cols)
 
-        for t, cols in ((0, whole), (3, whole), (1, halves[1]), (2, halves[1]), (2, halves[0]), (1, halves[0])):
-            nc.vector.tensor_tensor(z[:, t, cols], rr[t][:].indirect(entries(back_sb, cols)), y[t][:, cols], ADD)
-
-        w2_codes = sb("w2_codes", [P, N], U32, tag="rr2")
+        w2_codes = sb("w2_codes", [P, N], U32, tag="rr0")
         w2_scale = sb("w2_scale", [P, N], U8)
         nc.vector.quantize_mx(out=w2_codes[:].bitcast(FP8X4), scales=w2_scale[:], in_=w2_bf[:])
 

@@ -186,7 +186,11 @@ def tile_picked_yserial_silu_p_kernel(
 
         gg = [sb("gg%d" % t, [P, PAD + S], F32) for t in range(PACK)]
         filt = {2: sb("filt2", [P, S], F32)[:], 3: gg[2][:, :S]}
-        scaled = {(t, k): sb("scaled%d_%d" % (t, k), [P, S], F32) for t in (0, 1) for k in (1, 2)}
+        scaled = {
+            (t, k): sb("scaled%d_%d" % (t, k), [P, S], F32, tag="w1_codes1_1" if (t, k) == (0, 2) else "")
+            for t in (0, 1)
+            for k in (1, 2)
+        }
         summed_sb = {0: sb("summed_sb0", [P, S], F32)[:], 1: filt[2]}
         ident = sb("ident", [P, P], F32)
         make_identity(nc, ident[:])
@@ -207,6 +211,9 @@ def tile_picked_yserial_silu_p_kernel(
         def gather_by_order(t):
             if t < 2:
                 nc.vector.tensor_copy(delayed(t, 0, whole), y[t].indirect(order_sb[:]))
+            elif t == 2:
+                for cols in halves:
+                    nc.vector.tensor_copy(delayed(t, 0, cols), y[t].indirect(entries(order_sb, cols)))
             else:
                 nc.scalar.activation(delayed(t, 0, whole), y[t].indirect(order_sb[:]), COPY)
 
@@ -226,8 +233,11 @@ def tile_picked_yserial_silu_p_kernel(
             for k in range(TAPS):
                 term = delayed(t, k, whole)
                 if k > 0:
-                    engine = nc.gpsimd if t == 0 else nc.vector
-                    engine.tensor_scalar(scaled[t, k][:], term, ratio[:, t, k - 1 : k], 0.0, op0=MULT, op1=ADD)
+                    factor = ratio[:, t, k - 1 : k]
+                    if k == 1:
+                        nc.gpsimd.tensor_scalar(scaled[t, k][:], term, factor, 0.0, op0=MULT, op1=ADD)
+                    else:
+                        nc.scalar.activation(scaled[t, k][:], term, COPY, scale=factor)
                     term = scaled[t, k][:]
                 for chunk in chunks:
                     nc.tensor.matmul(
@@ -251,12 +261,14 @@ def tile_picked_yserial_silu_p_kernel(
         def gather_by_back(t, cols):
             nc.vector.tensor_tensor(z[:, t, cols], rr[t][:].indirect(entries(back_sb, cols)), y[t][:, cols], ADD)
 
-        for t in range(1, PACK):
+        for t in (1, 2):
             leave_bank(t)
-        for t in range(PACK):
+        for t in range(3):
             gather_by_order(t)
-        for t in (0, 1):
-            sum_by_transposes(t)
+        sum_by_transposes(0)
+        leave_bank(3)
+        sum_by_transposes(1)
+        gather_by_order(3)
         for t in (2, 3):
             sum_taps(t)
         turn_back(0)

@@ -34,6 +34,8 @@ Y_WINDOW = 704
 WINDOW = 528
 PAD = 8
 TINY = 2.0**-32
+W2BF = "summed_sb1"
+W2C = "rr0"
 
 
 def tile_picked_yserial_silu_p_kernel(
@@ -62,9 +64,9 @@ def tile_picked_yserial_silu_p_kernel(
         w1_raw = [sb("w1_raw%d" % n, [P, part[2], H], F32) for n, part in enumerate(w1_parts)]
         w2_raw = sb("w2_raw", [P, PACK, N], F32)
         taps_sb = sb("taps_sb", [P, PACK * TAPS], F32)
-        y = [sb("y%d" % t, [P, Y_WINDOW if t < 2 else WINDOW], F32)[:] for t in range(PACK)]
+        y = [sb("y%d" % t, [P, Y_WINDOW], F32)[:] for t in range(PACK)]
         z = sb("z", [P, PACK, S], F32)
-        rr = [sb("rr%d" % t, [P, WINDOW], F32) for t in range(PACK)]
+        rr = {t: sb("rr%d" % t, [P, WINDOW], F32) for t in (0, 1, 3)}
         zeros = sb("zeros", [P, WINDOW - S], F32)
 
         def load_words(o):
@@ -93,8 +95,10 @@ def tile_picked_yserial_silu_p_kernel(
         nc.sync.dma_start(back_sb[:], back)
 
         nc.gpsimd.memset(zeros[:], 0.0)
+        for t in rr:
+            spare = S + 5 if t == 3 else S
+            nc.scalar.activation(rr[t][:, spare:], zeros[:, : WINDOW - spare], SILU)
         for t in range(PACK):
-            nc.scalar.activation(rr[t][:, S:], zeros[:], SILU)
             nc.gpsimd.memset(y[t][:, S:], 0.0)
 
         x_codes0 = sb("x_codes0", [P, S], U32)
@@ -107,13 +111,13 @@ def tile_picked_yserial_silu_p_kernel(
         shift = sb("shift", [P, PACK], F32)
         lead = z[:, 0, :PACK]
         inverse = sb("inverse", [P, PACK], F32)
-        ratio = sb("ratio", [P, PACK, TAPS - 1], F32)
+        ratio = rr[3][:, S - 3 : S + 5].rearrange("p (t k) -> p t k", k=TAPS - 1)
         nc.gpsimd.tensor_tensor(square[:], taps3[:, :, 0], taps3[:, :, 0], MULT)
         nc.gpsimd.tensor_scalar(shift[:], square[:], TINY * TINY, 2.0 * TINY, op0=IS_LT, op1=MULT)
         nc.gpsimd.tensor_tensor(lead, taps3[:, :, 0], shift[:], ADD)
         nc.vector.reciprocal(inverse[:], lead)
         nc.gpsimd.tensor_tensor(
-            ratio[:], taps3[:, :, 1:], inverse[:].unsqueeze(2).to_broadcast([P, PACK, TAPS - 1]), MULT
+            ratio, taps3[:, :, 1:], inverse[:].unsqueeze(2).to_broadcast([P, PACK, TAPS - 1]), MULT
         )
 
         w1_bf = [[sb("w1_bf%d_%d" % (o, u), [P, 2 * P * PACK], BF16) for u in range(2)] for o in range(PASSES)]
@@ -186,12 +190,12 @@ def tile_picked_yserial_silu_p_kernel(
 
         gg = [sb("gg%d" % t, [P, PAD + S], F32) for t in range(PACK)]
         filt = {2: sb("filt2", [P, S], F32)[:], 3: gg[2][:, :S]}
-        scaled = {
-            (t, k): sb("scaled%d_%d" % (t, k), [P, S], F32, tag="w1_codes1_1" if (t, k) == (0, 2) else "")
-            for t in (0, 1)
-            for k in (1, 2)
-        }
-        summed_sb = {0: sb("summed_sb0", [P, S], F32)[:], 1: filt[2]}
+        rr[2] = sb("rr2", [P, WINDOW], F32, tag="w1_codes1_1")
+        nc.gpsimd.memset(rr[2][:, S:], 0.0)
+        scaled = {(t, 1): sb("scaled%d" % t, [P, S], F32) for t in (0, 1)}
+        scaled[0, 2] = rr[2][:, :S]
+        scaled[1, 2] = rr[3][:, :S]
+        summed_sb = {t: sb("summed_sb%d" % t, [P, S], F32)[:] for t in (0, 1)}
         ident = sb("ident", [P, P], F32)
         make_identity(nc, ident[:])
         sum_banks = {0: "summed0", 1: "y_rest3"}
@@ -205,17 +209,14 @@ def tile_picked_yserial_silu_p_kernel(
         def delayed(t, k, cols):
             return gg[t][:, PAD - k + cols.start : PAD - k + cols.stop]
 
-        def leave_bank(t):
-            nc.scalar.copy(out=y[t][:, :S], in_=y_rest[t - 1][:])
+        def leave_bank(t, copy=nc.scalar.copy):
+            copy(out=y[t][:, :S], in_=y_rest[t - 1][:])
 
-        def gather_by_order(t):
-            if t < 2:
-                nc.vector.tensor_copy(delayed(t, 0, whole), y[t].indirect(order_sb[:]))
-            elif t == 2:
-                for cols in halves:
-                    nc.vector.tensor_copy(delayed(t, 0, cols), y[t].indirect(entries(order_sb, cols)))
+        def gather_by_order(t, eng, cols=whole):
+            if eng == "V":
+                nc.vector.tensor_copy(delayed(t, 0, cols), y[t].indirect(entries(order_sb, cols)))
             else:
-                nc.scalar.activation(delayed(t, 0, whole), y[t].indirect(order_sb[:]), COPY)
+                nc.scalar.activation(delayed(t, 0, cols), y[t].indirect(entries(order_sb, cols)), COPY)
 
         def sum_taps(t):
             for k in range(1, TAPS):
@@ -229,28 +230,31 @@ def tile_picked_yserial_silu_p_kernel(
                         op1=ADD,
                     )
 
-        def sum_by_transposes(t):
-            for k in range(TAPS):
-                term = delayed(t, k, whole)
-                if k > 0:
-                    factor = ratio[:, t, k - 1 : k]
-                    if k == 1:
-                        nc.gpsimd.tensor_scalar(scaled[t, k][:], term, factor, 0.0, op0=MULT, op1=ADD)
-                    else:
-                        nc.scalar.activation(scaled[t, k][:], term, COPY, scale=factor)
-                    term = scaled[t, k][:]
-                for chunk in chunks:
-                    nc.tensor.matmul(
-                        summed[t][:, chunk],
-                        lhsT=term[:, chunk],
-                        rhs=ident[:],
-                        is_transpose=True,
-                        start=(k == 0 and chunk == chunks[0]),
-                        stop=(k == TAPS - 1 and chunk == chunks[-1]),
-                    )
+        def scale(t, k, eng):
+            term = delayed(t, k, whole)
+            factor = ratio[:, t, k - 1 : k]
+            if eng == "S":
+                nc.scalar.activation(scaled[t, k][:], term, COPY, scale=factor)
+            else:
+                engine = nc.vector if eng == "V" else nc.gpsimd
+                engine.tensor_scalar(scaled[t, k][:], term, factor, 0.0, op0=MULT, op1=ADD)
 
-        def turn_back(t):
-            nc.scalar.copy(out=summed_sb[t], in_=summed[t][:])
+        def add(t, k, first=0, last=2):
+            term = delayed(t, k, whole) if k == 0 else scaled[t, k][:]
+            for chunk in chunks:
+                nc.tensor.matmul(
+                    summed[t][:, chunk],
+                    lhsT=term[:, chunk],
+                    rhs=ident[:],
+                    is_transpose=True,
+                    start=(k == first and chunk == chunks[0]),
+                    stop=(k == last and chunk == chunks[-1]),
+                )
+
+        def sums(t, copy=nc.scalar.copy):
+            copy(out=summed_sb[t], in_=summed[t][:])
+
+        def turn(t):
             for chunk in chunks:
                 nc.tensor.transpose(restored[t][:, chunk], summed_sb[t][:, chunk], ident[:])
 
@@ -261,61 +265,42 @@ def tile_picked_yserial_silu_p_kernel(
         def gather_by_back(t, cols):
             nc.vector.tensor_tensor(z[:, t, cols], rr[t][:].indirect(entries(back_sb, cols)), y[t][:, cols], ADD)
 
-        for t in (1, 2):
-            leave_bank(t)
-        for t in range(3):
-            gather_by_order(t)
-        sum_by_transposes(0)
-        leave_bank(3)
-        sum_by_transposes(1)
-        gather_by_order(3)
-        for t in (2, 3):
-            sum_taps(t)
-        turn_back(0)
-        silu(2)
-        turn_back(1)
-        silu(3)
-        silu(0)
-        silu(1)
-
-        w2_bf = sb("w2_bf", [P, N * PACK], BF16, tag="filt2")
-        nc.scalar.copy(
-            out=w2_bf[:].rearrange("p (c i j) -> p c j i", i=LINE, j=PACK),
-            in_=w2_raw[:].rearrange("p j (c i) -> p c j i", i=LINE),
-        )
-        for t in (2, 3):
-            gather_by_back(t, whole)
-        for cols in reversed(halves):
-            for t in (0, 1):
-                gather_by_back(t, cols)
-
-        w2_codes = sb("w2_codes", [P, N], U32, tag="rr0")
+        w2_bf = sb("w2_bf", [P, N * PACK], BF16, tag=W2BF)
+        w2_codes = sb("w2_codes", [P, N], U32, tag=W2C)
         w2_scale = sb("w2_scale", [P, N], U8)
-        nc.vector.quantize_mx(out=w2_codes[:].bitcast(FP8X4), scales=w2_scale[:], in_=w2_bf[:])
-
         out_sb = sb("out_sb", [P, S], F32)
-        upper = [(HALF, HALF, nc.scalar.copy, nc.vector.tensor_copy)]
-        lower = [
-            (0, QUARTER, nc.vector.tensor_copy, nc.scalar.copy),
-            (QUARTER, QUARTER, nc.scalar.copy, nc.vector.tensor_copy),
-        ]
-        pieces = upper + lower
-        z_bf = [sb("z_bf%d" % n, [P, piece[1] * PACK], BF16) for n, piece in enumerate(pieces)]
-        out_tags = ("y_rest2", "y_first2", "summed0")
-        out_ps = [psum.tile([P, piece[1]], F32, name="out_ps%d" % n, tag=out_tags[n]) for n, piece in enumerate(pieces)]
-        for n, (start, width, weave, leave) in enumerate(pieces):
-            points = z[:, :, start : start + width]
-            weave(
-                out=z_bf[n][:].rearrange("p (c i t) -> p c t i", i=LINE, t=PACK),
-                in_=points.rearrange("p t (c i) -> p c t i", i=LINE),
+        z_bf = sb("z_bf", [P, S * PACK], BF16)
+        eng_copy = {"V": nc.vector.tensor_copy, "S": nc.scalar.copy}
+
+        def weave_w2(eng):
+            if eng == "P":
+                nc.gpsimd.tensor_scalar(
+                    w2_bf[:].rearrange("p (c j) -> p c j", j=PACK), w2_raw[:].rearrange("p j c -> p c j"), 1.0, 0.0, op0=MULT, op1=ADD
+                )
+            else:
+                eng_copy[eng](
+                    out=w2_bf[:].rearrange("p (c i j) -> p c j i", i=LINE, j=PACK),
+                    in_=w2_raw[:].rearrange("p j (c i) -> p c j i", i=LINE),
+                )
+
+        def quant_w2():
+            nc.vector.quantize_mx(out=w2_codes[:].bitcast(FP8X4), scales=w2_scale[:], in_=w2_bf[:])
+
+        def weave(a, b, eng):
+            eng_copy[eng](
+                out=z_bf[:, a * PACK : b * PACK].rearrange("p (c i t) -> p c t i", i=LINE, t=PACK),
+                in_=z[:, :, a:b].rearrange("p t (c i) -> p c t i", i=LINE),
             )
-        for n, (start, width, weave, leave) in enumerate(pieces):
-            cols = slice(start, start + width)
-            z_codes = sb("z_codes%d" % n, [P, width], U32, tag="z" if n == 1 else "")
-            z_scale = sb("z_scale%d" % n, [P, width], U8)
-            nc.vector.quantize_mx(out=z_codes[:].bitcast(FP8X4), scales=z_scale[:], in_=z_bf[n][:])
+
+        out_ps = {}
+
+        def product2(a, b, bank, tag=""):
+            z_codes = sb("z_codes%d" % a, [P, b - a], U32, tag=tag)
+            z_scale = sb("z_scale%d" % a, [P, b - a], U8)
+            out_ps[a] = psum.tile([P, b - a], F32, name="out_ps%d" % a, tag=bank)
+            nc.vector.quantize_mx(out=z_codes[:].bitcast(FP8X4), scales=z_scale[:], in_=z_bf[:, a * PACK : b * PACK])
             nc.tensor.matmul_mx(
-                out=out_ps[n][:],
+                out=out_ps[a][:],
                 lhsT=w2_codes[:].bitcast(FP8X4),
                 lhsT_scale=w2_scale[:],
                 rhs=z_codes[:].bitcast(FP8X4),
@@ -323,7 +308,63 @@ def tile_picked_yserial_silu_p_kernel(
                 start=True,
                 stop=True,
             )
-            leave(out=out_sb[:, cols], in_=out_ps[n][:])
-            if (start + width) % HALF == 0:
-                half = halves[start // HALF]
-                nc.sync.dma_start(out=out[:, half], in_=out_sb[:, half])
+
+        def leave(a, b, eng):
+            eng_copy[eng](out=out_sb[:, a:b], in_=out_ps[a][:])
+
+        def store(a, b):
+            nc.sync.dma_start(out=out[:, a:b], in_=out_sb[:, a:b])
+
+        def plain_back(t, cols):
+            nc.scalar.activation(z[:, t, cols], rr[t][:].indirect(entries(back_sb, cols)), COPY)
+
+        def add_y(t, cols):
+            nc.vector.tensor_tensor(z[:, t, cols], z[:, t, cols], y[t][:, cols], ADD)
+
+        gather_by_order(0,"V",whole)
+        leave_bank(1)
+        leave_bank(2)
+        leave_bank(3)
+        gather_by_order(1,"V",whole)
+        gather_by_order(2,"V",halves[0])
+        gather_by_order(2,"V",halves[1])
+        scale(0,1,"P")
+        scale(0,2,"S")
+        gather_by_order(3,"S",whole)
+        scale(1,1,"P")
+        scale(1,2,"V")
+        add(0,0)
+        add(0,1)
+        add(0,2)
+        add(1,0)
+        add(1,1)
+        add(1,2)
+        sums(0)
+        turn(0)
+        sum_taps(2)
+        sum_taps(3)
+        silu(2)
+        sums(1)
+        turn(1)
+        silu(3)
+        silu(0)
+        silu(1)
+        weave_w2("S")
+        gather_by_back(2,whole)
+        gather_by_back(3,whole)
+        gather_by_back(0,halves[1])
+        gather_by_back(1,halves[1])
+        gather_by_back(0,halves[0])
+        gather_by_back(1,halves[0])
+        quant_w2()
+        weave(256,512,"S")
+        weave(0,128,"V")
+        weave(128,256,"S")
+        product2(256,512,"y_rest2")
+        product2(0,128,"y_first2","z")
+        product2(128,256,"summed0")
+        leave(256,512,"V")
+        leave(0,128,"S")
+        leave(128,256,"V")
+        store(256,512)
+        store(0,256)

@@ -34,8 +34,8 @@ Y_WINDOW = 704
 WINDOW = 528
 PAD = 8
 TINY = 2.0**-32
-W2BF = "summed_sb1"
-W2C = "rr0"
+W2BF = "w1_bf1_1"
+W2C = "scaled1"
 
 
 def tile_picked_yserial_silu_p_kernel(
@@ -64,8 +64,15 @@ def tile_picked_yserial_silu_p_kernel(
         w1_raw = [sb("w1_raw%d" % n, [P, part[2], H], F32) for n, part in enumerate(w1_parts)]
         w2_raw = sb("w2_raw", [P, PACK, N], F32)
         taps_sb = sb("taps_sb", [P, PACK * TAPS], F32)
-        y = [sb("y%d" % t, [P, Y_WINDOW], F32)[:] for t in range(PACK)]
-        z = sb("z", [P, PACK, S], F32)
+        y = {t: sb("y%d" % t, [P, Y_WINDOW], F32)[:] for t in (0, 2, 3)}
+        yz = sb("yz", [P, HALF + PACK * HALF], F32)
+        z_half = [yz[:, HALF:].rearrange("p (t c) -> p t c", t=PACK), sb("z_upper", [P, PACK, HALF], F32)[:]]
+
+        def z_at(t, cols):
+            h = cols.start // HALF
+            return z_half[h][:, t, cols.start - h * HALF : cols.stop - h * HALF]
+
+        y[1] = yz[:, :Y_WINDOW]
         rr = {t: sb("rr%d" % t, [P, WINDOW], F32) for t in (0, 1, 3)}
         zeros = sb("zeros", [P, WINDOW - S], F32)
 
@@ -109,7 +116,7 @@ def tile_picked_yserial_silu_p_kernel(
         taps3 = taps_sb[:].rearrange("p (t k) -> p t k", k=TAPS)
         square = sb("square", [P, PACK], F32)
         shift = sb("shift", [P, PACK], F32)
-        lead = z[:, 0, :PACK]
+        lead = z_half[0][:, 3, :PACK]
         inverse = sb("inverse", [P, PACK], F32)
         ratio = rr[3][:, S - 3 : S + 5].rearrange("p (t k) -> p t k", k=TAPS - 1)
         nc.gpsimd.tensor_tensor(square[:], taps3[:, :, 0], taps3[:, :, 0], MULT)
@@ -263,13 +270,18 @@ def tile_picked_yserial_silu_p_kernel(
             nc.scalar.activation(rr[t][:, :S], source, SILU, scale=lead[:, t : t + 1])
 
         def gather_by_back(t, cols):
-            nc.vector.tensor_tensor(z[:, t, cols], rr[t][:].indirect(entries(back_sb, cols)), y[t][:, cols], ADD)
+            nc.vector.tensor_tensor(z_at(t, cols), rr[t][:].indirect(entries(back_sb, cols)), y[t][:, cols], ADD)
 
         w2_bf = sb("w2_bf", [P, N * PACK], BF16, tag=W2BF)
         w2_codes = sb("w2_codes", [P, N], U32, tag=W2C)
         w2_scale = sb("w2_scale", [P, N], U8)
         out_sb = sb("out_sb", [P, S], F32)
         z_bf = sb("z_bf", [P, S * PACK], BF16)
+        last_bf = sb("last_bf", [P, QUARTER * PACK], BF16, tag="z_upper")
+
+        def woven(a, b):
+            return last_bf[:] if a == 0 else z_bf[:, a * PACK : b * PACK]
+
         eng_copy = {"V": nc.vector.tensor_copy, "S": nc.scalar.copy}
 
         def weave_w2(eng):
@@ -288,8 +300,8 @@ def tile_picked_yserial_silu_p_kernel(
 
         def weave(a, b, eng):
             eng_copy[eng](
-                out=z_bf[:, a * PACK : b * PACK].rearrange("p (c i t) -> p c t i", i=LINE, t=PACK),
-                in_=z[:, :, a:b].rearrange("p t (c i) -> p c t i", i=LINE),
+                out=woven(a, b).rearrange("p (c i t) -> p c t i", i=LINE, t=PACK),
+                in_=z_at(slice(0, PACK), slice(a, b)).rearrange("p t (c i) -> p c t i", i=LINE),
             )
 
         out_ps = {}
@@ -298,7 +310,7 @@ def tile_picked_yserial_silu_p_kernel(
             z_codes = sb("z_codes%d" % a, [P, b - a], U32, tag=tag)
             z_scale = sb("z_scale%d" % a, [P, b - a], U8)
             out_ps[a] = psum.tile([P, b - a], F32, name="out_ps%d" % a, tag=bank)
-            nc.vector.quantize_mx(out=z_codes[:].bitcast(FP8X4), scales=z_scale[:], in_=z_bf[:, a * PACK : b * PACK])
+            nc.vector.quantize_mx(out=z_codes[:].bitcast(FP8X4), scales=z_scale[:], in_=woven(a, b))
             nc.tensor.matmul_mx(
                 out=out_ps[a][:],
                 lhsT=w2_codes[:].bitcast(FP8X4),
@@ -316,11 +328,12 @@ def tile_picked_yserial_silu_p_kernel(
             nc.sync.dma_start(out=out[:, a:b], in_=out_sb[:, a:b])
 
         def plain_back(t, cols):
-            nc.scalar.activation(z[:, t, cols], rr[t][:].indirect(entries(back_sb, cols)), COPY)
+            nc.scalar.activation(z_at(t, cols), rr[t][:].indirect(entries(back_sb, cols)), COPY)
 
         def add_y(t, cols):
-            nc.vector.tensor_tensor(z[:, t, cols], z[:, t, cols], y[t][:, cols], ADD)
+            nc.vector.tensor_tensor(z_at(t, cols), z_at(t, cols), y[t][:, cols], ADD)
 
+        weave_w2("P")
         gather_by_order(0,"V",whole)
         leave_bank(1)
         leave_bank(2)
@@ -332,7 +345,7 @@ def tile_picked_yserial_silu_p_kernel(
         scale(0,2,"S")
         gather_by_order(3,"S",whole)
         scale(1,1,"P")
-        scale(1,2,"V")
+        scale(1,2,"S")
         add(0,0)
         add(0,1)
         add(0,2)
@@ -349,22 +362,25 @@ def tile_picked_yserial_silu_p_kernel(
         silu(3)
         silu(0)
         silu(1)
-        weave_w2("S")
-        gather_by_back(2,whole)
-        gather_by_back(3,whole)
+        quant_w2()
+        gather_by_back(2,halves[0])
+        gather_by_back(2,halves[1])
+        gather_by_back(3,halves[1])
         gather_by_back(0,halves[1])
         gather_by_back(1,halves[1])
-        gather_by_back(0,halves[0])
+        plain_back(3,halves[0])
         gather_by_back(1,halves[0])
-        quant_w2()
+        add_y(3,halves[0])
+        gather_by_back(0,slice(128,256))
+        gather_by_back(0,slice(0,128))
         weave(256,512,"S")
-        weave(0,128,"V")
         weave(128,256,"S")
         product2(256,512,"y_rest2")
-        product2(0,128,"y_first2","z")
+        weave(0,128,"V")
         product2(128,256,"summed0")
-        leave(256,512,"V")
-        leave(0,128,"S")
+        product2(0,128,"y_first2")
+        leave(256,512,"S")
         leave(128,256,"V")
+        leave(0,128,"V")
         store(256,512)
         store(0,256)

@@ -65,13 +65,8 @@ def tile_picked_yserial_silu_p_kernel(
         w2_raw = sb("w2_raw", [P, PACK, N], F32)
         taps_sb = sb("taps_sb", [P, PACK * TAPS], F32)
         y = {t: sb("y%d" % t, [P, Y_WINDOW], F32)[:] for t in (0, 2, 3)}
-        yz = sb("yz", [P, HALF + PACK * HALF], F32)
-        z_half = [yz[:, HALF:].rearrange("p (t c) -> p t c", t=PACK), sb("z_upper", [P, PACK, HALF], F32)[:]]
-
-        def z_at(t, cols):
-            h = cols.start // HALF
-            return z_half[h][:, t, cols.start - h * HALF : cols.stop - h * HALF]
-
+        yz = sb("yz", [P, PACK * (HALF + S)], F32)
+        z = yz[:].rearrange("p (t c) -> p t c", t=PACK)[:, :, HALF:]
         y[1] = yz[:, :Y_WINDOW]
         rr = {t: sb("rr%d" % t, [P, WINDOW], F32) for t in (0, 1, 3)}
         zeros = sb("zeros", [P, WINDOW - S], F32)
@@ -92,9 +87,9 @@ def tile_picked_yserial_silu_p_kernel(
                 out=scale_table[32 * q : 32 * q + SCALE_ROWS * PASSES, :].bitcast(I32),
                 in_=x_scales[:, SCALE_ROWS * q : SCALE_ROWS * (q + 1), :].bitcast(I32),
             )
+        nc.sync.dma_start(out=taps_sb[:], in_=taps.rearrange("(p t) k -> p (t k)", t=PACK))
         load_w1(0)
         load_words(1)
-        nc.sync.dma_start(out=taps_sb[:], in_=taps.rearrange("(p t) k -> p (t k)", t=PACK))
         load_w1(1)
         load_w1(2)
         nc.sync.dma_start(out=w2_raw[:], in_=w2.rearrange("(p j) m -> p j m", j=PACK))
@@ -116,7 +111,7 @@ def tile_picked_yserial_silu_p_kernel(
         taps3 = taps_sb[:].rearrange("p (t k) -> p t k", k=TAPS)
         square = sb("square", [P, PACK], F32)
         shift = sb("shift", [P, PACK], F32)
-        lead = z_half[0][:, 3, :PACK]
+        lead = sb("lead", [P, PACK], F32)[:]
         inverse = sb("inverse", [P, PACK], F32)
         ratio = rr[3][:, S - 3 : S + 5].rearrange("p (t k) -> p t k", k=TAPS - 1)
         nc.gpsimd.tensor_tensor(square[:], taps3[:, :, 0], taps3[:, :, 0], MULT)
@@ -202,7 +197,7 @@ def tile_picked_yserial_silu_p_kernel(
         scaled = {(t, 1): sb("scaled%d" % t, [P, S], F32) for t in (0, 1)}
         scaled[0, 2] = rr[2][:, :S]
         scaled[1, 2] = rr[3][:, :S]
-        summed_sb = {t: sb("summed_sb%d" % t, [P, S], F32)[:] for t in (0, 1)}
+        summed_sb = {0: sb("summed_sb0", [P, S], F32)[:], 1: yz[:, 3 * (HALF + S) : 3 * (HALF + S) + S]}
         ident = sb("ident", [P, P], F32)
         make_identity(nc, ident[:])
         sum_banks = {0: "summed0", 1: "y_rest3"}
@@ -270,18 +265,13 @@ def tile_picked_yserial_silu_p_kernel(
             nc.scalar.activation(rr[t][:, :S], source, SILU, scale=lead[:, t : t + 1])
 
         def gather_by_back(t, cols):
-            nc.vector.tensor_tensor(z_at(t, cols), rr[t][:].indirect(entries(back_sb, cols)), y[t][:, cols], ADD)
+            nc.vector.tensor_tensor(z[:, t, cols], rr[t][:].indirect(entries(back_sb, cols)), y[t][:, cols], ADD)
 
         w2_bf = sb("w2_bf", [P, N * PACK], BF16, tag=W2BF)
         w2_codes = sb("w2_codes", [P, N], U32, tag=W2C)
         w2_scale = sb("w2_scale", [P, N], U8)
         out_sb = sb("out_sb", [P, S], F32)
         z_bf = sb("z_bf", [P, S * PACK], BF16)
-        last_bf = sb("last_bf", [P, QUARTER * PACK], BF16, tag="z_upper")
-
-        def woven(a, b):
-            return last_bf[:] if a == 0 else z_bf[:, a * PACK : b * PACK]
-
         eng_copy = {"V": nc.vector.tensor_copy, "S": nc.scalar.copy}
 
         def weave_w2(eng):
@@ -300,8 +290,8 @@ def tile_picked_yserial_silu_p_kernel(
 
         def weave(a, b, eng):
             eng_copy[eng](
-                out=woven(a, b).rearrange("p (c i t) -> p c t i", i=LINE, t=PACK),
-                in_=z_at(slice(0, PACK), slice(a, b)).rearrange("p t (c i) -> p c t i", i=LINE),
+                out=z_bf[:, a * PACK : b * PACK].rearrange("p (c i t) -> p c t i", i=LINE, t=PACK),
+                in_=z[:, :, a:b].rearrange("p t (c i) -> p c t i", i=LINE),
             )
 
         out_ps = {}
@@ -310,7 +300,7 @@ def tile_picked_yserial_silu_p_kernel(
             z_codes = sb("z_codes%d" % a, [P, b - a], U32, tag=tag)
             z_scale = sb("z_scale%d" % a, [P, b - a], U8)
             out_ps[a] = psum.tile([P, b - a], F32, name="out_ps%d" % a, tag=bank)
-            nc.vector.quantize_mx(out=z_codes[:].bitcast(FP8X4), scales=z_scale[:], in_=woven(a, b))
+            nc.vector.quantize_mx(out=z_codes[:].bitcast(FP8X4), scales=z_scale[:], in_=z_bf[:, a * PACK : b * PACK])
             nc.tensor.matmul_mx(
                 out=out_ps[a][:],
                 lhsT=w2_codes[:].bitcast(FP8X4),
@@ -328,10 +318,10 @@ def tile_picked_yserial_silu_p_kernel(
             nc.sync.dma_start(out=out[:, a:b], in_=out_sb[:, a:b])
 
         def plain_back(t, cols):
-            nc.scalar.activation(z_at(t, cols), rr[t][:].indirect(entries(back_sb, cols)), COPY)
+            nc.scalar.activation(z[:, t, cols], rr[t][:].indirect(entries(back_sb, cols)), COPY)
 
         def add_y(t, cols):
-            nc.vector.tensor_tensor(z_at(t, cols), z_at(t, cols), y[t][:, cols], ADD)
+            nc.vector.tensor_tensor(z[:, t, cols], z[:, t, cols], y[t][:, cols], ADD)
 
         weave_w2("P")
         gather_by_order(0,"V",whole)
@@ -363,24 +353,27 @@ def tile_picked_yserial_silu_p_kernel(
         silu(0)
         silu(1)
         quant_w2()
-        gather_by_back(2,halves[0])
-        gather_by_back(2,halves[1])
+        gather_by_back(2,whole)
         gather_by_back(3,halves[1])
         gather_by_back(0,halves[1])
         gather_by_back(1,halves[1])
         plain_back(3,halves[0])
-        gather_by_back(1,halves[0])
+        plain_back(1,slice(0,128))
+        gather_by_back(1,slice(128,256))
         add_y(3,halves[0])
-        gather_by_back(0,slice(128,256))
-        gather_by_back(0,slice(0,128))
-        weave(256,512,"S")
-        weave(128,256,"S")
-        product2(256,512,"y_rest2")
-        weave(0,128,"V")
-        product2(128,256,"summed0")
+        gather_by_back(0,halves[0])
+        add_y(1,slice(0,128))
+        weave(384,512,"S")
+        weave(256,384,"S")
+        weave(160,256,"S")
+        product2(384,512,"y_rest2")
+        weave(0,160,"V")
+        product2(256,384,"y_first1")
         product2(0,128,"y_first2")
-        leave(256,512,"S")
-        leave(128,256,"V")
+        product2(128,256,"summed0")
+        leave(384,512,"S")
+        leave(256,384,"S")
         leave(0,128,"V")
+        leave(128,256,"V")
         store(256,512)
         store(0,256)

@@ -35,7 +35,7 @@ WINDOW = 528
 PAD = 8
 TINY = 2.0**-32
 W2BF = "w1_bf1_1"
-W2C = "scaled1"
+W2C = "rr0"
 
 
 def tile_picked_yserial_silu_p_kernel(
@@ -98,8 +98,7 @@ def tile_picked_yserial_silu_p_kernel(
 
         nc.gpsimd.memset(zeros[:], 0.0)
         for t in rr:
-            spare = S + 5 if t == 3 else S
-            nc.scalar.activation(rr[t][:, spare:], zeros[:, : WINDOW - spare], SILU)
+            nc.scalar.activation(rr[t][:, S:], zeros[:], SILU)
         for t in range(PACK):
             nc.gpsimd.memset(y[t][:, S:], 0.0)
 
@@ -113,7 +112,7 @@ def tile_picked_yserial_silu_p_kernel(
         shift = sb("shift", [P, PACK], F32)
         lead = sb("lead", [P, PACK], F32)[:]
         inverse = sb("inverse", [P, PACK], F32)
-        ratio = rr[3][:, S - 3 : S + 5].rearrange("p (t k) -> p t k", k=TAPS - 1)
+        ratio = sb("ratio", [P, PACK, TAPS - 1], F32)[:]
         nc.gpsimd.tensor_tensor(square[:], taps3[:, :, 0], taps3[:, :, 0], MULT)
         nc.gpsimd.tensor_scalar(shift[:], square[:], TINY * TINY, 2.0 * TINY, op0=IS_LT, op1=MULT)
         nc.gpsimd.tensor_tensor(lead, taps3[:, :, 0], shift[:], ADD)
@@ -152,7 +151,8 @@ def tile_picked_yserial_silu_p_kernel(
         y_first = [
             psum.tile([P, cols.stop - cols.start], F32, name="y_first%d" % n) for n, cols in enumerate(first_pieces)
         ]
-        y_rest = [psum.tile([P, S], F32, name="y_rest%d" % t) for t in range(1, PACK)]
+        y_second = [psum.tile([P, HALF], F32, name=name) for name in ("summed0", "y_rest1")]
+        y_rest = {t: psum.tile([P, S], F32, name="y_rest%d" % t) for t in (2, 3)}
 
         def product1(o, t, acc, x_codes, cols):
             m = slice((t % 2) * P, (t % 2 + 1) * P)
@@ -169,8 +169,10 @@ def tile_picked_yserial_silu_p_kernel(
         def products(o, x_codes):
             for n, cols in enumerate(first_pieces):
                 product1(o, 0, y_first[n][:], x_codes, cols)
-            for t in range(1, PACK):
-                product1(o, t, y_rest[t - 1][:], x_codes, whole)
+            for n, cols in enumerate(halves):
+                product1(o, 1, y_second[n][:], x_codes, cols)
+            for t in (2, 3):
+                product1(o, t, y_rest[t][:], x_codes, whole)
 
         weave_w1(0)
         quantize_w1(0, 0, 2)
@@ -193,9 +195,9 @@ def tile_picked_yserial_silu_p_kernel(
         gg = [sb("gg%d" % t, [P, PAD + S], F32) for t in range(PACK)]
         filt = {2: sb("filt2", [P, S], F32)[:], 3: gg[2][:, :S]}
         rr[2] = sb("rr2", [P, WINDOW], F32, tag="w1_codes1_1")
-        nc.gpsimd.memset(rr[2][:, S:], 0.0)
+        nc.gpsimd.memset(rr[2][:, S + PAD :], 0.0)
         scaled = {(t, 1): sb("scaled%d" % t, [P, S], F32) for t in (0, 1)}
-        scaled[0, 2] = rr[2][:, :S]
+        scaled[0, 2] = rr[2][:, PAD : PAD + S]
         scaled[1, 2] = rr[3][:, :S]
         summed_sb = {0: sb("summed_sb0", [P, S], F32)[:], 1: yz[:, 3 * (HALF + S) : 3 * (HALF + S) + S]}
         ident = sb("ident", [P, P], F32)
@@ -212,7 +214,7 @@ def tile_picked_yserial_silu_p_kernel(
             return gg[t][:, PAD - k + cols.start : PAD - k + cols.stop]
 
         def leave_bank(t, copy=nc.scalar.copy):
-            copy(out=y[t][:, :S], in_=y_rest[t - 1][:])
+            copy(out=y[t][:, :S], in_=y_rest[t][:])
 
         def gather_by_order(t, eng, cols=whole):
             if eng == "V":
@@ -243,14 +245,15 @@ def tile_picked_yserial_silu_p_kernel(
 
         def add(t, k, first=0, last=2):
             term = delayed(t, k, whole) if k == 0 else scaled[t, k][:]
-            for chunk in chunks:
+            runs = [chunks[n] for n in (0, 2, 3, 1)]
+            for chunk in runs:
                 nc.tensor.matmul(
                     summed[t][:, chunk],
                     lhsT=term[:, chunk],
                     rhs=ident[:],
                     is_transpose=True,
-                    start=(k == first and chunk == chunks[0]),
-                    stop=(k == last and chunk == chunks[-1]),
+                    start=(k == first and chunk == runs[0]),
+                    stop=(k == last and chunk == runs[-1]),
                 )
 
         def sums(t, copy=nc.scalar.copy):
@@ -260,9 +263,9 @@ def tile_picked_yserial_silu_p_kernel(
             for chunk in chunks:
                 nc.tensor.transpose(restored[t][:, chunk], summed_sb[t][:, chunk], ident[:])
 
-        def silu(t):
-            source = restored[t][:] if t < 2 else filt[t]
-            nc.scalar.activation(rr[t][:, :S], source, SILU, scale=lead[:, t : t + 1])
+        def silu(t, cols=whole):
+            source = restored[t] if t < 2 else filt[t]
+            nc.scalar.activation(rr[t][:, cols], source[:, cols], SILU, scale=lead[:, t : t + 1])
 
         def gather_by_back(t, cols):
             nc.vector.tensor_tensor(z[:, t, cols], rr[t][:].indirect(entries(back_sb, cols)), y[t][:, cols], ADD)
@@ -324,8 +327,9 @@ def tile_picked_yserial_silu_p_kernel(
             nc.vector.tensor_tensor(z[:, t, cols], z[:, t, cols], y[t][:, cols], ADD)
 
         weave_w2("P")
+        nc.vector.tensor_copy(out=y[1][:, halves[0]], in_=y_second[0][:])
         gather_by_order(0,"V",whole)
-        leave_bank(1)
+        nc.scalar.copy(out=y[1][:, halves[1]], in_=y_second[1][:])
         leave_bank(2)
         leave_bank(3)
         gather_by_order(1,"V",whole)
@@ -346,28 +350,28 @@ def tile_picked_yserial_silu_p_kernel(
         turn(0)
         sum_taps(2)
         sum_taps(3)
-        silu(2)
+        silu(2,halves[0])
+        silu(2,halves[1])
         sums(1)
         turn(1)
-        silu(3)
         silu(0)
+        silu(3)
         silu(1)
-        quant_w2()
         gather_by_back(2,whole)
-        gather_by_back(3,halves[1])
         gather_by_back(0,halves[1])
+        gather_by_back(3,halves[1])
         gather_by_back(1,halves[1])
         plain_back(3,halves[0])
-        plain_back(1,slice(0,128))
-        gather_by_back(1,slice(128,256))
+        plain_back(1,halves[0])
         add_y(3,halves[0])
         gather_by_back(0,halves[0])
-        add_y(1,slice(0,128))
+        add_y(1,halves[0])
+        quant_w2()
         weave(384,512,"S")
         weave(256,384,"S")
-        weave(160,256,"S")
+        weave(192,256,"S")
         product2(384,512,"y_rest2")
-        weave(0,160,"V")
+        weave(0,192,"V")
         product2(256,384,"y_first1")
         product2(0,128,"y_first2")
         product2(128,256,"summed0")

@@ -198,8 +198,8 @@ def tile_picked_yserial_silu_p_kernel(
         nc.gpsimd.memset(rr[2][:, S + PAD :], 0.0)
         scaled = {(t, 1): sb("scaled%d" % t, [P, S], F32) for t in (0, 1)}
         scaled[0, 2] = rr[2][:, PAD : PAD + S]
-        scaled[1, 2] = rr[3][:, :S]
-        summed_sb = {0: sb("summed_sb0", [P, S], F32)[:], 1: yz[:, 3 * (HALF + S) : 3 * (HALF + S) + S]}
+        scaled[1, 2] = sb("scaled1_2", [P, S], F32)
+        summed_sb = {0: rr[3][:, :S], 1: yz[:, 3 * (HALF + S) : 3 * (HALF + S) + S]}
         ident = sb("ident", [P, P], F32)
         make_identity(nc, ident[:])
         sum_banks = {0: "summed0", 1: "y_rest3"}

@@ -30,12 +30,11 @@ HALF = S // 2
 QUARTER = S // 4
 QUADRANTS = 4
 SCALE_ROWS = 4
-Y_WINDOW = 704
+WIDE_WINDOW = 704
 WINDOW = 528
 PAD = 8
 TINY = 2.0**-32
-W2BF = "w1_bf1_1"
-W2C = "rr0"
+VECTOR_WEAVES = 192
 
 
 def tile_picked_yserial_silu_p_kernel(
@@ -64,11 +63,16 @@ def tile_picked_yserial_silu_p_kernel(
         w1_raw = [sb("w1_raw%d" % n, [P, part[2], H], F32) for n, part in enumerate(w1_parts)]
         w2_raw = sb("w2_raw", [P, PACK, N], F32)
         taps_sb = sb("taps_sb", [P, PACK * TAPS], F32)
-        y = {t: sb("y%d" % t, [P, Y_WINDOW], F32)[:] for t in (0, 2, 3)}
-        yz = sb("yz", [P, PACK * (HALF + S)], F32)
+        pitch = HALF + S
+        yz = sb("yz", [P, PACK * pitch], F32)
         z = yz[:].rearrange("p (t c) -> p t c", t=PACK)[:, :, HALF:]
-        y[1] = yz[:, :Y_WINDOW]
-        rr = {t: sb("rr%d" % t, [P, WINDOW], F32) for t in (0, 1, 3)}
+        y = [
+            sb("y0", [P, WIDE_WINDOW], F32)[:],
+            yz[:, :WIDE_WINDOW],
+            sb("y2", [P, S], F32)[:],
+            sb("y3", [P, WINDOW], F32)[:],
+        ]
+        rr = {t: sb("rr%d" % t, [P, S], F32) for t in (0, 1, 3)}
         zeros = sb("zeros", [P, WINDOW - S], F32)
 
         def load_words(o):
@@ -97,9 +101,8 @@ def tile_picked_yserial_silu_p_kernel(
         nc.sync.dma_start(back_sb[:], back)
 
         nc.gpsimd.memset(zeros[:], 0.0)
-        for t in rr:
-            nc.scalar.activation(rr[t][:, S:], zeros[:], SILU)
-        for t in range(PACK):
+        nc.scalar.activation(y[3][:, S:], zeros[:], SILU)
+        for t in (0, 1):
             nc.gpsimd.memset(y[t][:, S:], 0.0)
 
         x_codes0 = sb("x_codes0", [P, S], U32)
@@ -110,15 +113,15 @@ def tile_picked_yserial_silu_p_kernel(
         taps3 = taps_sb[:].rearrange("p (t k) -> p t k", k=TAPS)
         square = sb("square", [P, PACK], F32)
         shift = sb("shift", [P, PACK], F32)
-        lead = sb("lead", [P, PACK], F32)[:]
+        lead = sb("lead", [P, PACK], F32)
         inverse = sb("inverse", [P, PACK], F32)
-        ratio = sb("ratio", [P, PACK, TAPS - 1], F32)[:]
+        ratio = sb("ratio", [P, PACK, TAPS - 1], F32)
         nc.gpsimd.tensor_tensor(square[:], taps3[:, :, 0], taps3[:, :, 0], MULT)
         nc.gpsimd.tensor_scalar(shift[:], square[:], TINY * TINY, 2.0 * TINY, op0=IS_LT, op1=MULT)
-        nc.gpsimd.tensor_tensor(lead, taps3[:, :, 0], shift[:], ADD)
-        nc.vector.reciprocal(inverse[:], lead)
+        nc.gpsimd.tensor_tensor(lead[:], taps3[:, :, 0], shift[:], ADD)
+        nc.vector.reciprocal(inverse[:], lead[:])
         nc.gpsimd.tensor_tensor(
-            ratio, taps3[:, :, 1:], inverse[:].unsqueeze(2).to_broadcast([P, PACK, TAPS - 1]), MULT
+            ratio[:], taps3[:, :, 1:], inverse[:].unsqueeze(2).to_broadcast([P, PACK, TAPS - 1]), MULT
         )
 
         w1_bf = [[sb("w1_bf%d_%d" % (o, u), [P, 2 * P * PACK], BF16) for u in range(2)] for o in range(PASSES)]
@@ -147,11 +150,9 @@ def tile_picked_yserial_silu_p_kernel(
                 in_=w1_bf[o][u][:, e * P * PACK : (e + tiles) * P * PACK],
             )
 
-        first_pieces = [slice(start, start + QUARTER) for start in range(0, S, QUARTER)]
-        y_first = [
-            psum.tile([P, cols.stop - cols.start], F32, name="y_first%d" % n) for n, cols in enumerate(first_pieces)
-        ]
-        y_second = [psum.tile([P, HALF], F32, name=name) for name in ("summed0", "y_rest1")]
+        quarters = [slice(start, start + QUARTER) for start in range(0, S, QUARTER)]
+        y_first = [psum.tile([P, QUARTER], F32, name="y_first%d" % n) for n in range(len(quarters))]
+        y_second = [psum.tile([P, HALF], F32, name="y_second%d" % h) for h in range(len(halves))]
         y_rest = {t: psum.tile([P, S], F32, name="y_rest%d" % t) for t in (2, 3)}
 
         def product1(o, t, acc, x_codes, cols):
@@ -167,7 +168,7 @@ def tile_picked_yserial_silu_p_kernel(
             )
 
         def products(o, x_codes):
-            for n, cols in enumerate(first_pieces):
+            for n, cols in enumerate(quarters):
                 product1(o, 0, y_first[n][:], x_codes, cols)
             for n, cols in enumerate(halves):
                 product1(o, 1, y_second[n][:], x_codes, cols)
@@ -190,39 +191,58 @@ def tile_picked_yserial_silu_p_kernel(
         quantize_w1(1, 2, 2)
         products(1, x_codes1)
         for n, copy in enumerate((nc.vector.tensor_copy, nc.scalar.copy) * 2):
-            copy(out=y[0][:, first_pieces[n]], in_=y_first[n][:])
+            copy(out=y[0][:, quarters[n]], in_=y_first[n][:])
 
         gg = [sb("gg%d" % t, [P, PAD + S], F32) for t in range(PACK)]
         filt = {2: sb("filt2", [P, S], F32)[:], 3: gg[2][:, :S]}
         rr[2] = sb("rr2", [P, WINDOW], F32, tag="w1_codes1_1")
         nc.gpsimd.memset(rr[2][:, S + PAD :], 0.0)
-        scaled = {(t, 1): sb("scaled%d" % t, [P, S], F32) for t in (0, 1)}
-        scaled[0, 2] = rr[2][:, PAD : PAD + S]
-        scaled[1, 2] = sb("scaled1_2", [P, S], F32)
-        summed_sb = {0: rr[3][:, :S], 1: yz[:, 3 * (HALF + S) : 3 * (HALF + S) + S]}
+        scaled = {
+            (0, 1): sb("scaled0_1", [P, S], F32)[:],
+            (1, 1): sb("scaled1_1", [P, S], F32)[:],
+            (0, 2): rr[2][:, PAD : PAD + S],
+            (1, 2): sb("scaled1_2", [P, S], F32)[:],
+        }
+        summed_sb = {0: rr[3][:], 1: yz[:, 3 * pitch : 3 * pitch + S]}
         ident = sb("ident", [P, P], F32)
         make_identity(nc, ident[:])
-        sum_banks = {0: "summed0", 1: "y_rest3"}
+        sum_banks = {0: "y_second0", 1: "y_rest3"}
         back_banks = {0: "y_first3", 1: "y_first0"}
         summed = {t: psum.tile([P, S], F32, name="summed%d" % t, tag=sum_banks[t]) for t in (0, 1)}
         restored = {t: psum.tile([P, S], F32, name="restored%d" % t, tag=back_banks[t]) for t in (0, 1)}
-        chunks = [slice(start, start + P) for start in range(0, S, P)]
         for t in range(PACK):
             nc.gpsimd.memset(gg[t][:, :PAD], 0.0)
 
         def delayed(t, k, cols):
             return gg[t][:, PAD - k + cols.start : PAD - k + cols.stop]
 
-        def leave_bank(t, copy=nc.scalar.copy):
-            copy(out=y[t][:, :S], in_=y_rest[t][:])
+        def gather_by_order(t, cols):
+            nc.vector.tensor_copy(delayed(t, 0, cols), y[t].indirect(entries(order_sb, cols)))
 
-        def gather_by_order(t, eng, cols=whole):
-            if eng == "V":
-                nc.vector.tensor_copy(delayed(t, 0, cols), y[t].indirect(entries(order_sb, cols)))
-            else:
-                nc.scalar.activation(delayed(t, 0, cols), y[t].indirect(entries(order_sb, cols)), COPY)
+        def scale_terms(t):
+            nc.gpsimd.tensor_scalar(scaled[t, 1], delayed(t, 1, whole), ratio[:, t, 0:1], 0.0, op0=MULT, op1=ADD)
+            nc.scalar.activation(scaled[t, 2], delayed(t, 2, whole), COPY, scale=ratio[:, t, 1:2])
 
-        def sum_taps(t):
+        def sum_by_transposes(t):
+            runs = [quarters[0], quarters[2], quarters[3], quarters[1]]
+            for k in range(TAPS):
+                term = delayed(t, 0, whole) if k == 0 else scaled[t, k]
+                for run in runs:
+                    nc.tensor.matmul(
+                        summed[t][:, run],
+                        lhsT=term[:, run],
+                        rhs=ident[:],
+                        is_transpose=True,
+                        start=(k == 0 and run == runs[0]),
+                        stop=(k == TAPS - 1 and run == runs[-1]),
+                    )
+
+        def turn_back(t):
+            nc.scalar.copy(out=summed_sb[t], in_=summed[t][:])
+            for run in quarters:
+                nc.tensor.transpose(restored[t][:, run], summed_sb[t][:, run], ident[:])
+
+        def sum_on_vector(t):
             for k in range(1, TAPS):
                 for cols in halves:
                     nc.vector.scalar_tensor_tensor(
@@ -234,78 +254,86 @@ def tile_picked_yserial_silu_p_kernel(
                         op1=ADD,
                     )
 
-        def scale(t, k, eng):
-            term = delayed(t, k, whole)
-            factor = ratio[:, t, k - 1 : k]
-            if eng == "S":
-                nc.scalar.activation(scaled[t, k][:], term, COPY, scale=factor)
-            else:
-                engine = nc.vector if eng == "V" else nc.gpsimd
-                engine.tensor_scalar(scaled[t, k][:], term, factor, 0.0, op0=MULT, op1=ADD)
-
-        def add(t, k, first=0, last=2):
-            term = delayed(t, k, whole) if k == 0 else scaled[t, k][:]
-            runs = [chunks[n] for n in (0, 2, 3, 1)]
-            for chunk in runs:
-                nc.tensor.matmul(
-                    summed[t][:, chunk],
-                    lhsT=term[:, chunk],
-                    rhs=ident[:],
-                    is_transpose=True,
-                    start=(k == first and chunk == runs[0]),
-                    stop=(k == last and chunk == runs[-1]),
-                )
-
-        def sums(t, copy=nc.scalar.copy):
-            copy(out=summed_sb[t], in_=summed[t][:])
-
-        def turn(t):
-            for chunk in chunks:
-                nc.tensor.transpose(restored[t][:, chunk], summed_sb[t][:, chunk], ident[:])
-
-        def silu(t, cols=whole):
-            source = restored[t] if t < 2 else filt[t]
+        def silu(t, cols):
+            source = restored[t] if t in restored else filt[t]
             nc.scalar.activation(rr[t][:, cols], source[:, cols], SILU, scale=lead[:, t : t + 1])
 
-        def gather_by_back(t, cols):
-            nc.vector.tensor_tensor(z[:, t, cols], rr[t][:].indirect(entries(back_sb, cols)), y[t][:, cols], ADD)
+        w2_bf = sb("w2_bf", [P, N * PACK], BF16, tag="w1_bf1_1")
+        nc.gpsimd.tensor_scalar(
+            w2_bf[:].rearrange("p (c j) -> p c j", j=PACK),
+            w2_raw[:].rearrange("p j c -> p c j"),
+            1.0,
+            0.0,
+            op0=MULT,
+            op1=ADD,
+        )
 
-        w2_bf = sb("w2_bf", [P, N * PACK], BF16, tag=W2BF)
-        w2_codes = sb("w2_codes", [P, N], U32, tag=W2C)
+        lower, upper = halves
+        nc.vector.tensor_copy(out=y[1][:, lower], in_=y_second[0][:])
+        gather_by_order(0, whole)
+        nc.scalar.copy(out=y[1][:, upper], in_=y_second[1][:])
+        for t in y_rest:
+            nc.scalar.copy(out=y[t][:, :S], in_=y_rest[t][:])
+        gather_by_order(1, whole)
+        for cols in halves:
+            gather_by_order(2, cols)
+        scale_terms(0)
+        nc.scalar.activation(delayed(3, 0, whole), y[3].indirect(order_sb[:]), COPY)
+        scale_terms(1)
+        for t in (0, 1):
+            sum_by_transposes(t)
+        turn_back(0)
+        for t in filt:
+            sum_on_vector(t)
+        for cols in halves:
+            silu(2, cols)
+        turn_back(1)
+        for t in (0, 3, 1):
+            silu(t, whole)
+
+        def picked(t, cols):
+            return rr[t][:].indirect(entries(back_sb, cols))
+
+        def gather_and_add(t, cols):
+            nc.vector.tensor_tensor(z[:, t, cols], picked(t, cols), y[t][:, cols], ADD)
+
+        def add_y(t):
+            nc.vector.tensor_tensor(z[:, t, lower], z[:, t, lower], y[t][:, lower], ADD)
+
+        gather_and_add(2, whole)
+        for t in (0, 3, 1):
+            gather_and_add(t, upper)
+        for t in (3, 1):
+            nc.scalar.activation(z[:, t, lower], picked(t, lower), COPY)
+        add_y(3)
+        gather_and_add(0, lower)
+        add_y(1)
+
+        w2_codes = sb("w2_codes", [P, N], U32, tag="rr0")
         w2_scale = sb("w2_scale", [P, N], U8)
-        out_sb = sb("out_sb", [P, S], F32)
+        nc.vector.quantize_mx(out=w2_codes[:].bitcast(FP8X4), scales=w2_scale[:], in_=w2_bf[:])
+
         z_bf = sb("z_bf", [P, S * PACK], BF16)
-        eng_copy = {"V": nc.vector.tensor_copy, "S": nc.scalar.copy}
-
-        def weave_w2(eng):
-            if eng == "P":
-                nc.gpsimd.tensor_scalar(
-                    w2_bf[:].rearrange("p (c j) -> p c j", j=PACK), w2_raw[:].rearrange("p j c -> p c j"), 1.0, 0.0, op0=MULT, op1=ADD
-                )
-            else:
-                eng_copy[eng](
-                    out=w2_bf[:].rearrange("p (c i j) -> p c j i", i=LINE, j=PACK),
-                    in_=w2_raw[:].rearrange("p j (c i) -> p c j i", i=LINE),
-                )
-
-        def quant_w2():
-            nc.vector.quantize_mx(out=w2_codes[:].bitcast(FP8X4), scales=w2_scale[:], in_=w2_bf[:])
-
-        def weave(a, b, eng):
-            eng_copy[eng](
-                out=z_bf[:, a * PACK : b * PACK].rearrange("p (c i t) -> p c t i", i=LINE, t=PACK),
-                in_=z[:, :, a:b].rearrange("p t (c i) -> p c t i", i=LINE),
-            )
-
+        out_sb = sb("out_sb", [P, S], F32)
+        out_banks = ("y_first2", "y_second0", "y_first1", "y_rest2")
         out_ps = {}
 
-        def product2(a, b, bank, tag=""):
-            z_codes = sb("z_codes%d" % a, [P, b - a], U32, tag=tag)
-            z_scale = sb("z_scale%d" % a, [P, b - a], U8)
-            out_ps[a] = psum.tile([P, b - a], F32, name="out_ps%d" % a, tag=bank)
-            nc.vector.quantize_mx(out=z_codes[:].bitcast(FP8X4), scales=z_scale[:], in_=z_bf[:, a * PACK : b * PACK])
+        def weave_z(copy, cols):
+            copy(
+                out=z_bf[:, cols.start * PACK : cols.stop * PACK].rearrange("p (c i t) -> p c t i", i=LINE, t=PACK),
+                in_=z[:, :, cols].rearrange("p t (c i) -> p c t i", i=LINE),
+            )
+
+        def product2(n):
+            cols = quarters[n]
+            z_codes = sb("z_codes%d" % n, [P, QUARTER], U32)
+            z_scale = sb("z_scale%d" % n, [P, QUARTER], U8)
+            out_ps[n] = psum.tile([P, QUARTER], F32, name="out_ps%d" % n, tag=out_banks[n])
+            nc.vector.quantize_mx(
+                out=z_codes[:].bitcast(FP8X4), scales=z_scale[:], in_=z_bf[:, cols.start * PACK : cols.stop * PACK]
+            )
             nc.tensor.matmul_mx(
-                out=out_ps[a][:],
+                out=out_ps[n][:],
                 lhsT=w2_codes[:].bitcast(FP8X4),
                 lhsT_scale=w2_scale[:],
                 rhs=z_codes[:].bitcast(FP8X4),
@@ -314,70 +342,15 @@ def tile_picked_yserial_silu_p_kernel(
                 stop=True,
             )
 
-        def leave(a, b, eng):
-            eng_copy[eng](out=out_sb[:, a:b], in_=out_ps[a][:])
-
-        def store(a, b):
-            nc.sync.dma_start(out=out[:, a:b], in_=out_sb[:, a:b])
-
-        def plain_back(t, cols):
-            nc.scalar.activation(z[:, t, cols], rr[t][:].indirect(entries(back_sb, cols)), COPY)
-
-        def add_y(t, cols):
-            nc.vector.tensor_tensor(z[:, t, cols], z[:, t, cols], y[t][:, cols], ADD)
-
-        weave_w2("P")
-        nc.vector.tensor_copy(out=y[1][:, halves[0]], in_=y_second[0][:])
-        gather_by_order(0,"V",whole)
-        nc.scalar.copy(out=y[1][:, halves[1]], in_=y_second[1][:])
-        leave_bank(2)
-        leave_bank(3)
-        gather_by_order(1,"V",whole)
-        gather_by_order(2,"V",halves[0])
-        gather_by_order(2,"V",halves[1])
-        scale(0,1,"P")
-        scale(0,2,"S")
-        gather_by_order(3,"S",whole)
-        scale(1,1,"P")
-        scale(1,2,"S")
-        add(0,0)
-        add(0,1)
-        add(0,2)
-        add(1,0)
-        add(1,1)
-        add(1,2)
-        sums(0)
-        turn(0)
-        sum_taps(2)
-        sum_taps(3)
-        silu(2,halves[0])
-        silu(2,halves[1])
-        sums(1)
-        turn(1)
-        silu(0)
-        silu(3)
-        silu(1)
-        gather_by_back(2,whole)
-        gather_by_back(0,halves[1])
-        gather_by_back(3,halves[1])
-        gather_by_back(1,halves[1])
-        plain_back(3,halves[0])
-        plain_back(1,halves[0])
-        add_y(3,halves[0])
-        gather_by_back(0,halves[0])
-        add_y(1,halves[0])
-        quant_w2()
-        weave(384,512,"S")
-        weave(256,384,"S")
-        weave(192,256,"S")
-        product2(384,512,"y_rest2")
-        weave(0,192,"V")
-        product2(256,384,"y_first1")
-        product2(0,128,"y_first2")
-        product2(128,256,"summed0")
-        leave(384,512,"S")
-        leave(256,384,"S")
-        leave(0,128,"V")
-        leave(128,256,"V")
-        store(256,512)
-        store(0,256)
+        for cols in (quarters[3], quarters[2], slice(VECTOR_WEAVES, HALF)):
+            weave_z(nc.scalar.copy, cols)
+        product2(3)
+        weave_z(nc.vector.tensor_copy, slice(0, VECTOR_WEAVES))
+        for n in (2, 0, 1):
+            product2(n)
+        for n in (3, 2):
+            nc.scalar.copy(out=out_sb[:, quarters[n]], in_=out_ps[n][:])
+        for n in (0, 1):
+            nc.vector.tensor_copy(out=out_sb[:, quarters[n]], in_=out_ps[n][:])
+        for cols in (upper, lower):
+            nc.sync.dma_start(out=out[:, cols], in_=out_sb[:, cols])

@@ -67,7 +67,7 @@ def tile_picked_yserial_silu_p_kernel(
         yz = sb("yz", [P, PACK * pitch], F32)
         z = yz[:].rearrange("p (t c) -> p t c", t=PACK)[:, :, HALF:]
         y = [
-            sb("y0", [P, WIDE_WINDOW], F32)[:],
+            sb("y0", [P, S], F32)[:],
             yz[:, :WIDE_WINDOW],
             sb("y2", [P, S], F32)[:],
             sb("y3", [P, WINDOW], F32)[:],
@@ -102,8 +102,7 @@ def tile_picked_yserial_silu_p_kernel(
 
         nc.gpsimd.memset(zeros[:], 0.0)
         nc.scalar.activation(y[3][:, S:], zeros[:], SILU)
-        for t in (0, 1):
-            nc.gpsimd.memset(y[t][:, S:], 0.0)
+        nc.gpsimd.memset(y[1][:, S:], 0.0)
 
         x_codes0 = sb("x_codes0", [P, S], U32)
         x_scale = sb("x_scale", [P, S], U8)
@@ -172,7 +171,7 @@ def tile_picked_yserial_silu_p_kernel(
                 product1(o, 0, y_first[n][:], x_codes, cols)
             for n, cols in enumerate(halves):
                 product1(o, 1, y_second[n][:], x_codes, cols)
-            for t in (2, 3):
+            for t in (3, 2):
                 product1(o, t, y_rest[t][:], x_codes, whole)
 
         weave_w1(0)
@@ -196,14 +195,23 @@ def tile_picked_yserial_silu_p_kernel(
         gg = [sb("gg%d" % t, [P, PAD + S], F32) for t in range(PACK)]
         filt = {2: sb("filt2", [P, S], F32)[:], 3: gg[2][:, :S]}
         rr[2] = sb("rr2", [P, WINDOW], F32, tag="w1_codes1_1")
-        nc.gpsimd.memset(rr[2][:, S + PAD :], 0.0)
+        nc.gpsimd.memset(rr[2][:, S:], 0.0)
         scaled = {
             (0, 1): sb("scaled0_1", [P, S], F32)[:],
             (1, 1): sb("scaled1_1", [P, S], F32)[:],
-            (0, 2): rr[2][:, PAD : PAD + S],
+            (0, 2): sb("scaled0_2", [P, HALF], F32)[:],
             (1, 2): sb("scaled1_2", [P, S], F32)[:],
         }
         summed_sb = {0: rr[3][:], 1: yz[:, 3 * pitch : 3 * pitch + S]}
+        across = rr[2][:, QUARTER // 2 : QUARTER // 2 + HALF]
+
+        def term(t, k, cols):
+            if k == 0:
+                return delayed(t, 0, cols)
+            if (t, k) == (0, 2) and cols.start >= HALF:
+                return across[:, cols.start - HALF : cols.stop - HALF]
+            return scaled[t, k][:, cols]
+
         ident = sb("ident", [P, P], F32)
         make_identity(nc, ident[:])
         sum_banks = {0: "y_second0", 1: "y_rest3"}
@@ -219,23 +227,21 @@ def tile_picked_yserial_silu_p_kernel(
         def gather_by_order(t, cols):
             nc.vector.tensor_copy(delayed(t, 0, cols), y[t].indirect(entries(order_sb, cols)))
 
-        def scale_terms(t):
-            nc.gpsimd.tensor_scalar(scaled[t, 1], delayed(t, 1, whole), ratio[:, t, 0:1], 0.0, op0=MULT, op1=ADD)
-            nc.scalar.activation(scaled[t, 2], delayed(t, 2, whole), COPY, scale=ratio[:, t, 1:2])
+        def term_on_gpsimd(t, k, cols):
+            nc.gpsimd.tensor_scalar(term(t, k, cols), delayed(t, k, cols), ratio[:, t, k - 1 : k], 0.0, op0=MULT, op1=ADD)
 
         def sum_by_transposes(t):
-            runs = [quarters[0], quarters[2], quarters[3], quarters[1]]
-            for k in range(TAPS):
-                term = delayed(t, 0, whole) if k == 0 else scaled[t, k]
-                for run in runs:
-                    nc.tensor.matmul(
-                        summed[t][:, run],
-                        lhsT=term[:, run],
-                        rhs=ident[:],
-                        is_transpose=True,
-                        start=(k == 0 and run == runs[0]),
-                        stop=(k == TAPS - 1 and run == runs[-1]),
-                    )
+            groups = (quarters[:2], quarters[2:]) if t == 0 else (quarters,)
+            steps = [(k, run) for runs in groups for k in range(TAPS) for run in runs]
+            for k, run in steps:
+                nc.tensor.matmul(
+                    summed[t][:, run],
+                    lhsT=term(t, k, run),
+                    rhs=ident[:],
+                    is_transpose=True,
+                    start=((k, run) == steps[0]),
+                    stop=((k, run) == steps[-1]),
+                )
 
         def turn_back(t):
             nc.scalar.copy(out=summed_sb[t], in_=summed[t][:])
@@ -270,16 +276,21 @@ def tile_picked_yserial_silu_p_kernel(
 
         lower, upper = halves
         nc.vector.tensor_copy(out=y[1][:, lower], in_=y_second[0][:])
-        gather_by_order(0, whole)
+        for cols in halves:
+            gather_by_order(0, cols)
         nc.scalar.copy(out=y[1][:, upper], in_=y_second[1][:])
-        for t in y_rest:
+        for t in (3, 2):
             nc.scalar.copy(out=y[t][:, :S], in_=y_rest[t][:])
         gather_by_order(1, whole)
-        for cols in halves:
+        for cols in (lower, quarters[2]):
             gather_by_order(2, cols)
-        scale_terms(0)
+        for cols in halves:
+            for k in (1, 2):
+                term_on_gpsimd(0, k, cols)
         nc.scalar.activation(delayed(3, 0, whole), y[3].indirect(order_sb[:]), COPY)
-        scale_terms(1)
+        term_on_gpsimd(1, 1, whole)
+        nc.scalar.activation(delayed(2, 0, quarters[3]), y[2].indirect(entries(order_sb, quarters[3])), COPY)
+        nc.scalar.activation(scaled[1, 2], delayed(1, 2, whole), COPY, scale=ratio[:, 1, 1:2])
         for t in (0, 1):
             sum_by_transposes(t)
         turn_back(0)

from contextlib import ExitStack

import concourse.mybir as mybir
from concourse.masks import make_identity

K, T, S, H, N = 1024, 1024, 512, 512, 128
FLOPS = 2 * K * H * S + 2 * H * N * S

F32 = mybir.dt.float32
BF16 = mybir.dt.bfloat16
I32 = mybir.dt.int32
U32 = mybir.dt.uint32
U16 = mybir.dt.uint16
U8 = mybir.dt.uint8
FP8X4 = mybir.dt.float8_e4m3fn_x4
MULT = mybir.AluOpType.mult
ADD = mybir.AluOpType.add
IS_LT = mybir.AluOpType.is_lt
COPY = mybir.ActivationFunctionType.Copy
SILU = mybir.ActivationFunctionType.Silu

P = 128
PACK = 4
PASSES = K // (P * PACK)
TAPS = 3
LINE = 4
PER_COLUMN = 16
LIST_COLS = S // PER_COLUMN
HALF = S // 2
QUARTER = S // 4
QUADRANTS = 4
SCALE_ROWS = 4
WIDE_WINDOW = 704
WINDOW = 528
PAD = 8
TINY = 2.0**-32
VECTOR_WEAVES = 192


def tile_picked_yserial_silu_p_kernel(
    tc, x_words, x_scales, w1, w2, taps, offs, order, back, out
):
    nc = tc.nc
    with ExitStack() as ctx:
        keep = ctx.enter_context(tc.tile_pool(name="keep", bufs=1))
        psum = ctx.enter_context(tc.psum_pool(name="psum", bufs=1))

        def sb(name, shape, dtype, tag=""):
            return keep.tile(shape, dtype, name=name, tag=tag or name, align_bytes=64)

        whole = slice(0, S)
        halves = [slice(h * HALF, (h + 1) * HALF) for h in range(2)]

        def entries(lst, cols):
            return lst[:, cols.start // PER_COLUMN : cols.stop // PER_COLUMN]

        offs_sb = sb("offs_sb", [P, LIST_COLS], U16)
        order_sb = sb("order_sb", [P, LIST_COLS], U16)
        back_sb = sb("back_sb", [P, LIST_COLS], U16)
        x_table = [sb("x_table%d" % o, [P, T], I32) for o in range(PASSES)]
        scale_table = sb("scale_table", [P, T], U8)
        w1_parts = ((0, 0, PACK), (1, 0, 2), (1, 2, 2))
        w1_raw = [sb("w1_raw%d" % n, [P, part[2], H], F32) for n, part in enumerate(w1_parts)]
        w2_raw = sb("w2_raw", [P, PACK, N], F32)
        taps_sb = sb("taps_sb", [P, PACK * TAPS], F32)
        pitch = HALF + S
        yz = sb("yz", [P, PACK * pitch], F32)
        z = yz[:].rearrange("p (t c) -> p t c", t=PACK)[:, :, HALF:]
        y = [
            sb("y0", [P, S], F32)[:],
            yz[:, :WIDE_WINDOW],
            sb("y2", [P, S], F32)[:],
            sb("y3", [P, WINDOW], F32)[:],
        ]
        rr = {t: sb("rr%d" % t, [P, S], F32) for t in (0, 1, 3)}
        zeros = sb("zeros", [P, WINDOW - S], F32)

        def load_words(o):
            nc.sync.dma_start(out=x_table[o][:], in_=x_words[o].rearrange("p n r -> p (n r)").bitcast(I32))

        def load_w1(n):
            o, first, count = w1_parts[n]
            rows = w1[o * P * PACK : (o + 1) * P * PACK, :].rearrange("(p j) c -> p j c", j=PACK)
            nc.sync.dma_start(out=w1_raw[n][:], in_=rows[:, first : first + count, :])

        nc.gpsimd.memset(scale_table[:].bitcast(I32), 0)
        load_words(0)
        nc.sync.dma_start(offs_sb[:], offs)
        for q in range(QUADRANTS):
            nc.sync.dma_start(
                out=scale_table[32 * q : 32 * q + SCALE_ROWS * PASSES, :].bitcast(I32),
                in_=x_scales[:, SCALE_ROWS * q : SCALE_ROWS * (q + 1), :].bitcast(I32),
            )
        nc.sync.dma_start(out=taps_sb[:], in_=taps.rearrange("(p t) k -> p (t k)", t=PACK))
        load_w1(0)
        load_words(1)
        load_w1(1)
        load_w1(2)
        nc.sync.dma_start(out=w2_raw[:], in_=w2.rearrange("(p j) m -> p j m", j=PACK))
        nc.sync.dma_start(order_sb[:], order)
        nc.sync.dma_start(back_sb[:], back)

        nc.gpsimd.memset(zeros[:], 0.0)
        nc.scalar.activation(y[3][:, S:], zeros[:], SILU)
        nc.gpsimd.memset(y[1][:, S:], 0.0)

        x_codes0 = sb("x_codes0", [P, S], U32)
        x_scale = sb("x_scale", [P, S], U8)
        nc.vector.tensor_copy(x_codes0[:], x_table[0][:].bitcast(U32).indirect(offs_sb[:]))
        nc.vector.tensor_copy(x_scale[:], scale_table[:].indirect(offs_sb[:]))

        taps3 = taps_sb[:].rearrange("p (t k) -> p t k", k=TAPS)
        square = sb("square", [P, PACK], F32)
        shift = sb("shift", [P, PACK], F32)
        lead = sb("lead", [P, PACK], F32)
        inverse = sb("inverse", [P, PACK], F32)
        ratio = sb("ratio", [P, PACK, TAPS - 1], F32)
        nc.gpsimd.tensor_tensor(square[:], taps3[:, :, 0], taps3[:, :, 0], MULT)
        nc.gpsimd.tensor_scalar(shift[:], square[:], TINY * TINY, 2.0 * TINY, op0=IS_LT, op1=MULT)
        nc.gpsimd.tensor_tensor(lead[:], taps3[:, :, 0], shift[:], ADD)
        nc.vector.reciprocal(inverse[:], lead[:])
        nc.gpsimd.tensor_tensor(
            ratio[:], taps3[:, :, 1:], inverse[:].unsqueeze(2).to_broadcast([P, PACK, TAPS - 1]), MULT
        )

        w1_bf = [[sb("w1_bf%d_%d" % (o, u), [P, 2 * P * PACK], BF16) for u in range(2)] for o in range(PASSES)]
        w1_codes = [[sb("w1_codes%d_%d" % (o, u), [P, 2 * P], U32) for u in range(2)] for o in range(PASSES)]
        w1_scale = [[sb("w1_scale%d_%d" % (o, u), [P, 2 * P], U8) for u in range(2)] for o in range(PASSES)]

        def weave_tiles(n, copy, first_tile, tiles):
            o, first, count = w1_parts[n]
            u, e = divmod(first_tile, 2)
            woven = w1_bf[o][u][:].rearrange("p (e m j) -> p m j e", e=2, j=PACK)
            copy(
                out=woven[:, :, first : first + count, e : e + tiles],
                in_=w1_raw[n][:].rearrange("p j (m t) -> p m j t", t=PACK)[:, :, :, first_tile : first_tile + tiles],
            )

        def weave_w1(n):
            weave_tiles(n, nc.vector.tensor_copy, 0, 2)
            weave_tiles(n, nc.scalar.copy, 2, 2)

        def quantize_w1(o, first_tile, tiles):
            u, e = divmod(first_tile, 2)
            cols = slice(e * P, (e + tiles) * P)
            nc.vector.quantize_mx(
                out=w1_codes[o][u][:, cols].bitcast(FP8X4),
                scales=w1_scale[o][u][:, cols],
                in_=w1_bf[o][u][:, e * P * PACK : (e + tiles) * P * PACK],
            )

        quarters = [slice(start, start + QUARTER) for start in range(0, S, QUARTER)]
        y_first = [psum.tile([P, QUARTER], F32, name="y_first%d" % n) for n in range(len(quarters))]
        y_second = [psum.tile([P, HALF], F32, name="y_second%d" % h) for h in range(len(halves))]
        y_rest = {t: psum.tile([P, S], F32, name="y_rest%d" % t) for t in (2, 3)}

        def product1(o, t, acc, x_codes, cols):
            m = slice((t % 2) * P, (t % 2 + 1) * P)
            nc.tensor.matmul_mx(
                out=acc,
                lhsT=w1_codes[o][t // 2][:, m].bitcast(FP8X4),
                lhsT_scale=w1_scale[o][t // 2][:, m],
                rhs=x_codes[:, cols].bitcast(FP8X4),
                rhs_scale=x_scale[SCALE_ROWS * o :, cols],
                start=(o == 0),
                stop=(o == PASSES - 1),
            )

        def products(o, x_codes):
            for n, cols in enumerate(quarters):
                product1(o, 0, y_first[n][:], x_codes, cols)
            for n, cols in enumerate(halves):
                product1(o, 1, y_second[n][:], x_codes, cols)
            for t in (3, 2):
                product1(o, t, y_rest[t][:], x_codes, whole)

        weave_w1(0)
        quantize_w1(0, 0, 2)
        quantize_w1(0, 2, 2)
        products(0, x_codes0)

        x_codes1 = sb("x_codes1", [P, S], U32, tag="w1_raw0")
        nc.vector.tensor_copy(x_codes1[:], x_table[1][:].bitcast(U32).indirect(offs_sb[:]))
        weave_w1(1)
        weave_tiles(2, nc.vector.tensor_copy, 0, 1)
        weave_tiles(2, nc.vector.tensor_copy, 1, 1)
        weave_tiles(2, nc.scalar.copy, 2, 2)
        quantize_w1(1, 0, 1)
        quantize_w1(1, 1, 1)
        quantize_w1(1, 2, 2)
        products(1, x_codes1)
        for n, copy in enumerate((nc.vector.tensor_copy, nc.scalar.copy) * 2):
            copy(out=y[0][:, quarters[n]], in_=y_first[n][:])

        gg = [sb("gg%d" % t, [P, PAD + S], F32) for t in range(PACK)]
        filt = {2: sb("filt2", [P, S], F32)[:], 3: gg[2][:, :S]}
        rr[2] = sb("rr2", [P, WINDOW], F32, tag="w1_codes1_1")
        nc.gpsimd.memset(rr[2][:, S:], 0.0)
        scaled = {
            (0, 1): sb("scaled0_1", [P, S], F32)[:],
            (1, 1): sb("scaled1_1", [P, S], F32)[:],
            (0, 2): sb("scaled0_2", [P, HALF], F32)[:],
            (1, 2): sb("scaled1_2", [P, S], F32)[:],
        }
        summed_sb = {0: rr[3][:], 1: yz[:, 3 * pitch : 3 * pitch + S]}
        across = rr[2][:, QUARTER // 2 : QUARTER // 2 + HALF]

        def term(t, k, cols):
            if k == 0:
                return delayed(t, 0, cols)
            if (t, k) == (0, 2) and cols.start >= HALF:
                return across[:, cols.start - HALF : cols.stop - HALF]
            return scaled[t, k][:, cols]

        ident = sb("ident", [P, P], F32)
        make_identity(nc, ident[:])
        sum_banks = {0: "y_second0", 1: "y_rest3"}
        back_banks = {0: "y_first3", 1: "y_first0"}
        summed = {t: psum.tile([P, S], F32, name="summed%d" % t, tag=sum_banks[t]) for t in (0, 1)}
        restored = {t: psum.tile([P, S], F32, name="restored%d" % t, tag=back_banks[t]) for t in (0, 1)}
        for t in range(PACK):
            nc.gpsimd.memset(gg[t][:, :PAD], 0.0)

        def delayed(t, k, cols):
            return gg[t][:, PAD - k + cols.start : PAD - k + cols.stop]

        def gather_by_order(t, cols):
            nc.vector.tensor_copy(delayed(t, 0, cols), y[t].indirect(entries(order_sb, cols)))

        def term_on_gpsimd(t, k, cols):
            nc.gpsimd.tensor_scalar(term(t, k, cols), delayed(t, k, cols), ratio[:, t, k - 1 : k], 0.0, op0=MULT, op1=ADD)

        def sum_by_transposes(t):
            groups = (quarters[:2], quarters[2:]) if t == 0 else (quarters,)
            steps = [(k, run) for runs in groups for k in range(TAPS) for run in runs]
            for k, run in steps:
                nc.tensor.matmul(
                    summed[t][:, run],
                    lhsT=term(t, k, run),
                    rhs=ident[:],
                    is_transpose=True,
                    start=((k, run) == steps[0]),
                    stop=((k, run) == steps[-1]),
                )

        def turn_back(t):
            nc.scalar.copy(out=summed_sb[t], in_=summed[t][:])
            for run in quarters:
                nc.tensor.transpose(restored[t][:, run], summed_sb[t][:, run], ident[:])

        def sum_on_vector(t):
            for k in range(1, TAPS):
                for cols in halves:
                    nc.vector.scalar_tensor_tensor(
                        out=filt[t][:, cols],
                        in0=delayed(t, k, cols),
                        scalar=ratio[:, t, k - 1 : k],
                        in1=delayed(t, 0, cols) if k == 1 else filt[t][:, cols],
                        op0=MULT,
                        op1=ADD,
                    )

        def silu(t, cols):
            source = restored[t] if t in restored else filt[t]
            nc.scalar.activation(rr[t][:, cols], source[:, cols], SILU, scale=lead[:, t : t + 1])

        w2_bf = sb("w2_bf", [P, N * PACK], BF16, tag="w1_bf1_1")
        nc.gpsimd.tensor_scalar(
            w2_bf[:].rearrange("p (c j) -> p c j", j=PACK),
            w2_raw[:].rearrange("p j c -> p c j"),
            1.0,
            0.0,
            op0=MULT,
            op1=ADD,
        )

        lower, upper = halves
        nc.vector.tensor_copy(out=y[1][:, lower], in_=y_second[0][:])
        for cols in halves:
            gather_by_order(0, cols)
        nc.scalar.copy(out=y[1][:, upper], in_=y_second[1][:])
        for t in (3, 2):
            nc.scalar.copy(out=y[t][:, :S], in_=y_rest[t][:])
        gather_by_order(1, whole)
        for cols in (lower, quarters[2]):
            gather_by_order(2, cols)
        for cols in halves:
            for k in (1, 2):
                term_on_gpsimd(0, k, cols)
        nc.scalar.activation(delayed(3, 0, whole), y[3].indirect(order_sb[:]), COPY)
        term_on_gpsimd(1, 1, whole)
        nc.scalar.activation(delayed(2, 0, quarters[3]), y[2].indirect(entries(order_sb, quarters[3])), COPY)
        nc.scalar.activation(scaled[1, 2], delayed(1, 2, whole), COPY, scale=ratio[:, 1, 1:2])
        for t in (0, 1):
            sum_by_transposes(t)
        turn_back(0)
        for t in filt:
            sum_on_vector(t)
        for cols in halves:
            silu(2, cols)
        turn_back(1)
        for t in (0, 3, 1):
            silu(t, whole)

        def picked(t, cols):
            return rr[t][:].indirect(entries(back_sb, cols))

        def gather_and_add(t, cols):
            nc.vector.tensor_tensor(z[:, t, cols], picked(t, cols), y[t][:, cols], ADD)

        def add_y(t):
            nc.vector.tensor_tensor(z[:, t, lower], z[:, t, lower], y[t][:, lower], ADD)

        gather_and_add(2, whole)
        for t in (0, 3, 1):
            gather_and_add(t, upper)
        for t in (3, 1):
            nc.scalar.activation(z[:, t, lower], picked(t, lower), COPY)
        add_y(3)
        gather_and_add(0, lower)
        add_y(1)

        w2_codes = sb("w2_codes", [P, N], U32, tag="rr0")
        w2_scale = sb("w2_scale", [P, N], U8)
        nc.vector.quantize_mx(out=w2_codes[:].bitcast(FP8X4), scales=w2_scale[:], in_=w2_bf[:])

        z_bf = sb("z_bf", [P, S * PACK], BF16)
        out_sb = sb("out_sb", [P, S], F32)
        out_banks = ("y_first2", "y_second0", "y_first1", "y_rest2")
        out_ps = {}

        def weave_z(copy, cols):
            copy(
                out=z_bf[:, cols.start * PACK : cols.stop * PACK].rearrange("p (c i t) -> p c t i", i=LINE, t=PACK),
                in_=z[:, :, cols].rearrange("p t (c i) -> p c t i", i=LINE),
            )

        def product2(n):
            cols = quarters[n]
            z_codes = sb("z_codes%d" % n, [P, QUARTER], U32)
            z_scale = sb("z_scale%d" % n, [P, QUARTER], U8)
            out_ps[n] = psum.tile([P, QUARTER], F32, name="out_ps%d" % n, tag=out_banks[n])
            nc.vector.quantize_mx(
                out=z_codes[:].bitcast(FP8X4), scales=z_scale[:], in_=z_bf[:, cols.start * PACK : cols.stop * PACK]
            )
            nc.tensor.matmul_mx(
                out=out_ps[n][:],
                lhsT=w2_codes[:].bitcast(FP8X4),
                lhsT_scale=w2_scale[:],
                rhs=z_codes[:].bitcast(FP8X4),
                rhs_scale=z_scale[:],
                start=True,
                stop=True,
            )

        for cols in (quarters[3], quarters[2], slice(VECTOR_WEAVES, HALF)):
            weave_z(nc.scalar.copy, cols)
        product2(3)
        weave_z(nc.vector.tensor_copy, slice(0, VECTOR_WEAVES))
        for n in (2, 0, 1):
            product2(n)
        for n in (3, 2):
            nc.scalar.copy(out=out_sb[:, quarters[n]], in_=out_ps[n][:])
        for n in (0, 1):
            nc.vector.tensor_copy(out=out_sb[:, quarters[n]], in_=out_ps[n][:])
        for cols in (upper, lower):
            nc.sync.dma_start(out=out[:, cols], in_=out_sb[:, cols])
